import numpy as np
import ml_dtypes


def mxq(x, axis, fmt="e4m3"):
    dtype, down = {"e4m3": (ml_dtypes.float8_e4m3fn, 7), "e5m2": (ml_dtypes.float8_e5m2, 14)}[fmt]
    v = np.moveaxis(np.asarray(x, np.float32).astype(ml_dtypes.bfloat16).astype(np.float64), axis, -1)
    blocks = v.reshape(v.shape[:-1] + (-1, 32))
    amax = np.abs(blocks).max(-1, keepdims=True)
    byte = np.maximum(np.where(amax > 0, np.frexp(amax)[1] - 1 + 127, 0) - down, 1)
    scale = np.exp2(byte - 127.0)
    codes = (blocks / scale).astype(np.float32).astype(dtype).astype(np.float64)
    return np.moveaxis((codes * scale).reshape(v.shape), -1, axis)


WIDE = False


def mx_kscale(k):
    if not WIDE:
        return np.ones(k)
    levels = np.array([10, -10, 5, -5, 0])
    if k % 512:
        return np.exp2(np.random.permutation(np.resize(levels, k // 32))).repeat(32)
    a = np.empty((k // 512, 16))
    for p in range(k // 512):
        a[p, :8] = np.random.permutation(np.resize(levels, 8))
        for g in range(8):
            far = levels[np.abs(levels - a[p, g]) >= 10]
            a[p, g + 8] = far[np.random.randint(len(far))]
    return np.exp2(a.ravel()).repeat(32)


def f64(x):
    return np.asarray(x).astype(np.float64)


def striped(idx):
    return np.tile(idx.reshape(-1, 16).T, (8, 1)).astype(np.uint16)


def unstriped(offs):
    return offs[:16].T.reshape(-1).astype(np.int64)


def pack_weight(w):
    k, n = w.shape
    w = f64(np.asarray(w, np.float32).astype(ml_dtypes.bfloat16)).reshape(k // 32, 32, n)
    amax = np.abs(w).max(1)
    byte = np.clip(np.where(amax > 0, np.frexp(amax)[1] - 1 + 127 - 7, 1), 1, 254)
    scaled = (w * np.exp2(127.0 - byte)[:, None, :]).reshape(k, n).astype(np.float32)
    words = np.ascontiguousarray(scaled.reshape(k // 512, 128, 4, n).transpose(0, 1, 3, 2)).astype(ml_dtypes.float8_e4m3fn).view(np.uint8)
    return words, np.ascontiguousarray(byte.astype(np.uint8).reshape(k // 512, 16, n))


def unpack_weight(words, scales):
    g, p, n, _ = words.shape
    vals = np.ascontiguousarray(words).view(ml_dtypes.float8_e4m3fn).astype(np.float64) * np.repeat(np.exp2(scales.astype(np.float64) - 127.0), 8, axis=1)[..., None]
    return vals.transpose(0, 1, 3, 2).reshape(g * 512, n)


def relu(v):
    return np.maximum(v, 0.0)


K, T, S, D, V, H, N, U = 512, 2048, 512, 4, 512, 512, 128, 1024
P = 2 ** 7


def setup_inputs():
    n = np.random.standard_normal
    s = mx_kscale(K)[:, None]
    u = mx_kscale(H)
    packed_xT = pack_weight(n((K, T)) * s)
    return {
        "x_words": packed_xT[0],
        "x_scales": packed_xT[1],
        "w1": (n((K, H)) / np.sqrt(K) / s * u).astype(np.float32),
        "w2": (n((H, N)) / np.sqrt(H) / u[:, None]).astype(np.float32),
        "gate": np.tile(np.random.uniform(0.2, 0.6, (D, 1, V)), (1, P, 1)).astype(np.float32),
        "emb": (0.5 * n((H, U)) * u[:, None]).astype(np.float32),
        "offs": striped(np.random.permutation(T)[:S]),
        "cell": striped(np.random.permutation(U)[:S]),
        "pos1": striped(np.random.permutation(U)[:V]),
        "pos2": striped(np.random.permutation(U)[:V]),
        "pos3": striped(np.random.permutation(U)[:V]),
        "pos4": striped(np.random.permutation(U)[:V]),
    }


def reference(x_words, x_scales, w1, w2, gate, emb, offs, cell, pos1, pos2, pos3, pos4):
    xq = unpack_weight(x_words, x_scales)[:, unstriped(offs)]
    up = np.zeros((H, U))
    up[:, unstriped(cell)] = relu(mxq(f64(w1), 0, "e4m3").T @ xq)
    z = up + f64(emb)
    y = relu(mxq(f64(w2), 0, "e4m3").T @ mxq(z, 0, "e4m3"))
    return y[:, unstriped(pos1)] * f64(gate)[0, :1] + y[:, unstriped(pos2)] * f64(gate)[1, :1] + y[:, unstriped(pos3)] * f64(gate)[2, :1] + y[:, unstriped(pos4)] * f64(gate)[3, :1]

@@ -1,0 +1,164 @@
+from contextlib import ExitStack
+
+import concourse.mybir as mybir
+
+K, T, S, D, V, H, N, U = 512, 2048, 512, 4, 512, 512, 128, 1024
+FLOPS = 2 * K * H * S + 2 * H * N * U
+
+F32 = mybir.dt.float32
+BF16 = mybir.dt.bfloat16
+I32 = mybir.dt.int32
+U32 = mybir.dt.uint32
+U16 = mybir.dt.uint16
+U8 = mybir.dt.uint8
+FP8X4 = mybir.dt.float8_e4m3fn_x4
+ADD = mybir.AluOpType.add
+MULT = mybir.AluOpType.mult
+RELU = mybir.ActivationFunctionType.Relu
+
+P = 128
+PACK = 4
+HALF = S // 2
+CHUNK = 256
+CHUNKS = U // CHUNK
+W1_VECTOR = 88
+
+
+def tile_picked_devox_relu_p_kernel(tc, x_words, x_scales, w1, w2, gate, emb, offs, cell, pos1, pos2, pos3, pos4, out):
+    nc = tc.nc
+    with ExitStack() as ctx:
+        keep = ctx.enter_context(tc.tile_pool(name="keep", bufs=1))
+        psum = ctx.enter_context(tc.psum_pool(name="psum", bufs=8))
+
+        offs_t = keep.tile([P, S // 16], U16, name="offs_t")
+        cell_t = keep.tile([P, S // 16], U16, name="cell_t")
+        pos_t = [keep.tile([P, V // 16], U16, name=f"pos_t{d}") for d in range(D)]
+        table_words = keep.tile([P, T], U32, name="table_words", align_bytes=64)
+        table_scales = keep.tile([P, T], U8, name="table_scales", align_bytes=64)
+        w1_raw = keep.tile([P, PACK, H], F32, name="w1_raw", align_bytes=64)
+        w2_raw = keep.tile([P, PACK, N], F32, name="w2_raw", align_bytes=64)
+        emb_t = [keep.tile([P, U], F32, name=f"emb_t{t}", align_bytes=64) for t in range(PACK)]
+        gate_t = keep.tile([P, D, V], F32, name="gate_t", align_bytes=64)
+        windows = [keep.tile([P, U], F32, name=f"window{a}", align_bytes=64) for a in range(2)]
+        up = [windows[t % 2] for t in range(PACK)]
+
+        nc.vector.memset(table_scales[:].bitcast(I32), 0)
+        nc.sync.dma_start(offs_t[:], offs)
+        nc.sync.dma_start(w1_raw[:], w1.rearrange("(p j) c -> p j c", j=PACK))
+        for q in range(4):
+            nc.scalar.dma_start(table_scales[32 * q : 32 * q + 4, :].bitcast(I32), x_scales[0, 4 * q : 4 * q + 4, :].bitcast(I32))
+        nc.sync.dma_start(table_words[:].bitcast(I32), x_words[0].rearrange("p n r -> p (n r)").bitcast(I32))
+        nc.sync.dma_start(cell_t[:], cell)
+        nc.sync.dma_start(w2_raw[:], w2.rearrange("(p j) c -> p j c", j=PACK))
+        emb_rows = emb.rearrange("(p t) r -> p t r", t=PACK)
+        for t in range(PACK):
+            nc.sync.dma_start(emb_t[t][:], emb_rows[:, t, :])
+        for d, pos in enumerate((pos1, pos2, pos3, pos4)):
+            nc.sync.dma_start(pos_t[d][:], pos)
+        nc.sync.dma_start(gate_t[:], gate.rearrange("d p v -> p d v"))
+        for window in windows:
+            nc.vector.memset(window[:], 0.0)
+
+        x_scale = keep.tile([P, S], U8, name="x_scale", align_bytes=64)
+        nc.vector.tensor_copy(x_scale[:], table_scales[:].indirect(offs_t[:]))
+
+        w1_bf = keep.tile([P, PACK, P, PACK], BF16, name="w1_bf", align_bytes=64)
+        w1_dst = w1_bf[:].rearrange("p t m j -> p m j t")
+        w1_src = w1_raw[:].rearrange("p j (m t) -> p m j t", t=PACK)
+        nc.vector.tensor_copy(w1_dst[:, :W1_VECTOR], w1_src[:, :W1_VECTOR])
+        nc.scalar.copy(w1_dst[:, W1_VECTOR:], w1_src[:, W1_VECTOR:])
+        w1_code = keep.tile([P, H], U32, name="w1_code", align_bytes=64)
+        w1_scale = keep.tile([P, H], U8, name="w1_scale", align_bytes=64)
+        nc.vector.quantize_mx(out=w1_code[:].bitcast(FP8X4), scales=w1_scale[:], in_=w1_bf[:].rearrange("p t m j -> p (t m j)"))
+
+        x_code = keep.tile([P, S], U32, name="x_code", align_bytes=64)
+        for a in range(2):
+            nc.vector.tensor_copy(x_code[:, a * HALF : (a + 1) * HALF], table_words[:].indirect(offs_t[:, a * HALF // 16 : (a + 1) * HALF // 16]))
+
+        def first_layer(t, lo, hi):
+            bank = psum.tile([P, hi - lo], F32, name="bank")
+            nc.tensor.matmul_mx(
+                out=bank[:],
+                lhsT=w1_code[:, t * P : (t + 1) * P].bitcast(FP8X4),
+                lhsT_scale=w1_scale[:, t * P : (t + 1) * P],
+                rhs=x_code[:, lo:hi].bitcast(FP8X4),
+                rhs_scale=x_scale[:, lo:hi],
+                start=True,
+                stop=True,
+            )
+            h = keep.tile([P, hi - lo], F32, name=f"h{t}_{lo}", align_bytes=64)
+            nc.scalar.activation(h[:], bank[:], RELU)
+            return h
+
+        pieces = [(0, 0, HALF), (0, HALF, S)] + [(t, 0, S) for t in range(1, PACK)]
+        hs = [first_layer(t, lo, hi) for t, lo, hi in pieces]
+
+        w2_bf = keep.tile([P, N, PACK], BF16, name="w2_bf", align_bytes=64)
+        nc.scalar.copy(w2_bf[:], w2_raw[:].rearrange("p j n -> p n j"))
+        w2_code = keep.tile([P, N], U32, name="w2_code", align_bytes=64)
+        w2_scale = keep.tile([P, N], U8, name="w2_scale", align_bytes=64)
+
+        z01 = keep.tile([P, 2, U], BF16, name="z01", align_bytes=64)
+        z2 = keep.tile([P, U], BF16, name="z2", align_bytes=64)
+        pairs = [keep.tile([P, 2, CHUNK, 2], BF16, name=f"pairs{c}", align_bytes=64) for c in range(CHUNKS)]
+        cols = [slice(c * CHUNK, (c + 1) * CHUNK) for c in range(CHUNKS)]
+
+        for (t, lo, hi), h in zip(pieces, hs):
+            nc.vector.tensor_copy(up[t][:].indirect(cell_t[:, lo // 16 : hi // 16]), h[:])
+            if hi < S:
+                continue
+            if t == 0:
+                nc.vector.quantize_mx(out=w2_code[:].bitcast(FP8X4), scales=w2_scale[:], in_=w2_bf[:].rearrange("p n j -> p (n j)"))
+            if t < 2:
+                nc.gpsimd.tensor_tensor(z01[:, t, :], up[t][:], emb_t[t][:], ADD)
+            if t == 1:
+                for c in range(CHUNKS):
+                    nc.scalar.copy(pairs[c][:, 0], z01[:, :, cols[c]].rearrange("p e r -> p r e"))
+            if t == 2:
+                for a in range(2):
+                    half = slice(a * U // 2, (a + 1) * U // 2)
+                    nc.gpsimd.tensor_tensor(z2[:, half], up[t][:, half], emb_t[t][:, half], ADD)
+                for c in range(CHUNKS):
+                    nc.scalar.copy(pairs[c][:, 1], z2[:, cols[c]].unsqueeze(2).to_broadcast([P, CHUNK, 2]))
+
+        for c in range(CHUNKS):
+            nc.vector.tensor_tensor(pairs[c][:, 1, :, 1], up[3][:, cols[c]], emb_t[3][:, cols[c]], ADD)
+
+        y = keep.tile([P, U], F32, name="y", align_bytes=64)
+        for c in range(CHUNKS):
+            z_bf = keep.tile([P, CHUNK * PACK], BF16, name=f"z_bf{c}", align_bytes=64)
+            dst = z_bf[:].bitcast(F32).rearrange("p (r u) -> p r u", u=2)
+            src = pairs[c][:].rearrange("p u r e -> p (u r e)").bitcast(F32).rearrange("p (u r) -> p r u", u=2)
+            if c < CHUNKS - 1:
+                nc.scalar.copy(dst, src)
+            else:
+                nc.vector.tensor_copy(dst, src)
+            z_code = keep.tile([P, CHUNK], U32, name=f"z_code{c}", align_bytes=64)
+            z_scale = keep.tile([P, CHUNK], U8, name=f"z_scale{c}", align_bytes=64)
+            nc.vector.quantize_mx(out=z_code[:].bitcast(FP8X4), scales=z_scale[:], in_=z_bf[:])
+            bank = psum.tile([P, CHUNK], F32, name="bank")
+            nc.tensor.matmul_mx(
+                out=bank[:],
+                lhsT=w2_code[:].bitcast(FP8X4),
+                lhsT_scale=w2_scale[:],
+                rhs=z_code[:].bitcast(FP8X4),
+                rhs_scale=z_scale[:],
+                start=True,
+                stop=True,
+            )
+            nc.scalar.activation(y[:, cols[c]], bank[:], RELU)
+
+        terms = [keep.tile([P, V], F32, name=f"term{d}", align_bytes=64) for d in range(D)]
+        sum01 = keep.tile([P, V], F32, name="sum01", align_bytes=64)
+        sum012 = keep.tile([P, V], F32, name="sum012", align_bytes=64)
+        for d in range(D):
+            nc.vector.tensor_tensor(terms[d][:], y[:].indirect(pos_t[d][:]), gate_t[:, d, :], MULT)
+            if d == 2:
+                nc.vector.tensor_tensor(sum01[:], terms[0][:], terms[1][:], ADD)
+        halves = [slice(a * V // 2, (a + 1) * V // 2) for a in range(2)]
+        for v in halves:
+            nc.vector.tensor_tensor(sum012[:, v], sum01[:, v], terms[2][:, v], ADD)
+        for a, v in enumerate(halves):
+            res = keep.tile([P, V // 2], F32, name=f"res{a}", align_bytes=64)
+            nc.vector.tensor_tensor(res[:], sum012[:, v], terms[3][:, v], ADD)
+            (nc.sync if a == 0 else nc.scalar).dma_start(out[:, v], res[:])

@@ -1,6 +1,7 @@
 from contextlib import ExitStack
 
 import concourse.mybir as mybir
+from concourse.masks import make_identity
 
 K, T, S, D, V, H, N, U = 512, 2048, 512, 4, 512, 512, 128, 1024
 FLOPS = 2 * K * H * S + 2 * H * N * U
@@ -19,9 +20,10 @@ RELU = mybir.ActivationFunctionType.Relu
 P = 128
 PACK = 4
 HALF = S // 2
-CHUNK = 256
-CHUNKS = U // CHUNK
-W1_VECTOR = 88
+WIDTHS = (256, 256, 256, 128, 128)
+CHUNKS = len(WIDTHS)
+SCALAR_CHUNKS = 5
+W1_VECTOR = 56
 
 
 def tile_picked_devox_relu_p_kernel(tc, x_words, x_scales, w1, w2, gate, emb, offs, cell, pos1, pos2, pos3, pos4, out):
@@ -37,36 +39,38 @@ def tile_picked_devox_relu_p_kernel(tc, x_words, x_scales, w1, w2, gate, emb, of
         table_scales = keep.tile([P, T], U8, name="table_scales", align_bytes=64)
         w1_raw = keep.tile([P, PACK, H], F32, name="w1_raw", align_bytes=64)
         w2_raw = keep.tile([P, PACK, N], F32, name="w2_raw", align_bytes=64)
-        emb_t = [keep.tile([P, U], F32, name=f"emb_t{t}", align_bytes=64) for t in range(PACK)]
+        emb_t = [keep.tile([P, U], F32, name=f"emb_t{t}", align_bytes=64) for t in range(2)]
         gate_t = keep.tile([P, D, V], F32, name="gate_t", align_bytes=64)
-        windows = [keep.tile([P, U], F32, name=f"window{a}", align_bytes=64) for a in range(2)]
-        up = [windows[t % 2] for t in range(PACK)]
+        up = [keep.tile([P, U if t < 2 else 2 * U], F32, name=f"up{t}", align_bytes=64) for t in range(PACK)]
+        ident = keep.tile([P, P], F32, name="ident", align_bytes=64)
 
-        nc.vector.memset(table_scales[:].bitcast(I32), 0)
+        nc.gpsimd.memset(table_scales[:].bitcast(I32), 0)
         nc.sync.dma_start(offs_t[:], offs)
         nc.sync.dma_start(w1_raw[:], w1.rearrange("(p j) c -> p j c", j=PACK))
         for q in range(4):
-            nc.scalar.dma_start(table_scales[32 * q : 32 * q + 4, :].bitcast(I32), x_scales[0, 4 * q : 4 * q + 4, :].bitcast(I32))
+            nc.sync.dma_start(table_scales[32 * q : 32 * q + 4, :].bitcast(I32), x_scales[0, 4 * q : 4 * q + 4, :].bitcast(I32))
         nc.sync.dma_start(table_words[:].bitcast(I32), x_words[0].rearrange("p n r -> p (n r)").bitcast(I32))
         nc.sync.dma_start(cell_t[:], cell)
-        nc.sync.dma_start(w2_raw[:], w2.rearrange("(p j) c -> p j c", j=PACK))
         emb_rows = emb.rearrange("(p t) r -> p t r", t=PACK)
-        for t in range(PACK):
+        for t in range(2):
             nc.sync.dma_start(emb_t[t][:], emb_rows[:, t, :])
+        nc.sync.dma_start(w2_raw[:], w2.rearrange("(p j) c -> p j c", j=PACK))
+        nc.sync.dma_start(up[2][:, U:], emb_rows[:, 3, :])
+        nc.sync.dma_start(up[3][:, U:], emb_rows[:, 2, :])
         for d, pos in enumerate((pos1, pos2, pos3, pos4)):
             nc.sync.dma_start(pos_t[d][:], pos)
         nc.sync.dma_start(gate_t[:], gate.rearrange("d p v -> p d v"))
-        for window in windows:
-            nc.vector.memset(window[:], 0.0)
-
-        x_scale = keep.tile([P, S], U8, name="x_scale", align_bytes=64)
-        nc.vector.tensor_copy(x_scale[:], table_scales[:].indirect(offs_t[:]))
+        for t in range(PACK):
+            (nc.vector if t < 3 else nc.gpsimd).memset(up[t][:, :U], 0.0)
+        make_identity(nc, ident[:])
 
         w1_bf = keep.tile([P, PACK, P, PACK], BF16, name="w1_bf", align_bytes=64)
-        w1_dst = w1_bf[:].rearrange("p t m j -> p m j t")
-        w1_src = w1_raw[:].rearrange("p j (m t) -> p m j t", t=PACK)
+        w1_dst = w1_bf[:].rearrange("p t m j -> p m t j")
+        w1_src = w1_raw[:].rearrange("p j (m t) -> p m t j", t=PACK)
         nc.vector.tensor_copy(w1_dst[:, :W1_VECTOR], w1_src[:, :W1_VECTOR])
         nc.scalar.copy(w1_dst[:, W1_VECTOR:], w1_src[:, W1_VECTOR:])
+        x_scale = keep.tile([P, S], U8, name="x_scale", align_bytes=64)
+        nc.vector.tensor_copy(x_scale[:], table_scales[:].indirect(offs_t[:]))
         w1_code = keep.tile([P, H], U32, name="w1_code", align_bytes=64)
         w1_scale = keep.tile([P, H], U8, name="w1_scale", align_bytes=64)
         nc.vector.quantize_mx(out=w1_code[:].bitcast(FP8X4), scales=w1_scale[:], in_=w1_bf[:].rearrange("p t m j -> p (t m j)"))
@@ -90,7 +94,7 @@ def tile_picked_devox_relu_p_kernel(tc, x_words, x_scales, w1, w2, gate, emb, of
             nc.scalar.activation(h[:], bank[:], RELU)
             return h
 
-        pieces = [(0, 0, HALF), (0, HALF, S)] + [(t, 0, S) for t in range(1, PACK)]
+        pieces = [(0, 0, P), (0, P, HALF), (0, HALF, S)] + [(t, 0, S) for t in range(1, PACK)]
         hs = [first_layer(t, lo, hi) for t, lo, hi in pieces]
 
         w2_bf = keep.tile([P, N, PACK], BF16, name="w2_bf", align_bytes=64)
@@ -98,10 +102,9 @@ def tile_picked_devox_relu_p_kernel(tc, x_words, x_scales, w1, w2, gate, emb, of
         w2_code = keep.tile([P, N], U32, name="w2_code", align_bytes=64)
         w2_scale = keep.tile([P, N], U8, name="w2_scale", align_bytes=64)
 
-        z01 = keep.tile([P, 2, U], BF16, name="z01", align_bytes=64)
-        z2 = keep.tile([P, U], BF16, name="z2", align_bytes=64)
-        pairs = [keep.tile([P, 2, CHUNK, 2], BF16, name=f"pairs{c}", align_bytes=64) for c in range(CHUNKS)]
-        cols = [slice(c * CHUNK, (c + 1) * CHUNK) for c in range(CHUNKS)]
+        pairs = [keep.tile([P, 2, WIDTHS[c], 2], BF16, name=f"pairs{c}", align_bytes=64) for c in range(CHUNKS)]
+        cols = [slice(sum(WIDTHS[:c]), sum(WIDTHS[: c + 1])) for c in range(CHUNKS)]
+        turned = [psum.tile([P, 2, 2, P], F32, name="bank") for g in range(U // (2 * P))]
 
         for (t, lo, hi), h in zip(pieces, hs):
             nc.vector.tensor_copy(up[t][:].indirect(cell_t[:, lo // 16 : hi // 16]), h[:])
@@ -110,33 +113,43 @@ def tile_picked_devox_relu_p_kernel(tc, x_words, x_scales, w1, w2, gate, emb, of
             if t == 0:
                 nc.vector.quantize_mx(out=w2_code[:].bitcast(FP8X4), scales=w2_scale[:], in_=w2_bf[:].rearrange("p n j -> p (n j)"))
             if t < 2:
-                nc.gpsimd.tensor_tensor(z01[:, t, :], up[t][:], emb_t[t][:], ADD)
+                for b in range(U // P):
+                    cells = slice(b * P, (b + 1) * P)
+                    nc.tensor.matmul(turned[b // 2][:, b % 2, t, :], up[t][:, cells], ident[:], start=True, stop=False, is_transpose=True)
+                    nc.tensor.matmul(turned[b // 2][:, b % 2, t, :], emb_t[t][:, cells], ident[:], start=False, stop=True, is_transpose=True)
             if t == 1:
+                turned_bf = [keep.tile([P, 2, P, 2], BF16, name=f"turned_bf{g}", align_bytes=64) for g in range(len(turned))]
+                for g in range(len(turned)):
+                    nc.scalar.copy(turned_bf[g][:], turned[g][:].rearrange("r b e p -> r b p e"))
                 for c in range(CHUNKS):
-                    nc.scalar.copy(pairs[c][:, 0], z01[:, :, cols[c]].rearrange("p e r -> p r e"))
-            if t == 2:
-                for a in range(2):
-                    half = slice(a * U // 2, (a + 1) * U // 2)
-                    nc.gpsimd.tensor_tensor(z2[:, half], up[t][:, half], emb_t[t][:, half], ADD)
-                for c in range(CHUNKS):
-                    nc.scalar.copy(pairs[c][:, 1], z2[:, cols[c]].unsqueeze(2).to_broadcast([P, CHUNK, 2]))
+                    back = psum.tile([P, WIDTHS[c]], F32, name="bank")
+                    for b in range(cols[c].start // P, cols[c].stop // P):
+                        words = turned_bf[b // 2][:].rearrange("r b p e -> r (b p e)").bitcast(F32)
+                        at = b * P - cols[c].start
+                        nc.tensor.transpose(back[:, at : at + P], words[:, (b % 2) * P : (b % 2 + 1) * P], ident[:])
+                    nc.scalar.copy(pairs[c][:].rearrange("p u r e -> p (u r e)").bitcast(F32)[:, : WIDTHS[c]], back[:])
 
         for c in range(CHUNKS):
-            nc.vector.tensor_tensor(pairs[c][:, 1, :, 1], up[3][:, cols[c]], emb_t[3][:, cols[c]], ADD)
+            nc.vector.tensor_tensor(
+                pairs[c][:, 1].rearrange("p (g i) e -> p g e i", i=4),
+                up[2][:].rearrange("p (e r) -> p e r", e=2)[:, :, cols[c]].rearrange("p e (g i) -> p g e i", i=4),
+                up[3][:].rearrange("p (e r) -> p e r", e=2)[:, ::-1, cols[c]].rearrange("p e (g i) -> p g e i", i=4),
+                ADD,
+            )
 
         y = keep.tile([P, U], F32, name="y", align_bytes=64)
         for c in range(CHUNKS):
-            z_bf = keep.tile([P, CHUNK * PACK], BF16, name=f"z_bf{c}", align_bytes=64)
+            z_bf = keep.tile([P, WIDTHS[c] * PACK], BF16, name=f"z_bf{c}", align_bytes=64)
             dst = z_bf[:].bitcast(F32).rearrange("p (r u) -> p r u", u=2)
             src = pairs[c][:].rearrange("p u r e -> p (u r e)").bitcast(F32).rearrange("p (u r) -> p r u", u=2)
-            if c < CHUNKS - 1:
+            if c < SCALAR_CHUNKS:
                 nc.scalar.copy(dst, src)
             else:
                 nc.vector.tensor_copy(dst, src)
-            z_code = keep.tile([P, CHUNK], U32, name=f"z_code{c}", align_bytes=64)
-            z_scale = keep.tile([P, CHUNK], U8, name=f"z_scale{c}", align_bytes=64)
+            z_code = keep.tile([P, WIDTHS[c]], U32, name=f"z_code{c}", align_bytes=64)
+            z_scale = keep.tile([P, WIDTHS[c]], U8, name=f"z_scale{c}", align_bytes=64)
             nc.vector.quantize_mx(out=z_code[:].bitcast(FP8X4), scales=z_scale[:], in_=z_bf[:])
-            bank = psum.tile([P, CHUNK], F32, name="bank")
+            bank = psum.tile([P, WIDTHS[c]], F32, name="bank")
             nc.tensor.matmul_mx(
                 out=bank[:],
                 lhsT=w2_code[:].bitcast(FP8X4),

@@ -22,7 +22,6 @@ PACK = 4
 HALF = S // 2
 WIDTHS = (256, 256, 256, 128, 128)
 CHUNKS = len(WIDTHS)
-SCALAR_CHUNKS = 5
 W1_VECTOR = 56
 
 
@@ -73,11 +72,21 @@ def tile_picked_devox_relu_p_kernel(tc, x_words, x_scales, w1, w2, gate, emb, of
         nc.vector.tensor_copy(x_scale[:], table_scales[:].indirect(offs_t[:]))
         w1_code = keep.tile([P, H], U32, name="w1_code", align_bytes=64)
         w1_scale = keep.tile([P, H], U8, name="w1_scale", align_bytes=64)
-        nc.vector.quantize_mx(out=w1_code[:].bitcast(FP8X4), scales=w1_scale[:], in_=w1_bf[:].rearrange("p t m j -> p (t m j)"))
+
+        def quantize_w1(t0, t1):
+            nc.vector.quantize_mx(
+                out=w1_code[:, t0 * P : t1 * P].bitcast(FP8X4),
+                scales=w1_scale[:, t0 * P : t1 * P],
+                in_=w1_bf[:, t0:t1].rearrange("p t m j -> p (t m j)"),
+            )
+
+        quantize_w1(0, 1)
 
         x_code = keep.tile([P, S], U32, name="x_code", align_bytes=64)
         for a in range(2):
             nc.vector.tensor_copy(x_code[:, a * HALF : (a + 1) * HALF], table_words[:].indirect(offs_t[:, a * HALF // 16 : (a + 1) * HALF // 16]))
+        quantize_w1(1, 2)
+        quantize_w1(2, PACK)
 
         def first_layer(t, lo, hi):
             bank = psum.tile([P, hi - lo], F32, name="bank")
@@ -137,18 +146,17 @@ def tile_picked_devox_relu_p_kernel(tc, x_words, x_scales, w1, w2, gate, emb, of
                 ADD,
             )
 
+        z_bf = [keep.tile([P, WIDTHS[c] * PACK], BF16, name=f"z_bf{c}", align_bytes=64) for c in range(CHUNKS)]
+        for c in range(CHUNKS):
+            nc.scalar.copy(
+                z_bf[c][:].bitcast(F32).rearrange("p (r u) -> p r u", u=2),
+                pairs[c][:].rearrange("p u r e -> p (u r e)").bitcast(F32).rearrange("p (u r) -> p r u", u=2),
+            )
         y = keep.tile([P, U], F32, name="y", align_bytes=64)
         for c in range(CHUNKS):
-            z_bf = keep.tile([P, WIDTHS[c] * PACK], BF16, name=f"z_bf{c}", align_bytes=64)
-            dst = z_bf[:].bitcast(F32).rearrange("p (r u) -> p r u", u=2)
-            src = pairs[c][:].rearrange("p u r e -> p (u r e)").bitcast(F32).rearrange("p (u r) -> p r u", u=2)
-            if c < SCALAR_CHUNKS:
-                nc.scalar.copy(dst, src)
-            else:
-                nc.vector.tensor_copy(dst, src)
             z_code = keep.tile([P, WIDTHS[c]], U32, name=f"z_code{c}", align_bytes=64)
             z_scale = keep.tile([P, WIDTHS[c]], U8, name=f"z_scale{c}", align_bytes=64)
-            nc.vector.quantize_mx(out=z_code[:].bitcast(FP8X4), scales=z_scale[:], in_=z_bf[:])
+            nc.vector.quantize_mx(out=z_code[:].bitcast(FP8X4), scales=z_scale[:], in_=z_bf[c][:])
             bank = psum.tile([P, WIDTHS[c]], F32, name="bank")
             nc.tensor.matmul_mx(
                 out=bank[:],
@@ -162,15 +170,26 @@ def tile_picked_devox_relu_p_kernel(tc, x_words, x_scales, w1, w2, gate, emb, of
             nc.scalar.activation(y[:, cols[c]], bank[:], RELU)
 
         terms = [keep.tile([P, V], F32, name=f"term{d}", align_bytes=64) for d in range(D)]
-        sum01 = keep.tile([P, V], F32, name="sum01", align_bytes=64)
-        sum012 = keep.tile([P, V], F32, name="sum012", align_bytes=64)
+        halves = [slice(a * V // 2, (a + 1) * V // 2) for a in range(2)]
+        sum_turned = [psum.tile([P, 2, P], F32, name="bank") for a in range(2)]
         for d in range(D):
             nc.vector.tensor_tensor(terms[d][:], y[:].indirect(pos_t[d][:]), gate_t[:, d, :], MULT)
-            if d == 2:
-                nc.vector.tensor_tensor(sum01[:], terms[0][:], terms[1][:], ADD)
-        halves = [slice(a * V // 2, (a + 1) * V // 2) for a in range(2)]
-        for v in halves:
-            nc.vector.tensor_tensor(sum012[:, v], sum01[:, v], terms[2][:, v], ADD)
+            if d < 2:
+                for b in range(V // P):
+                    first = d == 0 and b % 2 == 0
+                    last = d == 1 and b % 2 == 1
+                    nc.tensor.matmul(sum_turned[b // 2][:, b % 2, :], terms[d][:, b * P : (b + 1) * P], ident[:], start=first, stop=last, is_transpose=True)
+        sum01 = []
+        for a in range(2):
+            staged = keep.tile([P, 2, P], F32, name=f"staged{a}", align_bytes=64)
+            nc.scalar.copy(staged[:], sum_turned[a][:])
+            bank = psum.tile([P, V // 2], F32, name="bank")
+            for b in range(2):
+                nc.tensor.transpose(bank[:, b * P : (b + 1) * P], staged[:, b, :], ident[:])
+            sum01.append(bank)
+        sum012 = keep.tile([P, V], F32, name="sum012", align_bytes=64)
+        for a, v in enumerate(halves):
+            nc.vector.tensor_tensor(sum012[:, v], terms[2][:, v], sum01[a][:], ADD)
         for a, v in enumerate(halves):
             res = keep.tile([P, V // 2], F32, name=f"res{a}", align_bytes=64)
             nc.vector.tensor_tensor(res[:], sum012[:, v], terms[3][:, v], ADD)

@@ -19,10 +19,14 @@ RELU = mybir.ActivationFunctionType.Relu
 
 P = 128
 PACK = 4
+LIST_ROWS = 16
+QUADRANT = 32
+LINE = 4
 HALF = S // 2
 WIDTHS = (256, 256, 256, 128, 128)
 CHUNKS = len(WIDTHS)
 W1_VECTOR = 56
+VECTOR_CLEARS = 3
 
 
 def tile_picked_devox_relu_p_kernel(tc, x_words, x_scales, w1, w2, gate, emb, offs, cell, pos1, pos2, pos3, pos4, out):
@@ -31,9 +35,9 @@ def tile_picked_devox_relu_p_kernel(tc, x_words, x_scales, w1, w2, gate, emb, of
         keep = ctx.enter_context(tc.tile_pool(name="keep", bufs=1))
         psum = ctx.enter_context(tc.psum_pool(name="psum", bufs=8))
 
-        offs_t = keep.tile([P, S // 16], U16, name="offs_t")
-        cell_t = keep.tile([P, S // 16], U16, name="cell_t")
-        pos_t = [keep.tile([P, V // 16], U16, name=f"pos_t{d}") for d in range(D)]
+        offs_t = keep.tile([P, S // LIST_ROWS], U16, name="offs_t")
+        cell_t = keep.tile([P, S // LIST_ROWS], U16, name="cell_t")
+        pos_t = [keep.tile([P, V // LIST_ROWS], U16, name=f"pos_t{d}") for d in range(D)]
         table_words = keep.tile([P, T], U32, name="table_words", align_bytes=64)
         table_scales = keep.tile([P, T], U8, name="table_scales", align_bytes=64)
         w1_raw = keep.tile([P, PACK, H], F32, name="w1_raw", align_bytes=64)
@@ -46,21 +50,21 @@ def tile_picked_devox_relu_p_kernel(tc, x_words, x_scales, w1, w2, gate, emb, of
         nc.gpsimd.memset(table_scales[:].bitcast(I32), 0)
         nc.sync.dma_start(offs_t[:], offs)
         nc.sync.dma_start(w1_raw[:], w1.rearrange("(p j) c -> p j c", j=PACK))
-        for q in range(4):
-            nc.sync.dma_start(table_scales[32 * q : 32 * q + 4, :].bitcast(I32), x_scales[0, 4 * q : 4 * q + 4, :].bitcast(I32))
+        for q in range(P // QUADRANT):
+            nc.sync.dma_start(table_scales[QUADRANT * q : QUADRANT * q + 4, :].bitcast(I32), x_scales[0, 4 * q : 4 * q + 4, :].bitcast(I32))
         nc.sync.dma_start(table_words[:].bitcast(I32), x_words[0].rearrange("p n r -> p (n r)").bitcast(I32))
         nc.sync.dma_start(cell_t[:], cell)
-        emb_rows = emb.rearrange("(p t) r -> p t r", t=PACK)
+        emb_planes = emb.rearrange("(p t) r -> p t r", t=PACK)
         for t in range(2):
-            nc.sync.dma_start(emb_t[t][:], emb_rows[:, t, :])
+            nc.sync.dma_start(emb_t[t][:], emb_planes[:, t, :])
         nc.sync.dma_start(w2_raw[:], w2.rearrange("(p j) c -> p j c", j=PACK))
-        nc.sync.dma_start(up[2][:, U:], emb_rows[:, 3, :])
-        nc.sync.dma_start(up[3][:, U:], emb_rows[:, 2, :])
+        nc.sync.dma_start(up[2][:, U:], emb_planes[:, 3, :])
+        nc.sync.dma_start(up[3][:, U:], emb_planes[:, 2, :])
         for d, pos in enumerate((pos1, pos2, pos3, pos4)):
             nc.sync.dma_start(pos_t[d][:], pos)
         nc.sync.dma_start(gate_t[:], gate.rearrange("d p v -> p d v"))
         for t in range(PACK):
-            (nc.vector if t < 3 else nc.gpsimd).memset(up[t][:, :U], 0.0)
+            (nc.vector if t < VECTOR_CLEARS else nc.gpsimd).memset(up[t][:, :U], 0.0)
         make_identity(nc, ident[:])
 
         w1_bf = keep.tile([P, PACK, P, PACK], BF16, name="w1_bf", align_bytes=64)
@@ -80,31 +84,33 @@ def tile_picked_devox_relu_p_kernel(tc, x_words, x_scales, w1, w2, gate, emb, of
                 in_=w1_bf[:, t0:t1].rearrange("p t m j -> p (t m j)"),
             )
 
-        quantize_w1(0, 1)
-
+        quantize_w1(0, 2)
         x_code = keep.tile([P, S], U32, name="x_code", align_bytes=64)
         for a in range(2):
-            nc.vector.tensor_copy(x_code[:, a * HALF : (a + 1) * HALF], table_words[:].indirect(offs_t[:, a * HALF // 16 : (a + 1) * HALF // 16]))
-        quantize_w1(1, 2)
+            nc.vector.tensor_copy(
+                x_code[:, a * HALF : (a + 1) * HALF],
+                table_words[:].indirect(offs_t[:, a * HALF // LIST_ROWS : (a + 1) * HALF // LIST_ROWS]),
+            )
         quantize_w1(2, PACK)
 
-        def first_layer(t, lo, hi):
-            bank = psum.tile([P, hi - lo], F32, name="bank")
-            nc.tensor.matmul_mx(
-                out=bank[:],
-                lhsT=w1_code[:, t * P : (t + 1) * P].bitcast(FP8X4),
-                lhsT_scale=w1_scale[:, t * P : (t + 1) * P],
-                rhs=x_code[:, lo:hi].bitcast(FP8X4),
-                rhs_scale=x_scale[:, lo:hi],
-                start=True,
-                stop=True,
-            )
-            h = keep.tile([P, hi - lo], F32, name=f"h{t}_{lo}", align_bytes=64)
-            nc.scalar.activation(h[:], bank[:], RELU)
+        def first_layer(t, cuts):
+            h = keep.tile([P, cuts[-1] - cuts[0]], F32, name=f"h{t}_{cuts[0]}", align_bytes=64)
+            for a, b in zip(cuts, cuts[1:]):
+                bank = psum.tile([P, b - a], F32, name="bank")
+                nc.tensor.matmul_mx(
+                    out=bank[:],
+                    lhsT=w1_code[:, t * P : (t + 1) * P].bitcast(FP8X4),
+                    lhsT_scale=w1_scale[:, t * P : (t + 1) * P],
+                    rhs=x_code[:, a:b].bitcast(FP8X4),
+                    rhs_scale=x_scale[:, a:b],
+                    start=True,
+                    stop=True,
+                )
+                nc.scalar.activation(h[:, a - cuts[0] : b - cuts[0]], bank[:], RELU)
             return h
 
-        pieces = [(0, 0, P), (0, P, HALF), (0, HALF, S)] + [(t, 0, S) for t in range(1, PACK)]
-        hs = [first_layer(t, lo, hi) for t, lo, hi in pieces]
+        pieces = [(0, (0, P)), (1, (0, HALF)), (0, (P, HALF, S)), (1, (HALF, S)), (2, (0, S)), (3, (0, S))]
+        hs = [first_layer(t, cuts) for t, cuts in pieces]
 
         w2_bf = keep.tile([P, N, PACK], BF16, name="w2_bf", align_bytes=64)
         nc.scalar.copy(w2_bf[:], w2_raw[:].rearrange("p j n -> p n j"))
@@ -115,9 +121,9 @@ def tile_picked_devox_relu_p_kernel(tc, x_words, x_scales, w1, w2, gate, emb, of
         cols = [slice(sum(WIDTHS[:c]), sum(WIDTHS[: c + 1])) for c in range(CHUNKS)]
         turned = [psum.tile([P, 2, 2, P], F32, name="bank") for g in range(U // (2 * P))]
 
-        for (t, lo, hi), h in zip(pieces, hs):
-            nc.vector.tensor_copy(up[t][:].indirect(cell_t[:, lo // 16 : hi // 16]), h[:])
-            if hi < S:
+        for (t, cuts), h in zip(pieces, hs):
+            nc.vector.tensor_copy(up[t][:].indirect(cell_t[:, cuts[0] // LIST_ROWS : cuts[-1] // LIST_ROWS]), h[:])
+            if cuts[-1] < S:
                 continue
             if t == 0:
                 nc.vector.quantize_mx(out=w2_code[:].bitcast(FP8X4), scales=w2_scale[:], in_=w2_bf[:].rearrange("p n j -> p (n j)"))
@@ -140,9 +146,9 @@ def tile_picked_devox_relu_p_kernel(tc, x_words, x_scales, w1, w2, gate, emb, of
 
         for c in range(CHUNKS):
             nc.vector.tensor_tensor(
-                pairs[c][:, 1].rearrange("p (g i) e -> p g e i", i=4),
-                up[2][:].rearrange("p (e r) -> p e r", e=2)[:, :, cols[c]].rearrange("p e (g i) -> p g e i", i=4),
-                up[3][:].rearrange("p (e r) -> p e r", e=2)[:, ::-1, cols[c]].rearrange("p e (g i) -> p g e i", i=4),
+                pairs[c][:, 1].rearrange("p (g i) e -> p g e i", i=LINE),
+                up[2][:].rearrange("p (e r) -> p e r", e=2)[:, :, cols[c]].rearrange("p e (g i) -> p g e i", i=LINE),
+                up[3][:].rearrange("p (e r) -> p e r", e=2)[:, ::-1, cols[c]].rearrange("p e (g i) -> p g e i", i=LINE),
                 ADD,
             )
 

@@ -25,7 +25,6 @@ LINE = 4
 HALF = S // 2
 WIDTHS = (256, 256, 256, 128, 128)
 CHUNKS = len(WIDTHS)
-W1_VECTOR = 56
 VECTOR_CLEARS = 3
 
 
@@ -40,7 +39,7 @@ def tile_picked_devox_relu_p_kernel(tc, x_words, x_scales, w1, w2, gate, emb, of
         pos_t = [keep.tile([P, V // LIST_ROWS], U16, name=f"pos_t{d}") for d in range(D)]
         table_words = keep.tile([P, T], U32, name="table_words", align_bytes=64)
         table_scales = keep.tile([P, T], U8, name="table_scales", align_bytes=64)
-        w1_raw = keep.tile([P, PACK, H], F32, name="w1_raw", align_bytes=64)
+        w1_raw = [keep.tile([P, PACK, H // 2], F32, name=f"w1_raw{a}", align_bytes=64) for a in range(2)]
         w2_raw = keep.tile([P, PACK, N], F32, name="w2_raw", align_bytes=64)
         emb_t = [keep.tile([P, U], F32, name=f"emb_t{t}", align_bytes=64) for t in range(2)]
         gate_t = keep.tile([P, D, V], F32, name="gate_t", align_bytes=64)
@@ -49,17 +48,20 @@ def tile_picked_devox_relu_p_kernel(tc, x_words, x_scales, w1, w2, gate, emb, of
 
         nc.gpsimd.memset(table_scales[:].bitcast(I32), 0)
         nc.sync.dma_start(offs_t[:], offs)
-        nc.sync.dma_start(w1_raw[:], w1.rearrange("(p j) c -> p j c", j=PACK))
+        w1_rows = w1.rearrange("(p j) c -> p j c", j=PACK)
+        nc.sync.dma_start(w1_raw[0][:], w1_rows[:, :, : H // 2])
         for q in range(P // QUADRANT):
             nc.sync.dma_start(table_scales[QUADRANT * q : QUADRANT * q + 4, :].bitcast(I32), x_scales[0, 4 * q : 4 * q + 4, :].bitcast(I32))
-        nc.sync.dma_start(table_words[:].bitcast(I32), x_words[0].rearrange("p n r -> p (n r)").bitcast(I32))
         nc.sync.dma_start(cell_t[:], cell)
+        nc.sync.dma_start(table_words[:].bitcast(I32), x_words[0].rearrange("p n r -> p (n r)").bitcast(I32))
+        nc.sync.dma_start(w1_raw[1][:], w1_rows[:, :, H // 2 :])
         emb_planes = emb.rearrange("(p t) r -> p t r", t=PACK)
-        for t in range(2):
-            nc.sync.dma_start(emb_t[t][:], emb_planes[:, t, :])
         nc.sync.dma_start(w2_raw[:], w2.rearrange("(p j) c -> p j c", j=PACK))
         nc.sync.dma_start(up[2][:, U:], emb_planes[:, 3, :])
         nc.sync.dma_start(up[3][:, U:], emb_planes[:, 2, :])
+        for a in range(2):
+            for e in range(2):
+                nc.sync.dma_start(emb_t[a][e:P:2, :], emb_planes[a * P // 2 : (a + 1) * P // 2, e, :])
         for d, pos in enumerate((pos1, pos2, pos3, pos4)):
             nc.sync.dma_start(pos_t[d][:], pos)
         nc.sync.dma_start(gate_t[:], gate.rearrange("d p v -> p d v"))
@@ -67,40 +69,50 @@ def tile_picked_devox_relu_p_kernel(tc, x_words, x_scales, w1, w2, gate, emb, of
             (nc.vector if t < VECTOR_CLEARS else nc.gpsimd).memset(up[t][:, :U], 0.0)
         make_identity(nc, ident[:])
 
-        w1_bf = keep.tile([P, PACK, P, PACK], BF16, name="w1_bf", align_bytes=64)
-        w1_dst = w1_bf[:].rearrange("p t m j -> p m t j")
-        w1_src = w1_raw[:].rearrange("p j (m t) -> p m t j", t=PACK)
-        nc.vector.tensor_copy(w1_dst[:, :W1_VECTOR], w1_src[:, :W1_VECTOR])
-        nc.scalar.copy(w1_dst[:, W1_VECTOR:], w1_src[:, W1_VECTOR:])
+        w1_low = [keep.tile([P, P // 2, 2, PACK], BF16, name=f"w1_low{a}", align_bytes=64) for a in range(2)]
+        w1_high = [keep.tile([P, 2, P // 2, PACK], BF16, name=f"w1_high{a}", align_bytes=64) for a in range(2)]
+        w1_code = [keep.tile([P, P], U32, name=f"w1_code{t}", align_bytes=64) for t in range(PACK)]
+        w1_scale = [keep.tile([P, P], U8, name=f"w1_scale{t}", align_bytes=64) for t in range(PACK)]
+
+        def round_low(a, copy):
+            copy(w1_low[a][:], w1_raw[a][:].rearrange("p j (m t) -> p m t j", t=PACK)[:, :, :2])
+
+        def round_high(a, copy):
+            copy(w1_high[a][:].rearrange("p f m j -> p m f j"), w1_raw[a][:].rearrange("p j (m t) -> p m t j", t=PACK)[:, :, 2:])
+
+        def quantize_low(a):
+            nc.vector.quantize_mx(out=w1_code[a][:].bitcast(FP8X4), scales=w1_scale[a][:], in_=w1_low[a][:].rearrange("p m e j -> p (m e j)"))
+
+        def quantize_high(a):
+            half = slice(a * P // 2, (a + 1) * P // 2)
+            for f in range(2):
+                nc.vector.quantize_mx(
+                    out=w1_code[2 + f][:, half].bitcast(FP8X4),
+                    scales=w1_scale[2 + f][:, half],
+                    in_=w1_high[a][:, f].rearrange("p m j -> p (m j)"),
+                )
+
+        round_low(0, nc.vector.tensor_copy)
+        round_high(0, nc.scalar.copy)
         x_scale = keep.tile([P, S], U8, name="x_scale", align_bytes=64)
         nc.vector.tensor_copy(x_scale[:], table_scales[:].indirect(offs_t[:]))
-        w1_code = keep.tile([P, H], U32, name="w1_code", align_bytes=64)
-        w1_scale = keep.tile([P, H], U8, name="w1_scale", align_bytes=64)
-
-        def quantize_w1(t0, t1):
-            nc.vector.quantize_mx(
-                out=w1_code[:, t0 * P : t1 * P].bitcast(FP8X4),
-                scales=w1_scale[:, t0 * P : t1 * P],
-                in_=w1_bf[:, t0:t1].rearrange("p t m j -> p (t m j)"),
-            )
-
-        quantize_w1(0, 2)
+        quantize_low(0)
+        quantize_high(0)
         x_code = keep.tile([P, S], U32, name="x_code", align_bytes=64)
         for a in range(2):
             nc.vector.tensor_copy(
                 x_code[:, a * HALF : (a + 1) * HALF],
                 table_words[:].indirect(offs_t[:, a * HALF // LIST_ROWS : (a + 1) * HALF // LIST_ROWS]),
             )
-        quantize_w1(2, PACK)
 
-        def first_layer(t, cuts):
-            h = keep.tile([P, cuts[-1] - cuts[0]], F32, name=f"h{t}_{cuts[0]}", align_bytes=64)
+        def first_layer(t, cuts, buffer):
+            h = keep.tile([P, cuts[-1] - cuts[0]], F32, name=buffer, align_bytes=64)
             for a, b in zip(cuts, cuts[1:]):
                 bank = psum.tile([P, b - a], F32, name="bank")
                 nc.tensor.matmul_mx(
                     out=bank[:],
-                    lhsT=w1_code[:, t * P : (t + 1) * P].bitcast(FP8X4),
-                    lhsT_scale=w1_scale[:, t * P : (t + 1) * P],
+                    lhsT=w1_code[t][:].bitcast(FP8X4),
+                    lhsT_scale=w1_scale[t][:],
                     rhs=x_code[:, a:b].bitcast(FP8X4),
                     rhs_scale=x_scale[:, a:b],
                     start=True,
@@ -109,8 +121,14 @@ def tile_picked_devox_relu_p_kernel(tc, x_words, x_scales, w1, w2, gate, emb, of
                 nc.scalar.activation(h[:, a - cuts[0] : b - cuts[0]], bank[:], RELU)
             return h
 
-        pieces = [(0, (0, P)), (1, (0, HALF)), (0, (P, HALF, S)), (1, (HALF, S)), (2, (0, S)), (3, (0, S))]
-        hs = [first_layer(t, cuts) for t, cuts in pieces]
+        pieces = [(0, (0, HALF)), (0, (HALF, S)), (1, (0, S)), (2, (0, S)), (3, (0, S))]
+        hs = [first_layer(*pieces[0], "h0")]
+        round_low(1, nc.scalar.copy)
+        quantize_low(1)
+        round_high(1, nc.scalar.copy)
+        quantize_high(1)
+        hs.append(first_layer(*pieces[1], "w1_raw1"))
+        hs.extend(first_layer(t, cuts, f"h{t}") for t, cuts in pieces[2:])
 
         w2_bf = keep.tile([P, N, PACK], BF16, name="w2_bf", align_bytes=64)
         nc.scalar.copy(w2_bf[:], w2_raw[:].rearrange("p j n -> p n j"))
@@ -125,21 +143,21 @@ def tile_picked_devox_relu_p_kernel(tc, x_words, x_scales, w1, w2, gate, emb, of
             nc.vector.tensor_copy(up[t][:].indirect(cell_t[:, cuts[0] // LIST_ROWS : cuts[-1] // LIST_ROWS]), h[:])
             if cuts[-1] < S:
                 continue
-            if t == 0:
+            if t == 1:
                 nc.vector.quantize_mx(out=w2_code[:].bitcast(FP8X4), scales=w2_scale[:], in_=w2_bf[:].rearrange("p n j -> p (n j)"))
             if t < 2:
                 for b in range(U // P):
                     cells = slice(b * P, (b + 1) * P)
-                    nc.tensor.matmul(turned[b // 2][:, b % 2, t, :], up[t][:, cells], ident[:], start=True, stop=False, is_transpose=True)
-                    nc.tensor.matmul(turned[b // 2][:, b % 2, t, :], emb_t[t][:, cells], ident[:], start=False, stop=True, is_transpose=True)
+                    nc.tensor.matmul(turned[b // 2][:, b % 2, t, :], emb_t[t][:, cells], ident[:], start=True, stop=False, is_transpose=True)
+                    nc.tensor.matmul(turned[b // 2][:, b % 2, t, :], up[t][:, cells], ident[:], start=False, stop=True, is_transpose=True)
             if t == 1:
-                turned_bf = [keep.tile([P, 2, P, 2], BF16, name=f"turned_bf{g}", align_bytes=64) for g in range(len(turned))]
+                turned_bf = [keep.tile([P, 2, 2, P], BF16, name=f"turned_bf{g}", align_bytes=64) for g in range(len(turned))]
                 for g in range(len(turned)):
-                    nc.scalar.copy(turned_bf[g][:], turned[g][:].rearrange("r b e p -> r b p e"))
+                    nc.scalar.copy(turned_bf[g][:], turned[g][:])
                 for c in range(CHUNKS):
                     back = psum.tile([P, WIDTHS[c]], F32, name="bank")
                     for b in range(cols[c].start // P, cols[c].stop // P):
-                        words = turned_bf[b // 2][:].rearrange("r b p e -> r (b p e)").bitcast(F32)
+                        words = turned_bf[b // 2][:].rearrange("r b a m -> r (b a m)").bitcast(F32)
                         at = b * P - cols[c].start
                         nc.tensor.transpose(back[:, at : at + P], words[:, (b % 2) * P : (b % 2 + 1) * P], ident[:])
                     nc.scalar.copy(pairs[c][:].rearrange("p u r e -> p (u r e)").bitcast(F32)[:, : WIDTHS[c]], back[:])

@@ -23,16 +23,18 @@ LIST_ROWS = 16
 QUADRANT = 32
 LINE = 4
 HALF = S // 2
-WIDTHS = (256, 256, 256, 128, 128)
-CHUNKS = len(WIDTHS)
-VECTOR_CLEARS = 3
+PAIR_WIDTHS = (128, 256, 256, 384)
+WIDTHS = (128, 256, 256, 256, 128)
 
 
 def tile_picked_devox_relu_p_kernel(tc, x_words, x_scales, w1, w2, gate, emb, offs, cell, pos1, pos2, pos3, pos4, out):
     nc = tc.nc
     with ExitStack() as ctx:
         keep = ctx.enter_context(tc.tile_pool(name="keep", bufs=1))
-        psum = ctx.enter_context(tc.psum_pool(name="psum", bufs=8))
+        psum = ctx.enter_context(tc.psum_pool(name="psum", bufs=1))
+
+        def bank(index, shape):
+            return psum.tile(shape, F32, name=f"bank{index}")
 
         offs_t = keep.tile([P, S // LIST_ROWS], U16, name="offs_t")
         cell_t = keep.tile([P, S // LIST_ROWS], U16, name="cell_t")
@@ -41,9 +43,10 @@ def tile_picked_devox_relu_p_kernel(tc, x_words, x_scales, w1, w2, gate, emb, of
         table_scales = keep.tile([P, T], U8, name="table_scales", align_bytes=64)
         w1_raw = [keep.tile([P, PACK, H // 2], F32, name=f"w1_raw{a}", align_bytes=64) for a in range(2)]
         w2_raw = keep.tile([P, PACK, N], F32, name="w2_raw", align_bytes=64)
-        emb_t = [keep.tile([P, U], F32, name=f"emb_t{t}", align_bytes=64) for t in range(2)]
+        emb_t = [keep.tile([P, U], F32, name=f"emb_t{t}", align_bytes=64) for t in range(PACK)]
         gate_t = keep.tile([P, D, V], F32, name="gate_t", align_bytes=64)
-        up = [keep.tile([P, U if t < 2 else 2 * U], F32, name=f"up{t}", align_bytes=64) for t in range(PACK)]
+        windows = [keep.tile([P, U], F32, name=f"window{t}", align_bytes=64) for t in range(3)]
+        up = windows + [windows[2]]
         ident = keep.tile([P, P], F32, name="ident", align_bytes=64)
 
         nc.gpsimd.memset(table_scales[:].bitcast(I32), 0)
@@ -56,17 +59,17 @@ def tile_picked_devox_relu_p_kernel(tc, x_words, x_scales, w1, w2, gate, emb, of
         nc.sync.dma_start(table_words[:].bitcast(I32), x_words[0].rearrange("p n r -> p (n r)").bitcast(I32))
         nc.sync.dma_start(w1_raw[1][:], w1_rows[:, :, H // 2 :])
         emb_planes = emb.rearrange("(p t) r -> p t r", t=PACK)
+        nc.sync.dma_start(emb_t[2][:], emb_planes[:, 2, :])
         nc.sync.dma_start(w2_raw[:], w2.rearrange("(p j) c -> p j c", j=PACK))
-        nc.sync.dma_start(up[2][:, U:], emb_planes[:, 3, :])
-        nc.sync.dma_start(up[3][:, U:], emb_planes[:, 2, :])
         for a in range(2):
             for e in range(2):
                 nc.sync.dma_start(emb_t[a][e:P:2, :], emb_planes[a * P // 2 : (a + 1) * P // 2, e, :])
         for d, pos in enumerate((pos1, pos2, pos3, pos4)):
             nc.sync.dma_start(pos_t[d][:], pos)
         nc.sync.dma_start(gate_t[:], gate.rearrange("d p v -> p d v"))
-        for t in range(PACK):
-            (nc.vector if t < VECTOR_CLEARS else nc.gpsimd).memset(up[t][:, :U], 0.0)
+        nc.sync.dma_start(emb_t[3][:], emb_planes[:, 3, :])
+        for window in windows:
+            nc.vector.memset(window[:], 0.0)
         make_identity(nc, ident[:])
 
         w1_low = [keep.tile([P, P // 2, 2, PACK], BF16, name=f"w1_low{a}", align_bytes=64) for a in range(2)]
@@ -105,85 +108,92 @@ def tile_picked_devox_relu_p_kernel(tc, x_words, x_scales, w1, w2, gate, emb, of
                 table_words[:].indirect(offs_t[:, a * HALF // LIST_ROWS : (a + 1) * HALF // LIST_ROWS]),
             )
 
-        def first_layer(t, cuts, buffer):
-            h = keep.tile([P, cuts[-1] - cuts[0]], F32, name=buffer, align_bytes=64)
-            for a, b in zip(cuts, cuts[1:]):
-                bank = psum.tile([P, b - a], F32, name="bank")
-                nc.tensor.matmul_mx(
-                    out=bank[:],
-                    lhsT=w1_code[t][:].bitcast(FP8X4),
-                    lhsT_scale=w1_scale[t][:],
-                    rhs=x_code[:, a:b].bitcast(FP8X4),
-                    rhs_scale=x_scale[:, a:b],
-                    start=True,
-                    stop=True,
-                )
-                nc.scalar.activation(h[:, a - cuts[0] : b - cuts[0]], bank[:], RELU)
-            return h
+        def first_layer(t, a, b, buffer, index):
+            h = keep.tile([P, b - a], F32, name=buffer, align_bytes=64)
+            acc = bank(index, [P, b - a])
+            nc.tensor.matmul_mx(
+                out=acc[:],
+                lhsT=w1_code[t][:].bitcast(FP8X4),
+                lhsT_scale=w1_scale[t][:],
+                rhs=x_code[:, a:b].bitcast(FP8X4),
+                rhs_scale=x_scale[:, a:b],
+                start=True,
+                stop=True,
+            )
+            nc.scalar.activation(h[:], acc[:], RELU)
+            return (t, a, b, h)
 
-        pieces = [(0, (0, HALF)), (0, (HALF, S)), (1, (0, S)), (2, (0, S)), (3, (0, S))]
-        hs = [first_layer(*pieces[0], "h0")]
-        round_low(1, nc.scalar.copy)
-        quantize_low(1)
+        pieces = [first_layer(0, 0, HALF, "h0", 0)]
         round_high(1, nc.scalar.copy)
         quantize_high(1)
-        hs.append(first_layer(*pieces[1], "w1_raw1"))
-        hs.extend(first_layer(t, cuts, f"h{t}") for t, cuts in pieces[2:])
+        round_low(1, nc.scalar.copy)
+        quantize_low(1)
+        pieces.append(first_layer(0, HALF, S, "w1_raw1", 1))
+        pieces.append(first_layer(2, 0, S, "h2", 2))
+        pieces.append(first_layer(1, 0, S, "h1", 3))
+        pieces.append(first_layer(3, 0, S, "h3", 4))
 
         w2_bf = keep.tile([P, N, PACK], BF16, name="w2_bf", align_bytes=64)
         nc.scalar.copy(w2_bf[:], w2_raw[:].rearrange("p j n -> p n j"))
         w2_code = keep.tile([P, N], U32, name="w2_code", align_bytes=64)
         w2_scale = keep.tile([P, N], U8, name="w2_scale", align_bytes=64)
 
-        pairs = [keep.tile([P, 2, WIDTHS[c], 2], BF16, name=f"pairs{c}", align_bytes=64) for c in range(CHUNKS)]
-        cols = [slice(sum(WIDTHS[:c]), sum(WIDTHS[: c + 1])) for c in range(CHUNKS)]
-        turned = [psum.tile([P, 2, 2, P], F32, name="bank") for g in range(U // (2 * P))]
+        pair_cols = [slice(sum(PAIR_WIDTHS[:c]), sum(PAIR_WIDTHS[: c + 1])) for c in range(len(PAIR_WIDTHS))]
+        pairs = [keep.tile([P, 2, width, 2], BF16, name=f"pairs{c}", align_bytes=64) for c, width in enumerate(PAIR_WIDTHS)]
+        turned_bf = [keep.tile([P, 2, 2, P], BF16, name=f"turned_bf{g}", align_bytes=64) for g in range(4)]
 
-        for (t, cuts), h in zip(pieces, hs):
-            nc.vector.tensor_copy(up[t][:].indirect(cell_t[:, cuts[0] // LIST_ROWS : cuts[-1] // LIST_ROWS]), h[:])
-            if cuts[-1] < S:
-                continue
-            if t == 1:
-                nc.vector.quantize_mx(out=w2_code[:].bitcast(FP8X4), scales=w2_scale[:], in_=w2_bf[:].rearrange("p n j -> p (n j)"))
-            if t < 2:
+        def turn(a, per_bank, first_bank):
+            banks = [bank(first_bank + g, [P, per_bank, P]) for g in range(U // P // per_bank)]
+            for source in (emb_t[a], up[a]):
                 for b in range(U // P):
-                    cells = slice(b * P, (b + 1) * P)
-                    nc.tensor.matmul(turned[b // 2][:, b % 2, t, :], emb_t[t][:, cells], ident[:], start=True, stop=False, is_transpose=True)
-                    nc.tensor.matmul(turned[b // 2][:, b % 2, t, :], up[t][:, cells], ident[:], start=False, stop=True, is_transpose=True)
+                    first = source is emb_t[a] and b % per_bank == 0
+                    last = source is up[a] and b % per_bank == per_bank - 1
+                    nc.tensor.matmul(banks[b // per_bank][:, b % per_bank, :], source[:, b * P : (b + 1) * P], ident[:], start=first, stop=last, is_transpose=True)
+            for g in range(4):
+                at = 2 * g % per_bank
+                nc.scalar.copy(turned_bf[g][:, :, a, :], banks[2 * g // per_bank][:, at : at + 2, :])
+
+        def add_plane(engine, t):
+            for c, cols in enumerate(pair_cols):
+                engine.tensor_tensor(pairs[c][:, 1, :, t - 2], up[t][:, cols], emb_t[t][:, cols], ADD)
+
+        for t, a, b, h in pieces:
+            nc.vector.tensor_copy(up[t][:].indirect(cell_t[:, a // LIST_ROWS : b // LIST_ROWS]), h[:])
+            if b < S:
+                continue
+            if t == 0:
+                turn(0, 4, 5)
+            if t == 2:
+                add_plane(nc.gpsimd, 2)
+                nc.vector.quantize_mx(out=w2_code[:].bitcast(FP8X4), scales=w2_scale[:], in_=w2_bf[:].rearrange("p n j -> p (n j)"))
             if t == 1:
-                turned_bf = [keep.tile([P, 2, 2, P], BF16, name=f"turned_bf{g}", align_bytes=64) for g in range(len(turned))]
-                for g in range(len(turned)):
-                    nc.scalar.copy(turned_bf[g][:], turned[g][:])
-                for c in range(CHUNKS):
-                    back = psum.tile([P, WIDTHS[c]], F32, name="bank")
-                    for b in range(cols[c].start // P, cols[c].stop // P):
+                turn(1, 2, 0)
+                for c, cols in enumerate(pair_cols):
+                    back = bank(4 + c, [P, PAIR_WIDTHS[c]])
+                    for b in range(cols.start // P, cols.stop // P):
                         words = turned_bf[b // 2][:].rearrange("r b a m -> r (b a m)").bitcast(F32)
-                        at = b * P - cols[c].start
+                        at = b * P - cols.start
                         nc.tensor.transpose(back[:, at : at + P], words[:, (b % 2) * P : (b % 2 + 1) * P], ident[:])
-                    nc.scalar.copy(pairs[c][:].rearrange("p u r e -> p (u r e)").bitcast(F32)[:, : WIDTHS[c]], back[:])
+                    nc.scalar.copy(pairs[c][:].rearrange("p u r e -> p (u r e)").bitcast(F32)[:, : PAIR_WIDTHS[c]], back[:])
+        add_plane(nc.vector, 3)
 
-        for c in range(CHUNKS):
-            nc.vector.tensor_tensor(
-                pairs[c][:, 1].rearrange("p (g i) e -> p g e i", i=LINE),
-                up[2][:].rearrange("p (e r) -> p e r", e=2)[:, :, cols[c]].rearrange("p e (g i) -> p g e i", i=LINE),
-                up[3][:].rearrange("p (e r) -> p e r", e=2)[:, ::-1, cols[c]].rearrange("p e (g i) -> p g e i", i=LINE),
-                ADD,
-            )
-
-        z_bf = [keep.tile([P, WIDTHS[c] * PACK], BF16, name=f"z_bf{c}", align_bytes=64) for c in range(CHUNKS)]
-        for c in range(CHUNKS):
+        cols = [slice(sum(WIDTHS[:c]), sum(WIDTHS[: c + 1])) for c in range(len(WIDTHS))]
+        z_bf = [keep.tile([P, width * PACK], BF16, name=f"z_bf{c}", align_bytes=64) for c, width in enumerate(WIDTHS)]
+        for c, span in enumerate(cols):
+            home = max(k for k, whole in enumerate(pair_cols) if whole.start <= span.start)
+            at = span.start - pair_cols[home].start
             nc.scalar.copy(
                 z_bf[c][:].bitcast(F32).rearrange("p (r u) -> p r u", u=2),
-                pairs[c][:].rearrange("p u r e -> p (u r e)").bitcast(F32).rearrange("p (u r) -> p r u", u=2),
+                pairs[home][:].rearrange("p u r e -> p (u r e)").bitcast(F32).rearrange("p (u r) -> p r u", u=2)[:, at : at + WIDTHS[c]],
             )
         y = keep.tile([P, U], F32, name="y", align_bytes=64)
-        for c in range(CHUNKS):
+        for c, span in enumerate(cols):
             z_code = keep.tile([P, WIDTHS[c]], U32, name=f"z_code{c}", align_bytes=64)
             z_scale = keep.tile([P, WIDTHS[c]], U8, name=f"z_scale{c}", align_bytes=64)
             nc.vector.quantize_mx(out=z_code[:].bitcast(FP8X4), scales=z_scale[:], in_=z_bf[c][:])
-            bank = psum.tile([P, WIDTHS[c]], F32, name="bank")
+            acc = bank(c, [P, WIDTHS[c]])
             nc.tensor.matmul_mx(
-                out=bank[:],
+                out=acc[:],
                 lhsT=w2_code[:].bitcast(FP8X4),
                 lhsT_scale=w2_scale[:],
                 rhs=z_code[:].bitcast(FP8X4),
@@ -191,11 +201,14 @@ def tile_picked_devox_relu_p_kernel(tc, x_words, x_scales, w1, w2, gate, emb, of
                 start=True,
                 stop=True,
             )
-            nc.scalar.activation(y[:, cols[c]], bank[:], RELU)
+            if c < len(WIDTHS) - 1:
+                nc.scalar.activation(y[:, span], acc[:], RELU)
+            else:
+                nc.vector.tensor_scalar_max(y[:, span], acc[:], 0.0)
 
         terms = [keep.tile([P, V], F32, name=f"term{d}", align_bytes=64) for d in range(D)]
         halves = [slice(a * V // 2, (a + 1) * V // 2) for a in range(2)]
-        sum_turned = [psum.tile([P, 2, P], F32, name="bank") for a in range(2)]
+        sum_turned = [bank(5 + a, [P, 2, P]) for a in range(2)]
         for d in range(D):
             nc.vector.tensor_tensor(terms[d][:], y[:].indirect(pos_t[d][:]), gate_t[:, d, :], MULT)
             if d < 2:
@@ -207,10 +220,10 @@ def tile_picked_devox_relu_p_kernel(tc, x_words, x_scales, w1, w2, gate, emb, of
         for a in range(2):
             staged = keep.tile([P, 2, P], F32, name=f"staged{a}", align_bytes=64)
             nc.scalar.copy(staged[:], sum_turned[a][:])
-            bank = psum.tile([P, V // 2], F32, name="bank")
+            acc = bank(a, [P, V // 2])
             for b in range(2):
-                nc.tensor.transpose(bank[:, b * P : (b + 1) * P], staged[:, b, :], ident[:])
-            sum01.append(bank)
+                nc.tensor.transpose(acc[:, b * P : (b + 1) * P], staged[:, b, :], ident[:])
+            sum01.append(acc)
         sum012 = keep.tile([P, V], F32, name="sum012", align_bytes=64)
         for a, v in enumerate(halves):
             nc.vector.tensor_tensor(sum012[:, v], terms[2][:, v], sum01[a][:], ADD)

@@ -23,8 +23,8 @@ LIST_ROWS = 16
 QUADRANT = 32
 LINE = 4
 HALF = S // 2
-PAIR_WIDTHS = (128, 256, 256, 384)
-WIDTHS = (128, 256, 256, 256, 128)
+PAIR_WIDTHS = (256, 256, 256, 256)
+WIDTHS = (256, 256, 256, 128, 128)
 
 
 def tile_picked_devox_relu_p_kernel(tc, x_words, x_scales, w1, w2, gate, emb, offs, cell, pos1, pos2, pos3, pos4, out):
@@ -43,33 +43,32 @@ def tile_picked_devox_relu_p_kernel(tc, x_words, x_scales, w1, w2, gate, emb, of
         table_scales = keep.tile([P, T], U8, name="table_scales", align_bytes=64)
         w1_raw = [keep.tile([P, PACK, H // 2], F32, name=f"w1_raw{a}", align_bytes=64) for a in range(2)]
         w2_raw = keep.tile([P, PACK, N], F32, name="w2_raw", align_bytes=64)
-        emb_t = [keep.tile([P, U], F32, name=f"emb_t{t}", align_bytes=64) for t in range(PACK)]
+        emb_t = [keep.tile([P, U], F32, name=f"emb_t{t}", align_bytes=64) for t in range(2)]
         gate_t = keep.tile([P, D, V], F32, name="gate_t", align_bytes=64)
-        windows = [keep.tile([P, U], F32, name=f"window{t}", align_bytes=64) for t in range(3)]
-        up = windows + [windows[2]]
+        up = [keep.tile([P, U if t < 2 else 2 * U], F32, name=f"up{t}", align_bytes=64) for t in range(PACK)]
         ident = keep.tile([P, P], F32, name="ident", align_bytes=64)
 
         nc.gpsimd.memset(table_scales[:].bitcast(I32), 0)
-        nc.sync.dma_start(offs_t[:], offs)
         w1_rows = w1.rearrange("(p j) c -> p j c", j=PACK)
         nc.sync.dma_start(w1_raw[0][:], w1_rows[:, :, : H // 2])
+        nc.sync.dma_start(offs_t[:], offs)
+        nc.sync.dma_start(cell_t[:], cell)
         for q in range(P // QUADRANT):
             nc.sync.dma_start(table_scales[QUADRANT * q : QUADRANT * q + 4, :].bitcast(I32), x_scales[0, 4 * q : 4 * q + 4, :].bitcast(I32))
-        nc.sync.dma_start(cell_t[:], cell)
         nc.sync.dma_start(table_words[:].bitcast(I32), x_words[0].rearrange("p n r -> p (n r)").bitcast(I32))
         nc.sync.dma_start(w1_raw[1][:], w1_rows[:, :, H // 2 :])
         emb_planes = emb.rearrange("(p t) r -> p t r", t=PACK)
-        nc.sync.dma_start(emb_t[2][:], emb_planes[:, 2, :])
         nc.sync.dma_start(w2_raw[:], w2.rearrange("(p j) c -> p j c", j=PACK))
         for a in range(2):
             for e in range(2):
                 nc.sync.dma_start(emb_t[a][e:P:2, :], emb_planes[a * P // 2 : (a + 1) * P // 2, e, :])
+        nc.sync.dma_start(up[2][:, U:], emb_planes[:, 3, :])
+        nc.sync.dma_start(up[3][:, U:], emb_planes[:, 2, :])
         for d, pos in enumerate((pos1, pos2, pos3, pos4)):
             nc.sync.dma_start(pos_t[d][:], pos)
         nc.sync.dma_start(gate_t[:], gate.rearrange("d p v -> p d v"))
-        nc.sync.dma_start(emb_t[3][:], emb_planes[:, 3, :])
-        for window in windows:
-            nc.vector.memset(window[:], 0.0)
+        for t in range(PACK):
+            (nc.vector if t < 3 else nc.gpsimd).memset(up[t][:, :U], 0.0)
         make_identity(nc, ident[:])
 
         w1_low = [keep.tile([P, P // 2, 2, PACK], BF16, name=f"w1_low{a}", align_bytes=64) for a in range(2)]
@@ -124,13 +123,13 @@ def tile_picked_devox_relu_p_kernel(tc, x_words, x_scales, w1, w2, gate, emb, of
             return (t, a, b, h)
 
         pieces = [first_layer(0, 0, HALF, "h0", 0)]
-        round_high(1, nc.scalar.copy)
-        quantize_high(1)
         round_low(1, nc.scalar.copy)
         quantize_low(1)
+        round_high(1, nc.scalar.copy)
+        quantize_high(1)
         pieces.append(first_layer(0, HALF, S, "w1_raw1", 1))
-        pieces.append(first_layer(2, 0, S, "h2", 2))
-        pieces.append(first_layer(1, 0, S, "h1", 3))
+        pieces.append(first_layer(1, 0, S, "h1", 2))
+        pieces.append(first_layer(2, 0, S, "h2", 3))
         pieces.append(first_layer(3, 0, S, "h3", 4))
 
         w2_bf = keep.tile([P, N, PACK], BF16, name="w2_bf", align_bytes=64)
@@ -153,44 +152,46 @@ def tile_picked_devox_relu_p_kernel(tc, x_words, x_scales, w1, w2, gate, emb, of
                 at = 2 * g % per_bank
                 nc.scalar.copy(turned_bf[g][:, :, a, :], banks[2 * g // per_bank][:, at : at + 2, :])
 
-        def add_plane(engine, t):
-            for c, cols in enumerate(pair_cols):
-                engine.tensor_tensor(pairs[c][:, 1, :, t - 2], up[t][:, cols], emb_t[t][:, cols], ADD)
-
         for t, a, b, h in pieces:
             nc.vector.tensor_copy(up[t][:].indirect(cell_t[:, a // LIST_ROWS : b // LIST_ROWS]), h[:])
             if b < S:
                 continue
             if t == 0:
-                turn(0, 4, 5)
-            if t == 2:
-                add_plane(nc.gpsimd, 2)
+                turn(0, 4, 3)
+            if t == 1:
                 nc.vector.quantize_mx(out=w2_code[:].bitcast(FP8X4), scales=w2_scale[:], in_=w2_bf[:].rearrange("p n j -> p (n j)"))
             if t == 1:
-                turn(1, 2, 0)
+                turn(1, 4, 5)
                 for c, cols in enumerate(pair_cols):
-                    back = bank(4 + c, [P, PAIR_WIDTHS[c]])
+                    back = bank((7 + c) % 8, [P, PAIR_WIDTHS[c]])
                     for b in range(cols.start // P, cols.stop // P):
                         words = turned_bf[b // 2][:].rearrange("r b a m -> r (b a m)").bitcast(F32)
                         at = b * P - cols.start
                         nc.tensor.transpose(back[:, at : at + P], words[:, (b % 2) * P : (b % 2 + 1) * P], ident[:])
                     nc.scalar.copy(pairs[c][:].rearrange("p u r e -> p (u r e)").bitcast(F32)[:, : PAIR_WIDTHS[c]], back[:])
-        add_plane(nc.vector, 3)
+        for c, cols in enumerate(pair_cols):
+            nc.vector.tensor_tensor(
+                pairs[c][:, 1].rearrange("p (g i) e -> p g e i", i=LINE),
+                up[2][:].rearrange("p (e r) -> p e r", e=2)[:, :, cols].rearrange("p e (g i) -> p g e i", i=LINE),
+                up[3][:].rearrange("p (e r) -> p e r", e=2)[:, ::-1, cols].rearrange("p e (g i) -> p g e i", i=LINE),
+                ADD,
+            )
 
         cols = [slice(sum(WIDTHS[:c]), sum(WIDTHS[: c + 1])) for c in range(len(WIDTHS))]
-        z_bf = [keep.tile([P, width * PACK], BF16, name=f"z_bf{c}", align_bytes=64) for c, width in enumerate(WIDTHS)]
+        z_all = keep.tile([P, U * PACK], BF16, name="turned_bf3", align_bytes=64)
+        z_bf = [z_all[:, span.start * PACK : span.stop * PACK] for span in cols]
         for c, span in enumerate(cols):
             home = max(k for k, whole in enumerate(pair_cols) if whole.start <= span.start)
             at = span.start - pair_cols[home].start
             nc.scalar.copy(
-                z_bf[c][:].bitcast(F32).rearrange("p (r u) -> p r u", u=2),
+                z_bf[c].bitcast(F32).rearrange("p (r u) -> p r u", u=2),
                 pairs[home][:].rearrange("p u r e -> p (u r e)").bitcast(F32).rearrange("p (u r) -> p r u", u=2)[:, at : at + WIDTHS[c]],
             )
         y = keep.tile([P, U], F32, name="y", align_bytes=64)
         for c, span in enumerate(cols):
             z_code = keep.tile([P, WIDTHS[c]], U32, name=f"z_code{c}", align_bytes=64)
             z_scale = keep.tile([P, WIDTHS[c]], U8, name=f"z_scale{c}", align_bytes=64)
-            nc.vector.quantize_mx(out=z_code[:].bitcast(FP8X4), scales=z_scale[:], in_=z_bf[c][:])
+            nc.vector.quantize_mx(out=z_code[:].bitcast(FP8X4), scales=z_scale[:], in_=z_bf[c])
             acc = bank(c, [P, WIDTHS[c]])
             nc.tensor.matmul_mx(
                 out=acc[:],
@@ -201,33 +202,32 @@ def tile_picked_devox_relu_p_kernel(tc, x_words, x_scales, w1, w2, gate, emb, of
                 start=True,
                 stop=True,
             )
-            if c < len(WIDTHS) - 1:
+            if c < len(WIDTHS) - 0:
                 nc.scalar.activation(y[:, span], acc[:], RELU)
             else:
                 nc.vector.tensor_scalar_max(y[:, span], acc[:], 0.0)
 
         terms = [keep.tile([P, V], F32, name=f"term{d}", align_bytes=64) for d in range(D)]
         halves = [slice(a * V // 2, (a + 1) * V // 2) for a in range(2)]
-        sum_turned = [bank(5 + a, [P, 2, P]) for a in range(2)]
-        for d in range(D):
-            nc.vector.tensor_tensor(terms[d][:], y[:].indirect(pos_t[d][:]), gate_t[:, d, :], MULT)
-            if d < 2:
-                for b in range(V // P):
-                    first = d == 0 and b % 2 == 0
-                    last = d == 1 and b % 2 == 1
-                    nc.tensor.matmul(sum_turned[b // 2][:, b % 2, :], terms[d][:, b * P : (b + 1) * P], ident[:], start=first, stop=last, is_transpose=True)
-        sum01 = []
-        for a in range(2):
-            staged = keep.tile([P, 2, P], F32, name=f"staged{a}", align_bytes=64)
-            nc.scalar.copy(staged[:], sum_turned[a][:])
-            acc = bank(a, [P, V // 2])
-            for b in range(2):
-                nc.tensor.transpose(acc[:, b * P : (b + 1) * P], staged[:, b, :], ident[:])
-            sum01.append(acc)
-        sum012 = keep.tile([P, V], F32, name="sum012", align_bytes=64)
-        for a, v in enumerate(halves):
-            nc.vector.tensor_tensor(sum012[:, v], terms[2][:, v], sum01[a][:], ADD)
-        for a, v in enumerate(halves):
-            res = keep.tile([P, V // 2], F32, name=f"res{a}", align_bytes=64)
-            nc.vector.tensor_tensor(res[:], sum012[:, v], terms[3][:, v], ADD)
-            (nc.sync if a == 0 else nc.scalar).dma_start(out[:, v], res[:])
+        sum_turned = [bank(4 + b, [P, P]) for b in range(V // P)]
+
+        def gather(d, v):
+            nc.vector.tensor_tensor(terms[d][:, v], y[:].indirect(pos_t[d][:, v.start // LIST_ROWS : v.stop // LIST_ROWS]), gate_t[:, d, v], MULT)
+            if d < D - 1:
+                for b in range(v.start // P, v.stop // P):
+                    nc.tensor.matmul(sum_turned[b][:], terms[d][:, b * P : (b + 1) * P], ident[:], start=d == 0, stop=d == D - 2, is_transpose=True)
+
+        gather(0, slice(0, V))
+        gather(1, slice(0, V))
+        for d in range(2, D):
+            for v in halves:
+                gather(d, v)
+        res = [keep.tile([P, V // 2], F32, name=f"res{a}", align_bytes=64) for a in range(2)]
+        for b in range(V // P):
+            staged = keep.tile([P, P], F32, name=f"staged{b}", align_bytes=64)
+            nc.scalar.copy(staged[:], sum_turned[b][:])
+            acc = bank(b, [P, P])
+            nc.tensor.transpose(acc[:], staged[:], ident[:])
+            nc.vector.tensor_tensor(res[b // 2][:, b % 2 * P : (b % 2 + 1) * P], terms[D - 1][:, b * P : (b + 1) * P], acc[:], ADD)
+            if b % 2 == 1:
+                (nc.sync if b == 1 else nc.scalar).dma_start(out[:, halves[b // 2]], res[b // 2][:])

@@ -49,13 +49,13 @@ def tile_picked_devox_relu_p_kernel(tc, x_words, x_scales, w1, w2, gate, emb, of
         ident = keep.tile([P, P], F32, name="ident", align_bytes=64)
 
         nc.gpsimd.memset(table_scales[:].bitcast(I32), 0)
+        nc.sync.dma_start(offs_t[:], offs)
         w1_rows = w1.rearrange("(p j) c -> p j c", j=PACK)
         nc.sync.dma_start(w1_raw[0][:], w1_rows[:, :, : H // 2])
-        nc.sync.dma_start(offs_t[:], offs)
-        nc.sync.dma_start(cell_t[:], cell)
         for q in range(P // QUADRANT):
             nc.sync.dma_start(table_scales[QUADRANT * q : QUADRANT * q + 4, :].bitcast(I32), x_scales[0, 4 * q : 4 * q + 4, :].bitcast(I32))
         nc.sync.dma_start(table_words[:].bitcast(I32), x_words[0].rearrange("p n r -> p (n r)").bitcast(I32))
+        nc.sync.dma_start(cell_t[:], cell)
         nc.sync.dma_start(w1_raw[1][:], w1_rows[:, :, H // 2 :])
         emb_planes = emb.rearrange("(p t) r -> p t r", t=PACK)
         nc.sync.dma_start(w2_raw[:], w2.rearrange("(p j) c -> p j c", j=PACK))
@@ -67,8 +67,12 @@ def tile_picked_devox_relu_p_kernel(tc, x_words, x_scales, w1, w2, gate, emb, of
         for d, pos in enumerate((pos1, pos2, pos3, pos4)):
             nc.sync.dma_start(pos_t[d][:], pos)
         nc.sync.dma_start(gate_t[:], gate.rearrange("d p v -> p d v"))
-        for t in range(PACK):
-            (nc.vector if t < 3 else nc.gpsimd).memset(up[t][:, :U], 0.0)
+        nc.gpsimd.memset(up[0][:], 0.0)
+        up_first = keep.tile([P, U], F32, name="up_first", align_bytes=64)
+        nc.scalar.copy(up_first[:], up[0][:])
+        nc.scalar.copy(up[1][:], up[0][:])
+        for t in range(2, PACK):
+            nc.vector.tensor_copy(up[t][:, :U], up[0][:])
         make_identity(nc, ident[:])
 
         w1_low = [keep.tile([P, P // 2, 2, PACK], BF16, name=f"w1_low{a}", align_bytes=64) for a in range(2)]
@@ -95,7 +99,7 @@ def tile_picked_devox_relu_p_kernel(tc, x_words, x_scales, w1, w2, gate, emb, of
                 )
 
         round_low(0, nc.vector.tensor_copy)
-        round_high(0, nc.scalar.copy)
+        round_high(0, nc.vector.tensor_copy)
         x_scale = keep.tile([P, S], U8, name="x_scale", align_bytes=64)
         nc.vector.tensor_copy(x_scale[:], table_scales[:].indirect(offs_t[:]))
         quantize_low(0)
@@ -122,7 +126,7 @@ def tile_picked_devox_relu_p_kernel(tc, x_words, x_scales, w1, w2, gate, emb, of
             nc.scalar.activation(h[:], acc[:], RELU)
             return (t, a, b, h)
 
-        pieces = [first_layer(0, 0, HALF, "h0", 0)]
+        pieces = [first_layer(0, 0, P, "h_first", 7), first_layer(0, P, HALF, "h0", 0)]
         round_low(1, nc.scalar.copy)
         quantize_low(1)
         round_high(1, nc.scalar.copy)
@@ -143,7 +147,7 @@ def tile_picked_devox_relu_p_kernel(tc, x_words, x_scales, w1, w2, gate, emb, of
 
         def turn(a, per_bank, first_bank):
             banks = [bank(first_bank + g, [P, per_bank, P]) for g in range(U // P // per_bank)]
-            for source in (emb_t[a], up[a]):
+            for source in (emb_t[a], up_first, up[a]) if a == 0 else (emb_t[a], up[a]):
                 for b in range(U // P):
                     first = source is emb_t[a] and b % per_bank == 0
                     last = source is up[a] and b % per_bank == per_bank - 1
@@ -153,7 +157,7 @@ def tile_picked_devox_relu_p_kernel(tc, x_words, x_scales, w1, w2, gate, emb, of
                 nc.scalar.copy(turned_bf[g][:, :, a, :], banks[2 * g // per_bank][:, at : at + 2, :])
 
         for t, a, b, h in pieces:
-            nc.vector.tensor_copy(up[t][:].indirect(cell_t[:, a // LIST_ROWS : b // LIST_ROWS]), h[:])
+            nc.vector.tensor_copy((up_first if b == P else up[t])[:].indirect(cell_t[:, a // LIST_ROWS : b // LIST_ROWS]), h[:])
             if b < S:
                 continue
             if t == 0:

@@ -49,13 +49,13 @@ def tile_picked_devox_relu_p_kernel(tc, x_words, x_scales, w1, w2, gate, emb, of
         ident = keep.tile([P, P], F32, name="ident", align_bytes=64)
 
         nc.gpsimd.memset(table_scales[:].bitcast(I32), 0)
-        nc.sync.dma_start(offs_t[:], offs)
         w1_rows = w1.rearrange("(p j) c -> p j c", j=PACK)
         nc.sync.dma_start(w1_raw[0][:], w1_rows[:, :, : H // 2])
+        nc.sync.dma_start(offs_t[:], offs)
+        nc.sync.dma_start(cell_t[:], cell)
         for q in range(P // QUADRANT):
             nc.sync.dma_start(table_scales[QUADRANT * q : QUADRANT * q + 4, :].bitcast(I32), x_scales[0, 4 * q : 4 * q + 4, :].bitcast(I32))
         nc.sync.dma_start(table_words[:].bitcast(I32), x_words[0].rearrange("p n r -> p (n r)").bitcast(I32))
-        nc.sync.dma_start(cell_t[:], cell)
         nc.sync.dma_start(w1_raw[1][:], w1_rows[:, :, H // 2 :])
         emb_planes = emb.rearrange("(p t) r -> p t r", t=PACK)
         nc.sync.dma_start(w2_raw[:], w2.rearrange("(p j) c -> p j c", j=PACK))
@@ -67,43 +67,36 @@ def tile_picked_devox_relu_p_kernel(tc, x_words, x_scales, w1, w2, gate, emb, of
         for d, pos in enumerate((pos1, pos2, pos3, pos4)):
             nc.sync.dma_start(pos_t[d][:], pos)
         nc.sync.dma_start(gate_t[:], gate.rearrange("d p v -> p d v"))
-        nc.gpsimd.memset(up[0][:], 0.0)
         up_first = keep.tile([P, U], F32, name="up_first", align_bytes=64)
-        nc.scalar.copy(up_first[:], up[0][:])
-        nc.scalar.copy(up[1][:], up[0][:])
-        for t in range(2, PACK):
-            nc.vector.tensor_copy(up[t][:, :U], up[0][:])
+        nc.vector.memset(up[0][:], 0.0)
+        nc.vector.memset(up_first[:], 0.0)
+        for t in range(1, PACK):
+            nc.scalar.copy(up[t][:, :U], up[0][:])
         make_identity(nc, ident[:])
 
         w1_low = [keep.tile([P, P // 2, 2, PACK], BF16, name=f"w1_low{a}", align_bytes=64) for a in range(2)]
-        w1_high = [keep.tile([P, 2, P // 2, PACK], BF16, name=f"w1_high{a}", align_bytes=64) for a in range(2)]
-        w1_code = [keep.tile([P, P], U32, name=f"w1_code{t}", align_bytes=64) for t in range(PACK)]
-        w1_scale = [keep.tile([P, P], U8, name=f"w1_scale{t}", align_bytes=64) for t in range(PACK)]
+        w1_high = keep.tile([P, 2, P, PACK], BF16, name="w1_high", align_bytes=64)
+        low_code = [keep.tile([P, P], U32, name=f"low_code{a}", align_bytes=64) for a in range(2)]
+        low_scale = [keep.tile([P, P], U8, name=f"low_scale{a}", align_bytes=64) for a in range(2)]
+        high_code = keep.tile([P, 2 * P], U32, name="high_code", align_bytes=64)
+        high_scale = keep.tile([P, 2 * P], U8, name="high_scale", align_bytes=64)
+        w1_code = [low_code[0][:], low_code[1][:], high_code[:, :P], high_code[:, P:]]
+        w1_scale = [low_scale[0][:], low_scale[1][:], high_scale[:, :P], high_scale[:, P:]]
 
         def round_low(a, copy):
             copy(w1_low[a][:], w1_raw[a][:].rearrange("p j (m t) -> p m t j", t=PACK)[:, :, :2])
 
         def round_high(a, copy):
-            copy(w1_high[a][:].rearrange("p f m j -> p m f j"), w1_raw[a][:].rearrange("p j (m t) -> p m t j", t=PACK)[:, :, 2:])
+            copy(w1_high[:, :, a * P // 2 : (a + 1) * P // 2, :].rearrange("p f m j -> p m f j"), w1_raw[a][:].rearrange("p j (m t) -> p m t j", t=PACK)[:, :, 2:])
 
         def quantize_low(a):
-            nc.vector.quantize_mx(out=w1_code[a][:].bitcast(FP8X4), scales=w1_scale[a][:], in_=w1_low[a][:].rearrange("p m e j -> p (m e j)"))
-
-        def quantize_high(a):
-            half = slice(a * P // 2, (a + 1) * P // 2)
-            for f in range(2):
-                nc.vector.quantize_mx(
-                    out=w1_code[2 + f][:, half].bitcast(FP8X4),
-                    scales=w1_scale[2 + f][:, half],
-                    in_=w1_high[a][:, f].rearrange("p m j -> p (m j)"),
-                )
+            nc.vector.quantize_mx(out=w1_code[a].bitcast(FP8X4), scales=w1_scale[a], in_=w1_low[a][:].rearrange("p m e j -> p (m e j)"))
 
         round_low(0, nc.vector.tensor_copy)
-        round_high(0, nc.vector.tensor_copy)
+        round_high(0, nc.scalar.copy)
         x_scale = keep.tile([P, S], U8, name="x_scale", align_bytes=64)
         nc.vector.tensor_copy(x_scale[:], table_scales[:].indirect(offs_t[:]))
         quantize_low(0)
-        quantize_high(0)
         x_code = keep.tile([P, S], U32, name="x_code", align_bytes=64)
         for a in range(2):
             nc.vector.tensor_copy(
@@ -116,8 +109,8 @@ def tile_picked_devox_relu_p_kernel(tc, x_words, x_scales, w1, w2, gate, emb, of
             acc = bank(index, [P, b - a])
             nc.tensor.matmul_mx(
                 out=acc[:],
-                lhsT=w1_code[t][:].bitcast(FP8X4),
-                lhsT_scale=w1_scale[t][:],
+                lhsT=w1_code[t].bitcast(FP8X4),
+                lhsT_scale=w1_scale[t],
                 rhs=x_code[:, a:b].bitcast(FP8X4),
                 rhs_scale=x_scale[:, a:b],
                 start=True,
@@ -130,7 +123,7 @@ def tile_picked_devox_relu_p_kernel(tc, x_words, x_scales, w1, w2, gate, emb, of
         round_low(1, nc.scalar.copy)
         quantize_low(1)
         round_high(1, nc.scalar.copy)
-        quantize_high(1)
+        nc.vector.quantize_mx(out=high_code[:].bitcast(FP8X4), scales=high_scale[:], in_=w1_high[:].rearrange("p f m j -> p (f m j)"))
         pieces.append(first_layer(0, HALF, S, "w1_raw1", 1))
         pieces.append(first_layer(1, 0, S, "h1", 2))
         pieces.append(first_layer(2, 0, S, "h2", 3))

@@ -62,8 +62,8 @@ def tile_picked_devox_relu_p_kernel(tc, x_words, x_scales, w1, w2, gate, emb, of
         for a in range(2):
             for e in range(2):
                 nc.sync.dma_start(emb_t[a][e:P:2, :], emb_planes[a * P // 2 : (a + 1) * P // 2, e, :])
-        nc.sync.dma_start(up[2][:, U:], emb_planes[:, 3, :])
         nc.sync.dma_start(up[3][:, U:], emb_planes[:, 2, :])
+        nc.sync.dma_start(up[2][:, U:], emb_planes[:, 3, :])
         for d, pos in enumerate((pos1, pos2, pos3, pos4)):
             nc.sync.dma_start(pos_t[d][:], pos)
         nc.sync.dma_start(gate_t[:], gate.rearrange("d p v -> p d v"))
@@ -131,7 +131,6 @@ def tile_picked_devox_relu_p_kernel(tc, x_words, x_scales, w1, w2, gate, emb, of
 
         w2_bf = keep.tile([P, N, PACK], BF16, name="w2_bf", align_bytes=64)
         nc.scalar.copy(w2_bf[:], w2_raw[:].rearrange("p j n -> p n j"))
-        w2_code = keep.tile([P, N], U32, name="w2_code", align_bytes=64)
         w2_scale = keep.tile([P, N], U8, name="w2_scale", align_bytes=64)
 
         pair_cols = [slice(sum(PAIR_WIDTHS[:c]), sum(PAIR_WIDTHS[: c + 1])) for c in range(len(PAIR_WIDTHS))]
@@ -156,8 +155,6 @@ def tile_picked_devox_relu_p_kernel(tc, x_words, x_scales, w1, w2, gate, emb, of
             if t == 0:
                 turn(0, 4, 3)
             if t == 1:
-                nc.vector.quantize_mx(out=w2_code[:].bitcast(FP8X4), scales=w2_scale[:], in_=w2_bf[:].rearrange("p n j -> p (n j)"))
-            if t == 1:
                 turn(1, 4, 5)
                 for c, cols in enumerate(pair_cols):
                     back = bank((7 + c) % 8, [P, PAIR_WIDTHS[c]])
@@ -166,6 +163,8 @@ def tile_picked_devox_relu_p_kernel(tc, x_words, x_scales, w1, w2, gate, emb, of
                         at = b * P - cols.start
                         nc.tensor.transpose(back[:, at : at + P], words[:, (b % 2) * P : (b % 2 + 1) * P], ident[:])
                     nc.scalar.copy(pairs[c][:].rearrange("p u r e -> p (u r e)").bitcast(F32)[:, : PAIR_WIDTHS[c]], back[:])
+        w2_code = keep.tile([P, N], U32, name="h2", align_bytes=64)
+        nc.vector.quantize_mx(out=w2_code[:].bitcast(FP8X4), scales=w2_scale[:], in_=w2_bf[:].rearrange("p n j -> p (n j)"))
         for c, cols in enumerate(pair_cols):
             nc.vector.tensor_tensor(
                 pairs[c][:, 1].rearrange("p (g i) e -> p g e i", i=LINE),
@@ -207,12 +206,18 @@ def tile_picked_devox_relu_p_kernel(tc, x_words, x_scales, w1, w2, gate, emb, of
         terms = [keep.tile([P, V], F32, name=f"term{d}", align_bytes=64) for d in range(D)]
         halves = [slice(a * V // 2, (a + 1) * V // 2) for a in range(2)]
         sum_turned = [bank(4 + b, [P, P]) for b in range(V // P)]
+        summed = (3, 2)
 
         def gather(d, v):
             nc.vector.tensor_tensor(terms[d][:, v], y[:].indirect(pos_t[d][:, v.start // LIST_ROWS : v.stop // LIST_ROWS]), gate_t[:, d, v], MULT)
-            if d < D - 1:
-                for b in range(v.start // P, v.stop // P):
-                    nc.tensor.matmul(sum_turned[b][:], terms[d][:, b * P : (b + 1) * P], ident[:], start=d == 0, stop=d == D - 2, is_transpose=True)
+            for b in range(v.start // P, v.stop // P):
+                if d < summed[b // 2]:
+                    nc.tensor.matmul(sum_turned[b][:], terms[d][:, b * P : (b + 1) * P], ident[:], start=d == 0, stop=d == summed[b // 2] - 1, is_transpose=True)
+
+        def turn_back(b, acc):
+            staged = keep.tile([P, P], F32, name=f"staged{b}", align_bytes=64)
+            nc.scalar.copy(staged[:], sum_turned[b][:])
+            nc.tensor.transpose(acc, staged[:], ident[:])
 
         gather(0, slice(0, V))
         gather(1, slice(0, V))
@@ -220,11 +225,15 @@ def tile_picked_devox_relu_p_kernel(tc, x_words, x_scales, w1, w2, gate, emb, of
             for v in halves:
                 gather(d, v)
         res = [keep.tile([P, V // 2], F32, name=f"res{a}", align_bytes=64) for a in range(2)]
-        for b in range(V // P):
-            staged = keep.tile([P, P], F32, name=f"staged{b}", align_bytes=64)
-            nc.scalar.copy(staged[:], sum_turned[b][:])
+        sum01 = bank(2, [P, V // 2])
+        for b in range(2):
+            turn_back(2 + b, sum01[:, b * P : (b + 1) * P])
+        sum012 = keep.tile([P, V // 2], F32, name="sum012", align_bytes=64)
+        nc.vector.tensor_tensor(sum012[:], terms[2][:, halves[1]], sum01[:], ADD)
+        for b in range(2):
             acc = bank(b, [P, P])
-            nc.tensor.transpose(acc[:], staged[:], ident[:])
-            nc.vector.tensor_tensor(res[b // 2][:, b % 2 * P : (b % 2 + 1) * P], terms[D - 1][:, b * P : (b + 1) * P], acc[:], ADD)
-            if b % 2 == 1:
-                (nc.sync if b == 1 else nc.scalar).dma_start(out[:, halves[b // 2]], res[b // 2][:])
+            turn_back(b, acc[:])
+            nc.vector.tensor_tensor(res[0][:, b * P : (b + 1) * P], terms[D - 1][:, b * P : (b + 1) * P], acc[:], ADD)
+        nc.sync.dma_start(out[:, halves[0]], res[0][:])
+        nc.vector.tensor_tensor(res[1][:], sum012[:], terms[D - 1][:, halves[1]], ADD)
+        nc.scalar.dma_start(out[:, halves[1]], res[1][:])

@@ -58,12 +58,16 @@ def tile_picked_devox_relu_p_kernel(tc, x_words, x_scales, w1, w2, gate, emb, of
         nc.sync.dma_start(table_words[:].bitcast(I32), x_words[0].rearrange("p n r -> p (n r)").bitcast(I32))
         nc.sync.dma_start(w1_raw[1][:], w1_rows[:, :, H // 2 :])
         emb_planes = emb.rearrange("(p t) r -> p t r", t=PACK)
-        nc.sync.dma_start(w2_raw[:], w2.rearrange("(p j) c -> p j c", j=PACK))
-        for a in range(2):
+
+        def load_pairs(a):
             for e in range(2):
                 nc.sync.dma_start(emb_t[a][e:P:2, :], emb_planes[a * P // 2 : (a + 1) * P // 2, e, :])
+
+        nc.sync.dma_start(w2_raw[:], w2.rearrange("(p j) c -> p j c", j=PACK))
+        load_pairs(0)
         nc.sync.dma_start(up[3][:, U:], emb_planes[:, 2, :])
         nc.sync.dma_start(up[2][:, U:], emb_planes[:, 3, :])
+        load_pairs(1)
         for d, pos in enumerate((pos1, pos2, pos3, pos4)):
             nc.sync.dma_start(pos_t[d][:], pos)
         nc.sync.dma_start(gate_t[:], gate.rearrange("d p v -> p d v"))
@@ -104,33 +108,32 @@ def tile_picked_devox_relu_p_kernel(tc, x_words, x_scales, w1, w2, gate, emb, of
                 table_words[:].indirect(offs_t[:, a * HALF // LIST_ROWS : (a + 1) * HALF // LIST_ROWS]),
             )
 
-        def first_layer(t, a, b, buffer, index):
-            h = keep.tile([P, b - a], F32, name=buffer, align_bytes=64)
-            acc = bank(index, [P, b - a])
-            nc.tensor.matmul_mx(
-                out=acc[:],
-                lhsT=w1_code[t].bitcast(FP8X4),
-                lhsT_scale=w1_scale[t],
-                rhs=x_code[:, a:b].bitcast(FP8X4),
-                rhs_scale=x_scale[:, a:b],
-                start=True,
-                stop=True,
-            )
-            nc.scalar.activation(h[:], acc[:], RELU)
-            return (t, a, b, h)
+        def first_layer(t, cuts, buffer, banks):
+            h = keep.tile([P, cuts[-1] - cuts[0]], F32, name=buffer, align_bytes=64)
+            for a, b, index in zip(cuts, cuts[1:], banks):
+                acc = bank(index, [P, b - a])
+                nc.tensor.matmul_mx(
+                    out=acc[:],
+                    lhsT=w1_code[t].bitcast(FP8X4),
+                    lhsT_scale=w1_scale[t],
+                    rhs=x_code[:, a:b].bitcast(FP8X4),
+                    rhs_scale=x_scale[:, a:b],
+                    start=True,
+                    stop=True,
+                )
+                nc.scalar.activation(h[:, a - cuts[0] : b - cuts[0]], acc[:], RELU)
+            return (t, cuts[0], cuts[-1], h)
 
-        pieces = [first_layer(0, 0, P, "h_first", 7), first_layer(0, P, HALF, "h0", 0)]
+        pieces = [first_layer(0, (0, P), "h_first", (7,)), first_layer(0, (P, HALF), "h0", (0,))]
         round_low(1, nc.scalar.copy)
         quantize_low(1)
         round_high(1, nc.scalar.copy)
         nc.vector.quantize_mx(out=high_code[:].bitcast(FP8X4), scales=high_scale[:], in_=w1_high[:].rearrange("p f m j -> p (f m j)"))
-        pieces.append(first_layer(0, HALF, S, "w1_raw1", 1))
-        pieces.append(first_layer(1, 0, S, "h1", 2))
-        pieces.append(first_layer(2, 0, S, "h2", 3))
-        pieces.append(first_layer(3, 0, S, "h3", 4))
+        pieces.append(first_layer(0, (HALF, S), "w1_raw1", (1,)))
+        pieces.append(first_layer(1, (0, HALF, S), "h1", (2, 7)))
+        pieces.append(first_layer(2, (0, S), "h2", (3,)))
+        pieces.append(first_layer(3, (0, S), "h3", (4,)))
 
-        w2_bf = keep.tile([P, N, PACK], BF16, name="w2_bf", align_bytes=64)
-        nc.scalar.copy(w2_bf[:], w2_raw[:].rearrange("p j n -> p n j"))
         w2_scale = keep.tile([P, N], U8, name="w2_scale", align_bytes=64)
 
         pair_cols = [slice(sum(PAIR_WIDTHS[:c]), sum(PAIR_WIDTHS[: c + 1])) for c in range(len(PAIR_WIDTHS))]
@@ -155,6 +158,8 @@ def tile_picked_devox_relu_p_kernel(tc, x_words, x_scales, w1, w2, gate, emb, of
             if t == 0:
                 turn(0, 4, 3)
             if t == 1:
+                w2_bf = keep.tile([P, N, PACK], BF16, name="h1", align_bytes=64)
+                nc.scalar.copy(w2_bf[:], w2_raw[:].rearrange("p j n -> p n j"))
                 turn(1, 4, 5)
                 for c, cols in enumerate(pair_cols):
                     back = bank((7 + c) % 8, [P, PAIR_WIDTHS[c]])
@@ -206,18 +211,12 @@ def tile_picked_devox_relu_p_kernel(tc, x_words, x_scales, w1, w2, gate, emb, of
         terms = [keep.tile([P, V], F32, name=f"term{d}", align_bytes=64) for d in range(D)]
         halves = [slice(a * V // 2, (a + 1) * V // 2) for a in range(2)]
         sum_turned = [bank(4 + b, [P, P]) for b in range(V // P)]
-        summed = (3, 2)
 
         def gather(d, v):
             nc.vector.tensor_tensor(terms[d][:, v], y[:].indirect(pos_t[d][:, v.start // LIST_ROWS : v.stop // LIST_ROWS]), gate_t[:, d, v], MULT)
-            for b in range(v.start // P, v.stop // P):
-                if d < summed[b // 2]:
-                    nc.tensor.matmul(sum_turned[b][:], terms[d][:, b * P : (b + 1) * P], ident[:], start=d == 0, stop=d == summed[b // 2] - 1, is_transpose=True)
-
-        def turn_back(b, acc):
-            staged = keep.tile([P, P], F32, name=f"staged{b}", align_bytes=64)
-            nc.scalar.copy(staged[:], sum_turned[b][:])
-            nc.tensor.transpose(acc, staged[:], ident[:])
+            if d < D - 1:
+                for b in range(v.start // P, v.stop // P):
+                    nc.tensor.matmul(sum_turned[b][:], terms[d][:, b * P : (b + 1) * P], ident[:], start=d == 0, stop=d == D - 2, is_transpose=True)
 
         gather(0, slice(0, V))
         gather(1, slice(0, V))
@@ -225,15 +224,11 @@ def tile_picked_devox_relu_p_kernel(tc, x_words, x_scales, w1, w2, gate, emb, of
             for v in halves:
                 gather(d, v)
         res = [keep.tile([P, V // 2], F32, name=f"res{a}", align_bytes=64) for a in range(2)]
-        sum01 = bank(2, [P, V // 2])
-        for b in range(2):
-            turn_back(2 + b, sum01[:, b * P : (b + 1) * P])
-        sum012 = keep.tile([P, V // 2], F32, name="sum012", align_bytes=64)
-        nc.vector.tensor_tensor(sum012[:], terms[2][:, halves[1]], sum01[:], ADD)
-        for b in range(2):
+        for b in range(V // P):
+            staged = keep.tile([P, P], F32, name=f"staged{b}", align_bytes=64)
+            nc.scalar.copy(staged[:], sum_turned[b][:])
             acc = bank(b, [P, P])
-            turn_back(b, acc[:])
-            nc.vector.tensor_tensor(res[0][:, b * P : (b + 1) * P], terms[D - 1][:, b * P : (b + 1) * P], acc[:], ADD)
-        nc.sync.dma_start(out[:, halves[0]], res[0][:])
-        nc.vector.tensor_tensor(res[1][:], sum012[:], terms[D - 1][:, halves[1]], ADD)
-        nc.scalar.dma_start(out[:, halves[1]], res[1][:])
+            nc.tensor.transpose(acc[:], staged[:], ident[:])
+            nc.vector.tensor_tensor(res[b // 2][:, b % 2 * P : (b % 2 + 1) * P], terms[D - 1][:, b * P : (b + 1) * P], acc[:], ADD)
+            if b % 2 == 1:
+                (nc.sync if b == 1 else nc.scalar).dma_start(out[:, halves[b // 2]], res[b // 2][:])

@@ -15,6 +15,7 @@ U8 = mybir.dt.uint8
 FP8X4 = mybir.dt.float8_e4m3fn_x4
 ADD = mybir.AluOpType.add
 MULT = mybir.AluOpType.mult
+COPY = mybir.ActivationFunctionType.Copy
 RELU = mybir.ActivationFunctionType.Relu
 
 P = 128
@@ -23,6 +24,7 @@ LIST_ROWS = 16
 QUADRANT = 32
 LINE = 4
 HALF = S // 2
+W1_VECTOR = 80
 PAIR_WIDTHS = (256, 256, 256, 256)
 WIDTHS = (256, 256, 256, 128, 128)
 
@@ -41,158 +43,106 @@ def tile_picked_devox_relu_p_kernel(tc, x_words, x_scales, w1, w2, gate, emb, of
         pos_t = [keep.tile([P, V // LIST_ROWS], U16, name=f"pos_t{d}") for d in range(D)]
         table_words = keep.tile([P, T], U32, name="table_words", align_bytes=64)
         table_scales = keep.tile([P, T], U8, name="table_scales", align_bytes=64)
-        w1_raw = [keep.tile([P, PACK, H // 2], F32, name=f"w1_raw{a}", align_bytes=64) for a in range(2)]
+        w1_raw = keep.tile([P, PACK, H], F32, name="w1_raw", align_bytes=64)
         w2_raw = keep.tile([P, PACK, N], F32, name="w2_raw", align_bytes=64)
-        emb_t = [keep.tile([P, U], F32, name=f"emb_t{t}", align_bytes=64) for t in range(2)]
-        gate_t = keep.tile([P, D, V], F32, name="gate_t", align_bytes=64)
-        up = [keep.tile([P, U if t < 2 else 2 * U], F32, name=f"up{t}", align_bytes=64) for t in range(PACK)]
+        gate_t = keep.tile([P, 2, V], F32, name="gate_t", align_bytes=64)
+        gate_rows = keep.tile([P, P], F32, name="gate_rows", align_bytes=64)
+        up = [keep.tile([P, 2 * U], F32, name=f"up{t}", align_bytes=64) for t in range(PACK)]
         ident = keep.tile([P, P], F32, name="ident", align_bytes=64)
 
         nc.gpsimd.memset(table_scales[:].bitcast(I32), 0)
-        w1_rows = w1.rearrange("(p j) c -> p j c", j=PACK)
-        nc.sync.dma_start(w1_raw[0][:], w1_rows[:, :, : H // 2])
+        nc.gpsimd.memset(gate_rows[:], 0.0)
         nc.sync.dma_start(offs_t[:], offs)
-        nc.sync.dma_start(cell_t[:], cell)
+        nc.sync.dma_start(w1_raw[:], w1.rearrange("(p j) c -> p j c", j=PACK))
         for q in range(P // QUADRANT):
             nc.sync.dma_start(table_scales[QUADRANT * q : QUADRANT * q + 4, :].bitcast(I32), x_scales[0, 4 * q : 4 * q + 4, :].bitcast(I32))
         nc.sync.dma_start(table_words[:].bitcast(I32), x_words[0].rearrange("p n r -> p (n r)").bitcast(I32))
-        nc.sync.dma_start(w1_raw[1][:], w1_rows[:, :, H // 2 :])
+        nc.sync.dma_start(cell_t[:], cell)
         emb_planes = emb.rearrange("(p t) r -> p t r", t=PACK)
-
-        def load_pairs(a):
-            for e in range(2):
-                nc.sync.dma_start(emb_t[a][e:P:2, :], emb_planes[a * P // 2 : (a + 1) * P // 2, e, :])
-
+        for t in (0, 2, 1, 3):
+            nc.sync.dma_start(up[t][:, U:], emb_planes[:, t ^ 1, :])
         nc.sync.dma_start(w2_raw[:], w2.rearrange("(p j) c -> p j c", j=PACK))
-        load_pairs(0)
-        nc.sync.dma_start(up[3][:, U:], emb_planes[:, 2, :])
-        nc.sync.dma_start(up[2][:, U:], emb_planes[:, 3, :])
-        load_pairs(1)
         for d, pos in enumerate((pos1, pos2, pos3, pos4)):
             nc.sync.dma_start(pos_t[d][:], pos)
-        nc.sync.dma_start(gate_t[:], gate.rearrange("d p v -> p d v"))
-        up_first = keep.tile([P, U], F32, name="up_first", align_bytes=64)
-        nc.vector.memset(up[0][:], 0.0)
-        nc.vector.memset(up_first[:], 0.0)
-        for t in range(1, PACK):
-            nc.scalar.copy(up[t][:, :U], up[0][:])
+        nc.sync.dma_start(gate_t[:], gate[:2].rearrange("d p v -> p d v"))
+        for d in range(2, D):
+            nc.sync.dma_start(gate_rows[4 * (d - 2) : 4 * (d - 1), :], gate[d, 0].rearrange("(b c) -> b c", c=P))
+        for t in range(PACK):
+            nc.vector.memset(up[t][:, :U], 0.0)
         make_identity(nc, ident[:])
 
-        w1_low = [keep.tile([P, P // 2, 2, PACK], BF16, name=f"w1_low{a}", align_bytes=64) for a in range(2)]
-        w1_high = keep.tile([P, 2, P, PACK], BF16, name="w1_high", align_bytes=64)
-        low_code = [keep.tile([P, P], U32, name=f"low_code{a}", align_bytes=64) for a in range(2)]
-        low_scale = [keep.tile([P, P], U8, name=f"low_scale{a}", align_bytes=64) for a in range(2)]
-        high_code = keep.tile([P, 2 * P], U32, name="high_code", align_bytes=64)
-        high_scale = keep.tile([P, 2 * P], U8, name="high_scale", align_bytes=64)
-        w1_code = [low_code[0][:], low_code[1][:], high_code[:, :P], high_code[:, P:]]
-        w1_scale = [low_scale[0][:], low_scale[1][:], high_scale[:, :P], high_scale[:, P:]]
-
-        def round_low(a, copy):
-            copy(w1_low[a][:], w1_raw[a][:].rearrange("p j (m t) -> p m t j", t=PACK)[:, :, :2])
-
-        def round_high(a, copy):
-            copy(w1_high[:, :, a * P // 2 : (a + 1) * P // 2, :].rearrange("p f m j -> p m f j"), w1_raw[a][:].rearrange("p j (m t) -> p m t j", t=PACK)[:, :, 2:])
-
-        def quantize_low(a):
-            nc.vector.quantize_mx(out=w1_code[a].bitcast(FP8X4), scales=w1_scale[a], in_=w1_low[a][:].rearrange("p m e j -> p (m e j)"))
-
-        round_low(0, nc.vector.tensor_copy)
-        round_high(0, nc.scalar.copy)
+        w1_bf = keep.tile([P, PACK, P, PACK], BF16, name="w1_bf", align_bytes=64)
+        w1_code = keep.tile([P, H], U32, name="w1_code", align_bytes=64)
+        w1_scale = keep.tile([P, H], U8, name="w1_scale", align_bytes=64)
+        for copy, cols in ((nc.vector.tensor_copy, slice(0, W1_VECTOR)), (nc.scalar.copy, slice(W1_VECTOR, P))):
+            copy(w1_bf[:, :, cols, :].rearrange("p t m j -> p m t j"), w1_raw[:].rearrange("p j (m t) -> p m t j", t=PACK)[:, cols])
         x_scale = keep.tile([P, S], U8, name="x_scale", align_bytes=64)
         nc.vector.tensor_copy(x_scale[:], table_scales[:].indirect(offs_t[:]))
-        quantize_low(0)
-        x_code = keep.tile([P, S], U32, name="x_code", align_bytes=64)
+        nc.vector.quantize_mx(out=w1_code[:].bitcast(FP8X4), scales=w1_scale[:], in_=w1_bf[:].rearrange("p t m j -> p (t m j)"))
+        x_code = [keep.tile([P, HALF], U32, name=f"x_code{a}", align_bytes=64) for a in range(2)]
         for a in range(2):
-            nc.vector.tensor_copy(
-                x_code[:, a * HALF : (a + 1) * HALF],
-                table_words[:].indirect(offs_t[:, a * HALF // LIST_ROWS : (a + 1) * HALF // LIST_ROWS]),
+            nc.vector.tensor_copy(x_code[a][:], table_words[:].indirect(offs_t[:, a * HALF // LIST_ROWS : (a + 1) * HALF // LIST_ROWS]))
+
+        def first_layer(t, a, index):
+            h = keep.tile([P, HALF], F32, name=f"h{t}{a}", align_bytes=64)
+            acc = bank(index, [P, HALF])
+            nc.tensor.matmul_mx(
+                out=acc[:],
+                lhsT=w1_code[:, t * P : (t + 1) * P].bitcast(FP8X4),
+                lhsT_scale=w1_scale[:, t * P : (t + 1) * P],
+                rhs=x_code[a][:].bitcast(FP8X4),
+                rhs_scale=x_scale[:, a * HALF : (a + 1) * HALF],
+                start=True,
+                stop=True,
             )
+            nc.scalar.activation(h[:], acc[:], RELU)
+            return h
 
-        def first_layer(t, cuts, buffer, banks):
-            h = keep.tile([P, cuts[-1] - cuts[0]], F32, name=buffer, align_bytes=64)
-            for a, b, index in zip(cuts, cuts[1:], banks):
-                acc = bank(index, [P, b - a])
-                nc.tensor.matmul_mx(
-                    out=acc[:],
-                    lhsT=w1_code[t].bitcast(FP8X4),
-                    lhsT_scale=w1_scale[t],
-                    rhs=x_code[:, a:b].bitcast(FP8X4),
-                    rhs_scale=x_scale[:, a:b],
-                    start=True,
-                    stop=True,
-                )
-                nc.scalar.activation(h[:, a - cuts[0] : b - cuts[0]], acc[:], RELU)
-            return (t, cuts[0], cuts[-1], h)
-
-        pieces = [first_layer(0, (0, P), "h_first", (7,)), first_layer(0, (P, HALF), "h0", (0,))]
-        round_low(1, nc.scalar.copy)
-        quantize_low(1)
-        round_high(1, nc.scalar.copy)
-        nc.vector.quantize_mx(out=high_code[:].bitcast(FP8X4), scales=high_scale[:], in_=w1_high[:].rearrange("p f m j -> p (f m j)"))
-        pieces.append(first_layer(0, (HALF, S), "w1_raw1", (1,)))
-        pieces.append(first_layer(1, (0, HALF, S), "h1", (2, 7)))
-        pieces.append(first_layer(2, (0, S), "h2", (3,)))
-        pieces.append(first_layer(3, (0, S), "h3", (4,)))
+        order = [(0, 0), (1, 0), (2, 0), (0, 1), (1, 1), (3, 0), (2, 1), (3, 1)]
+        h = {key: first_layer(*key, index) for index, key in enumerate(order)}
+        for a in range(2):
+            part = cell_t[:, a * HALF // LIST_ROWS : (a + 1) * HALF // LIST_ROWS]
+            for t in range(2):
+                nc.vector.tensor_copy(up[t][:].indirect(part), h[t, a][:])
+            for t in range(2, PACK):
+                nc.scalar.activation(up[t][:].indirect(part), h[t, a][:], COPY)
 
         w2_scale = keep.tile([P, N], U8, name="w2_scale", align_bytes=64)
+        w2_bf = keep.tile([P, N, PACK], BF16, name="w2_bf", align_bytes=64)
+        nc.gpsimd.tensor_copy(w2_bf[:], w2_raw[:].rearrange("p j n -> p n j"))
+        w2_code = keep.tile([P, N], U32, name="h11", align_bytes=64)
+        nc.vector.quantize_mx(out=w2_code[:].bitcast(FP8X4), scales=w2_scale[:], in_=w2_bf[:].rearrange("p n j -> p (n j)"))
+
+        gate_bank = bank(7, [P, P])
+        nc.tensor.transpose(gate_bank[:], gate_rows[:], ident[:])
+        gate_cols = keep.tile([P, 8], F32, name="gate_cols", align_bytes=64)
+        nc.vector.tensor_copy(gate_cols[:], gate_bank[:, :8])
 
         pair_cols = [slice(sum(PAIR_WIDTHS[:c]), sum(PAIR_WIDTHS[: c + 1])) for c in range(len(PAIR_WIDTHS))]
         pairs = [keep.tile([P, 2, width, 2], BF16, name=f"pairs{c}", align_bytes=64) for c, width in enumerate(PAIR_WIDTHS)]
-        turned_bf = [keep.tile([P, 2, 2, P], BF16, name=f"turned_bf{g}", align_bytes=64) for g in range(4)]
-
-        def turn(a, per_bank, first_bank):
-            banks = [bank(first_bank + g, [P, per_bank, P]) for g in range(U // P // per_bank)]
-            for source in (emb_t[a], up_first, up[a]) if a == 0 else (emb_t[a], up[a]):
-                for b in range(U // P):
-                    first = source is emb_t[a] and b % per_bank == 0
-                    last = source is up[a] and b % per_bank == per_bank - 1
-                    nc.tensor.matmul(banks[b // per_bank][:, b % per_bank, :], source[:, b * P : (b + 1) * P], ident[:], start=first, stop=last, is_transpose=True)
-            for g in range(4):
-                at = 2 * g % per_bank
-                nc.scalar.copy(turned_bf[g][:, :, a, :], banks[2 * g // per_bank][:, at : at + 2, :])
-
-        for t, a, b, h in pieces:
-            nc.vector.tensor_copy((up_first if b == P else up[t])[:].indirect(cell_t[:, a // LIST_ROWS : b // LIST_ROWS]), h[:])
-            if b < S:
-                continue
-            if t == 0:
-                turn(0, 4, 3)
-            if t == 1:
-                w2_bf = keep.tile([P, N, PACK], BF16, name="h1", align_bytes=64)
-                nc.scalar.copy(w2_bf[:], w2_raw[:].rearrange("p j n -> p n j"))
-                turn(1, 4, 5)
-                for c, cols in enumerate(pair_cols):
-                    back = bank((7 + c) % 8, [P, PAIR_WIDTHS[c]])
-                    for b in range(cols.start // P, cols.stop // P):
-                        words = turned_bf[b // 2][:].rearrange("r b a m -> r (b a m)").bitcast(F32)
-                        at = b * P - cols.start
-                        nc.tensor.transpose(back[:, at : at + P], words[:, (b % 2) * P : (b % 2 + 1) * P], ident[:])
-                    nc.scalar.copy(pairs[c][:].rearrange("p u r e -> p (u r e)").bitcast(F32)[:, : PAIR_WIDTHS[c]], back[:])
-        w2_code = keep.tile([P, N], U32, name="h2", align_bytes=64)
-        nc.vector.quantize_mx(out=w2_code[:].bitcast(FP8X4), scales=w2_scale[:], in_=w2_bf[:].rearrange("p n j -> p (n j)"))
-        for c, cols in enumerate(pair_cols):
-            nc.vector.tensor_tensor(
-                pairs[c][:, 1].rearrange("p (g i) e -> p g e i", i=LINE),
-                up[2][:].rearrange("p (e r) -> p e r", e=2)[:, :, cols].rearrange("p e (g i) -> p g e i", i=LINE),
-                up[3][:].rearrange("p (e r) -> p e r", e=2)[:, ::-1, cols].rearrange("p e (g i) -> p g e i", i=LINE),
-                ADD,
-            )
+        for u in range(2):
+            for c, cols in enumerate(pair_cols):
+                nc.vector.tensor_tensor(
+                    pairs[c][:, u].rearrange("p (g i) e -> p g e i", i=LINE),
+                    up[2 * u][:].rearrange("p (e r) -> p e r", e=2)[:, :, cols].rearrange("p e (g i) -> p g e i", i=LINE),
+                    up[2 * u + 1][:].rearrange("p (e r) -> p e r", e=2)[:, ::-1, cols].rearrange("p e (g i) -> p g e i", i=LINE),
+                    ADD,
+                )
 
         cols = [slice(sum(WIDTHS[:c]), sum(WIDTHS[: c + 1])) for c in range(len(WIDTHS))]
-        z_all = keep.tile([P, U * PACK], BF16, name="turned_bf3", align_bytes=64)
-        z_bf = [z_all[:, span.start * PACK : span.stop * PACK] for span in cols]
+        z_bf = [keep.tile([P, width * PACK], BF16, name=f"z_bf{c}", align_bytes=64) for c, width in enumerate(WIDTHS)]
         for c, span in enumerate(cols):
             home = max(k for k, whole in enumerate(pair_cols) if whole.start <= span.start)
             at = span.start - pair_cols[home].start
             nc.scalar.copy(
-                z_bf[c].bitcast(F32).rearrange("p (r u) -> p r u", u=2),
+                z_bf[c][:].bitcast(F32).rearrange("p (r u) -> p r u", u=2),
                 pairs[home][:].rearrange("p u r e -> p (u r e)").bitcast(F32).rearrange("p (u r) -> p r u", u=2)[:, at : at + WIDTHS[c]],
             )
         y = keep.tile([P, U], F32, name="y", align_bytes=64)
         for c, span in enumerate(cols):
             z_code = keep.tile([P, WIDTHS[c]], U32, name=f"z_code{c}", align_bytes=64)
             z_scale = keep.tile([P, WIDTHS[c]], U8, name=f"z_scale{c}", align_bytes=64)
-            nc.vector.quantize_mx(out=z_code[:].bitcast(FP8X4), scales=z_scale[:], in_=z_bf[c])
+            nc.vector.quantize_mx(out=z_code[:].bitcast(FP8X4), scales=z_scale[:], in_=z_bf[c][:])
             acc = bank(c, [P, WIDTHS[c]])
             nc.tensor.matmul_mx(
                 out=acc[:],
@@ -203,32 +153,31 @@ def tile_picked_devox_relu_p_kernel(tc, x_words, x_scales, w1, w2, gate, emb, of
                 start=True,
                 stop=True,
             )
-            if c < len(WIDTHS) - 0:
-                nc.scalar.activation(y[:, span], acc[:], RELU)
-            else:
-                nc.vector.tensor_scalar_max(y[:, span], acc[:], 0.0)
+            nc.scalar.activation(y[:, span], acc[:], RELU)
 
-        terms = [keep.tile([P, V], F32, name=f"term{d}", align_bytes=64) for d in range(D)]
-        halves = [slice(a * V // 2, (a + 1) * V // 2) for a in range(2)]
-        sum_turned = [bank(4 + b, [P, P]) for b in range(V // P)]
-
-        def gather(d, v):
-            nc.vector.tensor_tensor(terms[d][:, v], y[:].indirect(pos_t[d][:, v.start // LIST_ROWS : v.stop // LIST_ROWS]), gate_t[:, d, v], MULT)
-            if d < D - 1:
-                for b in range(v.start // P, v.stop // P):
-                    nc.tensor.matmul(sum_turned[b][:], terms[d][:, b * P : (b + 1) * P], ident[:], start=d == 0, stop=d == D - 2, is_transpose=True)
-
-        gather(0, slice(0, V))
-        gather(1, slice(0, V))
-        for d in range(2, D):
-            for v in halves:
-                gather(d, v)
-        res = [keep.tile([P, V // 2], F32, name=f"res{a}", align_bytes=64) for a in range(2)]
-        for b in range(V // P):
-            staged = keep.tile([P, P], F32, name=f"staged{b}", align_bytes=64)
-            nc.scalar.copy(staged[:], sum_turned[b][:])
-            acc = bank(b, [P, P])
-            nc.tensor.transpose(acc[:], staged[:], ident[:])
-            nc.vector.tensor_tensor(res[b // 2][:, b % 2 * P : (b % 2 + 1) * P], terms[D - 1][:, b * P : (b + 1) * P], acc[:], ADD)
-            if b % 2 == 1:
-                (nc.sync if b == 1 else nc.scalar).dma_start(out[:, halves[b // 2]], res[b // 2][:])
+        W = V // 2
+        for a in range(2):
+            v = slice(a * W, (a + 1) * W)
+            part = slice(v.start // LIST_ROWS, v.stop // LIST_ROWS)
+            terms = [keep.tile([P, W], F32, name=f"term{d}{a}", align_bytes=64) for d in range(D)]
+            for d in range(2):
+                nc.vector.tensor_tensor(terms[d][:], y[:].indirect(pos_t[d][:, part]), gate_t[:, d, v], MULT)
+            turned = [bank(4 * a + d, [P, 2, P]) for d in range(2)]
+            for d in range(2, D):
+                nc.scalar.activation(terms[d][:], y[:].indirect(pos_t[d][:, part]), COPY)
+                for b in range(2):
+                    nc.tensor.transpose(turned[d - 2][:, b, :], terms[d][:, b * P : (b + 1) * P], ident[:])
+            scaled = keep.tile([P, 2, 2, P], F32, name=f"scaled{a}", align_bytes=64)
+            for d in range(2):
+                for b in range(2):
+                    col = 4 * d + 2 * a + b
+                    nc.scalar.activation(scaled[:, d, b, :], turned[d][:, b, :], COPY, scale=gate_cols[:, col : col + 1])
+            back = bank(4 * a + 2, [P, 2, P])
+            for d in range(2):
+                for b in range(2):
+                    nc.tensor.matmul(back[:, b, :], scaled[:, d, b, :], ident[:], start=d == 0 and b == 0, stop=d == 1 and b == 1, is_transpose=True)
+            both = keep.tile([P, W], F32, name=f"both{a}", align_bytes=64)
+            nc.vector.tensor_tensor(both[:], terms[0][:], terms[1][:], ADD)
+            res = keep.tile([P, W], F32, name=f"res{a}", align_bytes=64)
+            nc.vector.tensor_tensor(res[:], both[:], back[:].rearrange("p b m -> p (b m)"), ADD)
+            nc.sync.dma_start(out[:, v], res[:])

@@ -25,7 +25,7 @@ QUADRANT = 32
 LINE = 4
 HALF = S // 2
 W1_VECTOR = 80
-PAIR_WIDTHS = (256, 256, 256, 256)
+PAIR_WIDTH = 256
 WIDTHS = (256, 256, 256, 128, 128)
 
 
@@ -33,6 +33,7 @@ def tile_picked_devox_relu_p_kernel(tc, x_words, x_scales, w1, w2, gate, emb, of
     nc = tc.nc
     with ExitStack() as ctx:
         keep = ctx.enter_context(tc.tile_pool(name="keep", bufs=1))
+        shared = ctx.enter_context(tc.tile_pool(name="shared", bufs=1))
         psum = ctx.enter_context(tc.psum_pool(name="psum", bufs=1))
 
         def bank(index, shape):
@@ -44,7 +45,7 @@ def tile_picked_devox_relu_p_kernel(tc, x_words, x_scales, w1, w2, gate, emb, of
         table_words = keep.tile([P, T], U32, name="table_words", align_bytes=64)
         table_scales = keep.tile([P, T], U8, name="table_scales", align_bytes=64)
         w1_raw = keep.tile([P, PACK, H], F32, name="w1_raw", align_bytes=64)
-        w2_raw = keep.tile([P, PACK, N], F32, name="w2_raw", align_bytes=64)
+        w2_raw = shared.tile([P, PACK, N], F32, name="w2_raw", offset=5 * 1024, align_bytes=64)
         gate_t = keep.tile([P, 2, V], F32, name="gate_t", align_bytes=64)
         gate_rows = keep.tile([P, P], F32, name="gate_rows", align_bytes=64)
         up = [keep.tile([P, 2 * U], F32, name=f"up{t}", align_bytes=64) for t in range(PACK)]
@@ -59,7 +60,7 @@ def tile_picked_devox_relu_p_kernel(tc, x_words, x_scales, w1, w2, gate, emb, of
         nc.sync.dma_start(table_words[:].bitcast(I32), x_words[0].rearrange("p n r -> p (n r)").bitcast(I32))
         nc.sync.dma_start(cell_t[:], cell)
         emb_planes = emb.rearrange("(p t) r -> p t r", t=PACK)
-        for t in (0, 2, 1, 3):
+        for t in range(PACK):
             nc.sync.dma_start(up[t][:, U:], emb_planes[:, t ^ 1, :])
         nc.sync.dma_start(w2_raw[:], w2.rearrange("(p j) c -> p j c", j=PACK))
         for d, pos in enumerate((pos1, pos2, pos3, pos4)):
@@ -79,67 +80,76 @@ def tile_picked_devox_relu_p_kernel(tc, x_words, x_scales, w1, w2, gate, emb, of
         x_scale = keep.tile([P, S], U8, name="x_scale", align_bytes=64)
         nc.vector.tensor_copy(x_scale[:], table_scales[:].indirect(offs_t[:]))
         nc.vector.quantize_mx(out=w1_code[:].bitcast(FP8X4), scales=w1_scale[:], in_=w1_bf[:].rearrange("p t m j -> p (t m j)"))
-        x_code = [keep.tile([P, HALF], U32, name=f"x_code{a}", align_bytes=64) for a in range(2)]
-        for a in range(2):
-            nc.vector.tensor_copy(x_code[a][:], table_words[:].indirect(offs_t[:, a * HALF // LIST_ROWS : (a + 1) * HALF // LIST_ROWS]))
+        x_code = keep.tile([P, S], U32, name="x_code", align_bytes=64)
+        for a, b in ((0, P), (P, HALF), (HALF, S)):
+            nc.vector.tensor_copy(x_code[:, a:b], table_words[:].indirect(offs_t[:, a // LIST_ROWS : b // LIST_ROWS]))
 
-        def first_layer(t, a, index):
-            h = keep.tile([P, HALF], F32, name=f"h{t}{a}", align_bytes=64)
-            acc = bank(index, [P, HALF])
+        def first_layer(t, a, b, index):
+            acc = bank(index, [P, b - a])
             nc.tensor.matmul_mx(
                 out=acc[:],
                 lhsT=w1_code[:, t * P : (t + 1) * P].bitcast(FP8X4),
                 lhsT_scale=w1_scale[:, t * P : (t + 1) * P],
-                rhs=x_code[a][:].bitcast(FP8X4),
-                rhs_scale=x_scale[:, a * HALF : (a + 1) * HALF],
+                rhs=x_code[:, a:b].bitcast(FP8X4),
+                rhs_scale=x_scale[:, a:b],
                 start=True,
                 stop=True,
             )
-            nc.scalar.activation(h[:], acc[:], RELU)
-            return h
+            return acc
 
-        order = [(0, 0), (1, 0), (2, 0), (0, 1), (1, 1), (3, 0), (2, 1), (3, 1)]
-        h = {key: first_layer(*key, index) for index, key in enumerate(order)}
+        lists = [cell_t[:, : HALF // LIST_ROWS], cell_t[:, HALF // LIST_ROWS :]]
+        h0 = [keep.tile([P, HALF], F32, name=f"h0{a}", align_bytes=64) for a in range(2)]
+        h1 = [shared.tile([P, HALF], F32, name="h10", offset=1024, align_bytes=64), keep.tile([P, HALF], F32, name="h11", align_bytes=64)]
+        nc.scalar.activation(h0[0][:, :P], first_layer(0, 0, P, 0)[:], RELU)
+        nc.scalar.activation(h0[0][:, P:], first_layer(0, P, HALF, 1)[:], RELU)
+        nc.scalar.activation(h1[0][:], first_layer(1, 0, HALF, 2)[:], RELU)
+        nc.scalar.activation(h0[1][:], first_layer(0, HALF, S, 3)[:], RELU)
+        nc.scalar.activation(h1[1][:], first_layer(1, HALF, S, 4)[:], RELU)
+        acc2 = first_layer(2, 0, S, 5)
+        acc3 = first_layer(3, 0, S, 6)
+        nc.vector.tensor_copy(up[0][:].indirect(lists[0]), h0[0][:])
+        nc.scalar.activation(up[1][:].indirect(lists[0]), h1[0][:], COPY)
+        h3 = keep.tile([P, S], F32, name="h00", align_bytes=64)
+        nc.vector.tensor_scalar_max(h3[:], acc3[:], 0.0)
+        h2 = shared.tile([P, S], F32, name="h2", offset=1024, align_bytes=64)
+        nc.scalar.activation(h2[:], acc2[:], RELU)
+        nc.vector.tensor_copy(up[0][:].indirect(lists[1]), h0[1][:])
+        nc.scalar.activation(up[1][:].indirect(lists[1]), h1[1][:], COPY)
+        nc.vector.tensor_copy(up[2][:].indirect(cell_t[:]), h2[:])
         for a in range(2):
-            part = cell_t[:, a * HALF // LIST_ROWS : (a + 1) * HALF // LIST_ROWS]
-            for t in range(2):
-                nc.vector.tensor_copy(up[t][:].indirect(part), h[t, a][:])
-            for t in range(2, PACK):
-                nc.scalar.activation(up[t][:].indirect(part), h[t, a][:], COPY)
+            nc.scalar.activation(up[3][:].indirect(lists[a]), h3[:, a * HALF : (a + 1) * HALF], COPY)
 
         w2_scale = keep.tile([P, N], U8, name="w2_scale", align_bytes=64)
         w2_bf = keep.tile([P, N, PACK], BF16, name="w2_bf", align_bytes=64)
         nc.gpsimd.tensor_copy(w2_bf[:], w2_raw[:].rearrange("p j n -> p n j"))
-        w2_code = keep.tile([P, N], U32, name="h11", align_bytes=64)
-        nc.vector.quantize_mx(out=w2_code[:].bitcast(FP8X4), scales=w2_scale[:], in_=w2_bf[:].rearrange("p n j -> p (n j)"))
-
+        w2_code = keep.tile([P, N], U32, name="w2_code", align_bytes=64)
         gate_bank = bank(7, [P, P])
         nc.tensor.transpose(gate_bank[:], gate_rows[:], ident[:])
         gate_cols = keep.tile([P, 8], F32, name="gate_cols", align_bytes=64)
         nc.vector.tensor_copy(gate_cols[:], gate_bank[:, :8])
 
-        pair_cols = [slice(sum(PAIR_WIDTHS[:c]), sum(PAIR_WIDTHS[: c + 1])) for c in range(len(PAIR_WIDTHS))]
-        pairs = [keep.tile([P, 2, width, 2], BF16, name=f"pairs{c}", align_bytes=64) for c, width in enumerate(PAIR_WIDTHS)]
-        for u in range(2):
-            for c, cols in enumerate(pair_cols):
-                nc.vector.tensor_tensor(
-                    pairs[c][:, u].rearrange("p (g i) e -> p g e i", i=LINE),
-                    up[2 * u][:].rearrange("p (e r) -> p e r", e=2)[:, :, cols].rearrange("p e (g i) -> p g e i", i=LINE),
-                    up[2 * u + 1][:].rearrange("p (e r) -> p e r", e=2)[:, ::-1, cols].rearrange("p e (g i) -> p g e i", i=LINE),
-                    ADD,
-                )
-
         cols = [slice(sum(WIDTHS[:c]), sum(WIDTHS[: c + 1])) for c in range(len(WIDTHS))]
+        pairs = [shared.tile([P, 2, PAIR_WIDTH * 2], BF16, name=f"pairs{c}", offset=c * PAIR_WIDTH * PACK * 2, align_bytes=64) for c in range(U // PAIR_WIDTH)]
+        y = keep.tile([P, U], F32, name="y", align_bytes=64)
         z_bf = [keep.tile([P, width * PACK], BF16, name=f"z_bf{c}", align_bytes=64) for c, width in enumerate(WIDTHS)]
-        for c, span in enumerate(cols):
-            home = max(k for k, whole in enumerate(pair_cols) if whole.start <= span.start)
-            at = span.start - pair_cols[home].start
+
+        def add_pair(engine, u, c):
+            span = slice(c * PAIR_WIDTH, (c + 1) * PAIR_WIDTH)
+            engine.tensor_tensor(
+                pairs[c][:, u].rearrange("p (g i e) -> p g e i", i=LINE, e=2),
+                up[2 * u][:].rearrange("p (e r) -> p e r", e=2)[:, :, span].rearrange("p e (g i) -> p g e i", i=LINE),
+                up[2 * u + 1][:].rearrange("p (e r) -> p e r", e=2)[:, ::-1, span].rearrange("p e (g i) -> p g e i", i=LINE),
+                ADD,
+            )
+
+        def weave(c):
+            home, at = divmod(cols[c].start, PAIR_WIDTH)
             nc.scalar.copy(
                 z_bf[c][:].bitcast(F32).rearrange("p (r u) -> p r u", u=2),
-                pairs[home][:].rearrange("p u r e -> p (u r e)").bitcast(F32).rearrange("p (u r) -> p r u", u=2)[:, at : at + WIDTHS[c]],
+                pairs[home][:].rearrange("p u x -> p (u x)").bitcast(F32).rearrange("p (u r) -> p r u", u=2)[:, at : at + WIDTHS[c]],
             )
-        y = keep.tile([P, U], F32, name="y", align_bytes=64)
-        for c, span in enumerate(cols):
+
+        def second_layer(c):
             z_code = keep.tile([P, WIDTHS[c]], U32, name=f"z_code{c}", align_bytes=64)
             z_scale = keep.tile([P, WIDTHS[c]], U8, name=f"z_scale{c}", align_bytes=64)
             nc.vector.quantize_mx(out=z_code[:].bitcast(FP8X4), scales=z_scale[:], in_=z_bf[c][:])
@@ -153,31 +163,52 @@ def tile_picked_devox_relu_p_kernel(tc, x_words, x_scales, w1, w2, gate, emb, of
                 start=True,
                 stop=True,
             )
-            nc.scalar.activation(y[:, span], acc[:], RELU)
+            return acc
+
+        for c in range(U // PAIR_WIDTH):
+            add_pair(nc.vector if c < 2 else nc.gpsimd, 0, c)
+        nc.vector.quantize_mx(out=w2_code[:].bitcast(FP8X4), scales=w2_scale[:], in_=w2_bf[:].rearrange("p n j -> p (n j)"))
+        for c in range(U // PAIR_WIDTH):
+            add_pair(nc.vector, 1, c)
+        for c in range(len(WIDTHS)):
+            weave(c)
+        for c in range(len(WIDTHS)):
+            acc = second_layer(c)
+            nc.scalar.activation(y[:, cols[c]], acc[:], RELU)
 
         W = V // 2
+        halves = [slice(0, W), slice(W, V)]
+        terms = [[keep.tile([P, W], F32, name=f"term{d}{a}", align_bytes=64) for a in range(2)] for d in range(D)]
+        turned = [[bank(4 * a + d, [P, 2, P]) for a in range(2)] for d in range(2)]
+
+        def window(d, a):
+            return y[:].indirect(pos_t[d][:, halves[a].start // LIST_ROWS : halves[a].stop // LIST_ROWS])
+
+        def turn(d, a):
+            for b in range(2):
+                nc.tensor.transpose(turned[d - 2][a][:, b, :], terms[d][a][:, b * P : (b + 1) * P], ident[:])
+
+        nc.vector.tensor_copy(terms[3][1][:], window(3, 1))
+        for d, a in ((2, 0), (3, 0), (2, 1)):
+            nc.scalar.activation(terms[d][a][:], window(d, a), COPY)
+        for d, a in ((2, 0), (3, 1), (3, 0), (2, 1)):
+            turn(d, a)
+        both = [keep.tile([P, W], F32, name=f"both{a}", align_bytes=64) for a in range(2)]
         for a in range(2):
-            v = slice(a * W, (a + 1) * W)
-            part = slice(v.start // LIST_ROWS, v.stop // LIST_ROWS)
-            terms = [keep.tile([P, W], F32, name=f"term{d}{a}", align_bytes=64) for d in range(D)]
             for d in range(2):
-                nc.vector.tensor_tensor(terms[d][:], y[:].indirect(pos_t[d][:, part]), gate_t[:, d, v], MULT)
-            turned = [bank(4 * a + d, [P, 2, P]) for d in range(2)]
-            for d in range(2, D):
-                nc.scalar.activation(terms[d][:], y[:].indirect(pos_t[d][:, part]), COPY)
-                for b in range(2):
-                    nc.tensor.transpose(turned[d - 2][:, b, :], terms[d][:, b * P : (b + 1) * P], ident[:])
+                nc.vector.tensor_tensor(terms[d][a][:], window(d, a), gate_t[:, d, halves[a]], MULT)
+        for a in range(2):
+            nc.vector.tensor_tensor(both[a][:], terms[0][a][:], terms[1][a][:], ADD)
+        for a, v in enumerate(halves):
             scaled = keep.tile([P, 2, 2, P], F32, name=f"scaled{a}", align_bytes=64)
             for d in range(2):
                 for b in range(2):
                     col = 4 * d + 2 * a + b
-                    nc.scalar.activation(scaled[:, d, b, :], turned[d][:, b, :], COPY, scale=gate_cols[:, col : col + 1])
+                    nc.scalar.activation(scaled[:, d, b, :], turned[d][a][:, b, :], COPY, scale=gate_cols[:, col : col + 1])
             back = bank(4 * a + 2, [P, 2, P])
             for d in range(2):
                 for b in range(2):
                     nc.tensor.matmul(back[:, b, :], scaled[:, d, b, :], ident[:], start=d == 0 and b == 0, stop=d == 1 and b == 1, is_transpose=True)
-            both = keep.tile([P, W], F32, name=f"both{a}", align_bytes=64)
-            nc.vector.tensor_tensor(both[:], terms[0][:], terms[1][:], ADD)
             res = keep.tile([P, W], F32, name=f"res{a}", align_bytes=64)
-            nc.vector.tensor_tensor(res[:], both[:], back[:].rearrange("p b m -> p (b m)"), ADD)
+            nc.vector.tensor_tensor(res[:], both[a][:], back[:].rearrange("p b m -> p (b m)"), ADD)
             nc.sync.dma_start(out[:, v], res[:])

@@ -24,7 +24,7 @@ LIST_ROWS = 16
 QUADRANT = 32
 LINE = 4
 HALF = S // 2
-W1_VECTOR = 80
+W1_VECTOR = 40
 PAIR_WIDTH = 256
 WIDTHS = (256, 256, 256, 128, 128)
 
@@ -53,8 +53,8 @@ def tile_picked_devox_relu_p_kernel(tc, x_words, x_scales, w1, w2, gate, emb, of
 
         nc.gpsimd.memset(table_scales[:].bitcast(I32), 0)
         nc.gpsimd.memset(gate_rows[:], 0.0)
-        nc.sync.dma_start(offs_t[:], offs)
         nc.sync.dma_start(w1_raw[:], w1.rearrange("(p j) c -> p j c", j=PACK))
+        nc.sync.dma_start(offs_t[:], offs)
         for q in range(P // QUADRANT):
             nc.sync.dma_start(table_scales[QUADRANT * q : QUADRANT * q + 4, :].bitcast(I32), x_scales[0, 4 * q : 4 * q + 4, :].bitcast(I32))
         nc.sync.dma_start(table_words[:].bitcast(I32), x_words[0].rearrange("p n r -> p (n r)").bitcast(I32))
@@ -178,7 +178,7 @@ def tile_picked_devox_relu_p_kernel(tc, x_words, x_scales, w1, w2, gate, emb, of
 
         W = V // 2
         halves = [slice(0, W), slice(W, V)]
-        terms = [[keep.tile([P, W], F32, name=f"term{d}{a}", align_bytes=64) for a in range(2)] for d in range(D)]
+        terms = {d: [keep.tile([P, W], F32, name=f"term{d}{a}", align_bytes=64) for a in range(2)] for d in range(2, D)}
         turned = [[bank(4 * a + d, [P, 2, P]) for a in range(2)] for d in range(2)]
 
         def window(d, a):
@@ -189,26 +189,27 @@ def tile_picked_devox_relu_p_kernel(tc, x_words, x_scales, w1, w2, gate, emb, of
                 nc.tensor.transpose(turned[d - 2][a][:, b, :], terms[d][a][:, b * P : (b + 1) * P], ident[:])
 
         nc.vector.tensor_copy(terms[3][1][:], window(3, 1))
-        for d, a in ((2, 0), (3, 0), (2, 1)):
+        for b in range(2):
+            nc.scalar.activation(terms[2][0][:, b * P : (b + 1) * P], y[:].indirect(pos_t[2][:, b * P // LIST_ROWS : (b + 1) * P // LIST_ROWS]), COPY)
+        for d, a in ((3, 0), (2, 1)):
             nc.scalar.activation(terms[d][a][:], window(d, a), COPY)
         for d, a in ((2, 0), (3, 1), (3, 0), (2, 1)):
             turn(d, a)
-        both = [keep.tile([P, W], F32, name=f"both{a}", align_bytes=64) for a in range(2)]
-        for a in range(2):
-            for d in range(2):
-                nc.vector.tensor_tensor(terms[d][a][:], window(d, a), gate_t[:, d, halves[a]], MULT)
-        for a in range(2):
-            nc.vector.tensor_tensor(both[a][:], terms[0][a][:], terms[1][a][:], ADD)
+        fused = [keep.tile([P, V], F32, name=f"fused{d}", align_bytes=64) for d in range(2)]
+        nc.vector.tensor_tensor(fused[0][:], y[:].indirect(pos_t[0][:]), gate_t[:, 0, :], MULT)
+        for a, v in enumerate(halves):
+            nc.vector.tensor_tensor(fused[1][:, v], window(1, a), gate_t[:, 1, v], MULT)
+        both = keep.tile([P, V], F32, name="both", align_bytes=64)
+        for v in halves:
+            nc.vector.tensor_tensor(both[:, v], fused[0][:, v], fused[1][:, v], ADD)
         for a, v in enumerate(halves):
             scaled = keep.tile([P, 2, 2, P], F32, name=f"scaled{a}", align_bytes=64)
-            for d in range(2):
-                for b in range(2):
+            back = [bank(4 * a + 2 + b, [P, P]) for b in range(2)]
+            res = keep.tile([P, W], F32, name=f"res{a}", align_bytes=64)
+            for b in range(2):
+                for d in range(2):
                     col = 4 * d + 2 * a + b
                     nc.scalar.activation(scaled[:, d, b, :], turned[d][a][:, b, :], COPY, scale=gate_cols[:, col : col + 1])
-            back = bank(4 * a + 2, [P, 2, P])
-            for d in range(2):
-                for b in range(2):
-                    nc.tensor.matmul(back[:, b, :], scaled[:, d, b, :], ident[:], start=d == 0 and b == 0, stop=d == 1 and b == 1, is_transpose=True)
-            res = keep.tile([P, W], F32, name=f"res{a}", align_bytes=64)
-            nc.vector.tensor_tensor(res[:], both[a][:], back[:].rearrange("p b m -> p (b m)"), ADD)
+                    nc.tensor.matmul(back[b][:], scaled[:, d, b, :], ident[:], start=d == 0, stop=d == 1, is_transpose=True)
+                nc.vector.tensor_tensor(res[:, b * P : (b + 1) * P], both[:, v.start + b * P : v.start + (b + 1) * P], back[b][:], ADD)
             nc.sync.dma_start(out[:, v], res[:])

@@ -45,29 +45,29 @@ def tile_picked_devox_relu_p_kernel(tc, x_words, x_scales, w1, w2, gate, emb, of
         table_words = keep.tile([P, T], U32, name="table_words", align_bytes=64)
         table_scales = keep.tile([P, T], U8, name="table_scales", align_bytes=64)
         w1_raw = keep.tile([P, PACK, H], F32, name="w1_raw", align_bytes=64)
-        w2_raw = shared.tile([P, PACK, N], F32, name="w2_raw", offset=5 * 1024, align_bytes=64)
+        w2_raw = keep.tile([P, PACK, N], F32, name="w2_raw", align_bytes=64)
         gate_t = keep.tile([P, 2, V], F32, name="gate_t", align_bytes=64)
-        gate_rows = keep.tile([P, P], F32, name="gate_rows", align_bytes=64)
+        gate_cols = [keep.tile([P, V // P], F32, name=f"gate_cols{d}", align_bytes=64) for d in range(2)]
         up = [keep.tile([P, 2 * U], F32, name=f"up{t}", align_bytes=64) for t in range(PACK)]
         ident = keep.tile([P, P], F32, name="ident", align_bytes=64)
 
         nc.gpsimd.memset(table_scales[:].bitcast(I32), 0)
-        nc.gpsimd.memset(gate_rows[:], 0.0)
         nc.sync.dma_start(w1_raw[:], w1.rearrange("(p j) c -> p j c", j=PACK))
         nc.sync.dma_start(offs_t[:], offs)
         for q in range(P // QUADRANT):
             nc.sync.dma_start(table_scales[QUADRANT * q : QUADRANT * q + 4, :].bitcast(I32), x_scales[0, 4 * q : 4 * q + 4, :].bitcast(I32))
         nc.sync.dma_start(table_words[:].bitcast(I32), x_words[0].rearrange("p n r -> p (n r)").bitcast(I32))
+        nc.sync.dma_start(w2_raw[:], w2.rearrange("(p j) c -> p j c", j=PACK))
         nc.sync.dma_start(cell_t[:], cell)
         emb_planes = emb.rearrange("(p t) r -> p t r", t=PACK)
         for t in range(PACK):
             nc.sync.dma_start(up[t][:, U:], emb_planes[:, t ^ 1, :])
-        nc.sync.dma_start(w2_raw[:], w2.rearrange("(p j) c -> p j c", j=PACK))
         for d, pos in enumerate((pos1, pos2, pos3, pos4)):
             nc.sync.dma_start(pos_t[d][:], pos)
         nc.sync.dma_start(gate_t[:], gate[:2].rearrange("d p v -> p d v"))
         for d in range(2, D):
-            nc.sync.dma_start(gate_rows[4 * (d - 2) : 4 * (d - 1), :], gate[d, 0].rearrange("(b c) -> b c", c=P))
+            with nc.allow_non_contiguous_dma(reason="one gate value a partition"):
+                nc.sync.dma_start(gate_cols[d - 2][:], gate[d, 0].rearrange("(b p) -> p b", p=P))
         for t in range(PACK):
             nc.vector.memset(up[t][:, :U], 0.0)
         make_identity(nc, ident[:])
@@ -123,11 +123,6 @@ def tile_picked_devox_relu_p_kernel(tc, x_words, x_scales, w1, w2, gate, emb, of
         w2_bf = keep.tile([P, N, PACK], BF16, name="w2_bf", align_bytes=64)
         nc.gpsimd.tensor_copy(w2_bf[:], w2_raw[:].rearrange("p j n -> p n j"))
         w2_code = keep.tile([P, N], U32, name="w2_code", align_bytes=64)
-        gate_bank = bank(7, [P, P])
-        nc.tensor.transpose(gate_bank[:], gate_rows[:], ident[:])
-        gate_cols = keep.tile([P, 8], F32, name="gate_cols", align_bytes=64)
-        nc.vector.tensor_copy(gate_cols[:], gate_bank[:, :8])
-
         cols = [slice(sum(WIDTHS[:c]), sum(WIDTHS[: c + 1])) for c in range(len(WIDTHS))]
         pairs = [shared.tile([P, 2, PAIR_WIDTH * 2], BF16, name=f"pairs{c}", offset=c * PAIR_WIDTH * PACK * 2, align_bytes=64) for c in range(U // PAIR_WIDTH)]
         y = keep.tile([P, U], F32, name="y", align_bytes=64)
@@ -172,9 +167,12 @@ def tile_picked_devox_relu_p_kernel(tc, x_words, x_scales, w1, w2, gate, emb, of
             add_pair(nc.vector, 1, c)
         for c in range(len(WIDTHS)):
             weave(c)
+        accs = []
         for c in range(len(WIDTHS)):
-            acc = second_layer(c)
-            nc.scalar.activation(y[:, cols[c]], acc[:], RELU)
+            accs.append(second_layer(c))
+        for c in (0, 1, 3, 4):
+            nc.scalar.activation(y[:, cols[c]], accs[c][:], RELU)
+        nc.vector.tensor_scalar_max(y[:, cols[2]], accs[2][:], 0.0)
 
         W = V // 2
         halves = [slice(0, W), slice(W, V)]
@@ -202,14 +200,14 @@ def tile_picked_devox_relu_p_kernel(tc, x_words, x_scales, w1, w2, gate, emb, of
         both = keep.tile([P, V], F32, name="both", align_bytes=64)
         for v in halves:
             nc.vector.tensor_tensor(both[:, v], fused[0][:, v], fused[1][:, v], ADD)
-        for a, v in enumerate(halves):
-            scaled = keep.tile([P, 2, 2, P], F32, name=f"scaled{a}", align_bytes=64)
-            back = [bank(4 * a + 2 + b, [P, P]) for b in range(2)]
-            res = keep.tile([P, W], F32, name=f"res{a}", align_bytes=64)
-            for b in range(2):
+        res = keep.tile([P, V], F32, name="res", align_bytes=64)
+        scaled = [keep.tile([P, 2, P], F32, name=f"scaled{b}", align_bytes=64) for b in range(V // P)]
+        for index, (first, last) in zip((2, 6, 7), ((0, 2), (2, 3), (3, 4))):
+            back = bank(index, [P, last - first, P])
+            for b in range(first, last):
                 for d in range(2):
-                    col = 4 * d + 2 * a + b
-                    nc.scalar.activation(scaled[:, d, b, :], turned[d][a][:, b, :], COPY, scale=gate_cols[:, col : col + 1])
-                    nc.tensor.matmul(back[b][:], scaled[:, d, b, :], ident[:], start=d == 0, stop=d == 1, is_transpose=True)
-                nc.vector.tensor_tensor(res[:, b * P : (b + 1) * P], both[:, v.start + b * P : v.start + (b + 1) * P], back[b][:], ADD)
-            nc.sync.dma_start(out[:, v], res[:])
+                    nc.scalar.activation(scaled[b][:, d, :], turned[d][b // 2][:, b % 2, :], COPY, scale=gate_cols[d][:, b : b + 1])
+                    nc.tensor.matmul(back[:, b - first, :], scaled[b][:, d, :], ident[:], start=d == 0 and b == first, stop=d == 1 and b == last - 1, is_transpose=True)
+            v = slice(first * P, last * P)
+            nc.vector.tensor_tensor(res[:, v], both[:, v], back[:].rearrange("p b m -> p (b m)"), ADD)
+            nc.sync.dma_start(out[:, v], res[:, v])

@@ -52,15 +52,18 @@ def tile_picked_devox_relu_p_kernel(tc, x_words, x_scales, w1, w2, gate, emb, of
         ident = keep.tile([P, P], F32, name="ident", align_bytes=64)
 
         nc.gpsimd.memset(table_scales[:].bitcast(I32), 0)
+        zero = keep.tile([P, LINE], F32, name="zero", align_bytes=64)
+        nc.gpsimd.memset(zero[:], 0.0)
         nc.sync.dma_start(w1_raw[:], w1.rearrange("(p j) c -> p j c", j=PACK))
         nc.sync.dma_start(offs_t[:], offs)
         for q in range(P // QUADRANT):
             nc.sync.dma_start(table_scales[QUADRANT * q : QUADRANT * q + 4, :].bitcast(I32), x_scales[0, 4 * q : 4 * q + 4, :].bitcast(I32))
         nc.sync.dma_start(table_words[:].bitcast(I32), x_words[0].rearrange("p n r -> p (n r)").bitcast(I32))
-        nc.sync.dma_start(w2_raw[:], w2.rearrange("(p j) c -> p j c", j=PACK))
         nc.sync.dma_start(cell_t[:], cell)
         emb_planes = emb.rearrange("(p t) r -> p t r", t=PACK)
         for t in range(PACK):
+            if t == 2:
+                nc.sync.dma_start(w2_raw[:], w2.rearrange("(p j) c -> p j c", j=PACK))
             nc.sync.dma_start(up[t][:, U:], emb_planes[:, t ^ 1, :])
         for d, pos in enumerate((pos1, pos2, pos3, pos4)):
             nc.sync.dma_start(pos_t[d][:], pos)
@@ -69,7 +72,7 @@ def tile_picked_devox_relu_p_kernel(tc, x_words, x_scales, w1, w2, gate, emb, of
             with nc.allow_non_contiguous_dma(reason="one gate value a partition"):
                 nc.sync.dma_start(gate_cols[d - 2][:], gate[d, 0].rearrange("(b p) -> p b", p=P))
         for t in range(PACK):
-            nc.vector.memset(up[t][:, :U], 0.0)
+            nc.vector.tensor_copy(up[t][:, :U].rearrange("p (g i) -> p g i", i=LINE), zero[:].unsqueeze(1).to_broadcast([P, U // LINE, LINE]))
         make_identity(nc, ident[:])
 
         w1_bf = keep.tile([P, PACK, P, PACK], BF16, name="w1_bf", align_bytes=64)

@@ -24,20 +24,27 @@ LIST_ROWS = 16
 QUADRANT = 32
 LINE = 4
 HALF = S // 2
+FUSED = 2
 W1_VECTOR = 40
-PAIR_WIDTH = 256
+PAIR_CELLS = U // 2
+ADD_CELLS = 256
 WIDTHS = (256, 256, 256, 128, 128)
+VECTOR_RELU = 2
+STORES = ((0, 2), (2, 3), (3, 4))
 
 
 def tile_picked_devox_relu_p_kernel(tc, x_words, x_scales, w1, w2, gate, emb, offs, cell, pos1, pos2, pos3, pos4, out):
     nc = tc.nc
     with ExitStack() as ctx:
         keep = ctx.enter_context(tc.tile_pool(name="keep", bufs=1))
-        shared = ctx.enter_context(tc.tile_pool(name="shared", bufs=1))
+        reused = ctx.enter_context(tc.tile_pool(name="reused", bufs=1))
         psum = ctx.enter_context(tc.psum_pool(name="psum", bufs=1))
 
         def bank(index, shape):
             return psum.tile(shape, F32, name=f"bank{index}")
+
+        def entries(list_tile, first, last):
+            return list_tile[:, first // LIST_ROWS : last // LIST_ROWS]
 
         offs_t = keep.tile([P, S // LIST_ROWS], U16, name="offs_t")
         cell_t = keep.tile([P, S // LIST_ROWS], U16, name="cell_t")
@@ -46,14 +53,15 @@ def tile_picked_devox_relu_p_kernel(tc, x_words, x_scales, w1, w2, gate, emb, of
         table_scales = keep.tile([P, T], U8, name="table_scales", align_bytes=64)
         w1_raw = keep.tile([P, PACK, H], F32, name="w1_raw", align_bytes=64)
         w2_raw = keep.tile([P, PACK, N], F32, name="w2_raw", align_bytes=64)
-        gate_t = keep.tile([P, 2, V], F32, name="gate_t", align_bytes=64)
-        gate_cols = [keep.tile([P, V // P], F32, name=f"gate_cols{d}", align_bytes=64) for d in range(2)]
+        gate_rows = keep.tile([P, FUSED, V], F32, name="gate_rows", align_bytes=64)
+        gate_cols = [keep.tile([P, V // P], F32, name=f"gate_cols{d}", align_bytes=64) for d in range(D - FUSED)]
         up = [keep.tile([P, 2 * U], F32, name=f"up{t}", align_bytes=64) for t in range(PACK)]
         ident = keep.tile([P, P], F32, name="ident", align_bytes=64)
 
         nc.gpsimd.memset(table_scales[:].bitcast(I32), 0)
         zero = keep.tile([P, LINE], F32, name="zero", align_bytes=64)
         nc.gpsimd.memset(zero[:], 0.0)
+
         nc.sync.dma_start(w1_raw[:], w1.rearrange("(p j) c -> p j c", j=PACK))
         nc.sync.dma_start(offs_t[:], offs)
         for q in range(P // QUADRANT):
@@ -61,16 +69,17 @@ def tile_picked_devox_relu_p_kernel(tc, x_words, x_scales, w1, w2, gate, emb, of
         nc.sync.dma_start(table_words[:].bitcast(I32), x_words[0].rearrange("p n r -> p (n r)").bitcast(I32))
         nc.sync.dma_start(cell_t[:], cell)
         emb_planes = emb.rearrange("(p t) r -> p t r", t=PACK)
-        for t in range(PACK):
-            if t == 2:
-                nc.sync.dma_start(w2_raw[:], w2.rearrange("(p j) c -> p j c", j=PACK))
-            nc.sync.dma_start(up[t][:, U:], emb_planes[:, t ^ 1, :])
+        for t in range(2):
+            nc.sync.dma_start(up[t][:, U:], emb_planes[:, 1 - t, :])
+        nc.sync.dma_start(w2_raw[:], w2.rearrange("(p j) c -> p j c", j=PACK))
+        for t in range(2):
+            nc.sync.dma_start(up[2 + t][:, U:], emb_planes[:, 3 - t, :])
         for d, pos in enumerate((pos1, pos2, pos3, pos4)):
             nc.sync.dma_start(pos_t[d][:], pos)
-        nc.sync.dma_start(gate_t[:], gate[:2].rearrange("d p v -> p d v"))
-        for d in range(2, D):
+        nc.sync.dma_start(gate_rows[:], gate[:FUSED].rearrange("d p v -> p d v"))
+        for d in range(FUSED, D):
             with nc.allow_non_contiguous_dma(reason="one gate value a partition"):
-                nc.sync.dma_start(gate_cols[d - 2][:], gate[d, 0].rearrange("(b p) -> p b", p=P))
+                nc.sync.dma_start(gate_cols[d - FUSED][:], gate[d, 0].rearrange("(b p) -> p b", p=P))
         for t in range(PACK):
             nc.vector.tensor_copy(up[t][:, :U].rearrange("p (g i) -> p g i", i=LINE), zero[:].unsqueeze(1).to_broadcast([P, U // LINE, LINE]))
         make_identity(nc, ident[:])
@@ -78,73 +87,81 @@ def tile_picked_devox_relu_p_kernel(tc, x_words, x_scales, w1, w2, gate, emb, of
         w1_bf = keep.tile([P, PACK, P, PACK], BF16, name="w1_bf", align_bytes=64)
         w1_code = keep.tile([P, H], U32, name="w1_code", align_bytes=64)
         w1_scale = keep.tile([P, H], U8, name="w1_scale", align_bytes=64)
-        for copy, cols in ((nc.vector.tensor_copy, slice(0, W1_VECTOR)), (nc.scalar.copy, slice(W1_VECTOR, P))):
-            copy(w1_bf[:, :, cols, :].rearrange("p t m j -> p m t j"), w1_raw[:].rearrange("p j (m t) -> p m t j", t=PACK)[:, cols])
+        for copy, share in ((nc.vector.tensor_copy, slice(0, W1_VECTOR)), (nc.scalar.copy, slice(W1_VECTOR, P))):
+            copy(w1_bf[:, :, share, :].rearrange("p t m j -> p m t j"), w1_raw[:].rearrange("p j (m t) -> p m t j", t=PACK)[:, share])
         x_scale = keep.tile([P, S], U8, name="x_scale", align_bytes=64)
         nc.vector.tensor_copy(x_scale[:], table_scales[:].indirect(offs_t[:]))
         nc.vector.quantize_mx(out=w1_code[:].bitcast(FP8X4), scales=w1_scale[:], in_=w1_bf[:].rearrange("p t m j -> p (t m j)"))
         x_code = keep.tile([P, S], U32, name="x_code", align_bytes=64)
-        for a, b in ((0, P), (P, HALF), (HALF, S)):
-            nc.vector.tensor_copy(x_code[:, a:b], table_words[:].indirect(offs_t[:, a // LIST_ROWS : b // LIST_ROWS]))
+        for first, last in ((0, P), (P, HALF), (HALF, S)):
+            nc.vector.tensor_copy(x_code[:, first:last], table_words[:].indirect(entries(offs_t, first, last)))
 
-        def first_layer(t, a, b, index):
-            acc = bank(index, [P, b - a])
+        def first_layer(t, first, last, index):
+            acc = bank(index, [P, last - first])
             nc.tensor.matmul_mx(
                 out=acc[:],
                 lhsT=w1_code[:, t * P : (t + 1) * P].bitcast(FP8X4),
                 lhsT_scale=w1_scale[:, t * P : (t + 1) * P],
-                rhs=x_code[:, a:b].bitcast(FP8X4),
-                rhs_scale=x_scale[:, a:b],
+                rhs=x_code[:, first:last].bitcast(FP8X4),
+                rhs_scale=x_scale[:, first:last],
                 start=True,
                 stop=True,
             )
             return acc
 
-        lists = [cell_t[:, : HALF // LIST_ROWS], cell_t[:, HALF // LIST_ROWS :]]
-        h0 = [keep.tile([P, HALF], F32, name=f"h0{a}", align_bytes=64) for a in range(2)]
-        h1 = [shared.tile([P, HALF], F32, name="h10", offset=1024, align_bytes=64), keep.tile([P, HALF], F32, name="h11", align_bytes=64)]
+        half_bytes = HALF * 4
+        pair_bytes = PAIR_CELLS * PACK * 2
+        cell_halves = [entries(cell_t, 0, HALF), entries(cell_t, HALF, S)]
+        h0 = [reused.tile([P, HALF], F32, name="h0_first", offset=pair_bytes, align_bytes=64), keep.tile([P, HALF], F32, name="h0_second", align_bytes=64)]
+        h1 = [keep.tile([P, HALF], F32, name="h1_first", align_bytes=64), keep.tile([P, HALF], F32, name="h1_second", align_bytes=64)]
         nc.scalar.activation(h0[0][:, :P], first_layer(0, 0, P, 0)[:], RELU)
         nc.scalar.activation(h0[0][:, P:], first_layer(0, P, HALF, 1)[:], RELU)
         nc.scalar.activation(h1[0][:], first_layer(1, 0, HALF, 2)[:], RELU)
         nc.scalar.activation(h0[1][:], first_layer(0, HALF, S, 3)[:], RELU)
         nc.scalar.activation(h1[1][:], first_layer(1, HALF, S, 4)[:], RELU)
         acc2 = first_layer(2, 0, S, 5)
-        acc3 = first_layer(3, 0, S, 6)
-        nc.vector.tensor_copy(up[0][:].indirect(lists[0]), h0[0][:])
-        nc.scalar.activation(up[1][:].indirect(lists[0]), h1[0][:], COPY)
-        h3 = keep.tile([P, S], F32, name="h00", align_bytes=64)
-        nc.vector.tensor_scalar_max(h3[:], acc3[:], 0.0)
-        h2 = shared.tile([P, S], F32, name="h2", offset=1024, align_bytes=64)
+        acc3 = [first_layer(3, 0, HALF, 6), first_layer(3, HALF, S, 7)]
+        nc.vector.tensor_copy(up[0][:].indirect(cell_halves[0]), h0[0][:])
+        nc.scalar.activation(up[1][:].indirect(cell_halves[0]), h1[0][:], COPY)
+        h3 = [reused.tile([P, HALF], F32, name=f"h3_{a}", offset=pair_bytes - half_bytes // 2 + a * half_bytes, align_bytes=64) for a in range(2)]
+        for a in range(2):
+            nc.vector.tensor_scalar_max(h3[a][:], acc3[a][:], 0.0)
+        h2 = keep.tile([P, S], F32, name="h1_first", align_bytes=64)
         nc.scalar.activation(h2[:], acc2[:], RELU)
-        nc.vector.tensor_copy(up[0][:].indirect(lists[1]), h0[1][:])
-        nc.scalar.activation(up[1][:].indirect(lists[1]), h1[1][:], COPY)
+        nc.vector.tensor_copy(up[0][:].indirect(cell_halves[1]), h0[1][:])
+        nc.scalar.activation(up[1][:].indirect(cell_halves[1]), h1[1][:], COPY)
         nc.vector.tensor_copy(up[2][:].indirect(cell_t[:]), h2[:])
         for a in range(2):
-            nc.scalar.activation(up[3][:].indirect(lists[a]), h3[:, a * HALF : (a + 1) * HALF], COPY)
+            nc.scalar.activation(up[3][:].indirect(cell_halves[a]), h3[a][:], COPY)
 
         w2_scale = keep.tile([P, N], U8, name="w2_scale", align_bytes=64)
         w2_bf = keep.tile([P, N, PACK], BF16, name="w2_bf", align_bytes=64)
         nc.gpsimd.tensor_copy(w2_bf[:], w2_raw[:].rearrange("p j n -> p n j"))
         w2_code = keep.tile([P, N], U32, name="w2_code", align_bytes=64)
-        cols = [slice(sum(WIDTHS[:c]), sum(WIDTHS[: c + 1])) for c in range(len(WIDTHS))]
-        pairs = [shared.tile([P, 2, PAIR_WIDTH * 2], BF16, name=f"pairs{c}", offset=c * PAIR_WIDTH * PACK * 2, align_bytes=64) for c in range(U // PAIR_WIDTH)]
+
+        chunks = [slice(sum(WIDTHS[:c]), sum(WIDTHS[: c + 1])) for c in range(len(WIDTHS))]
+        pairs = [
+            reused.tile([P, PAIR_CELLS * PACK], BF16, name="pairs_vector", offset=0, align_bytes=64),
+            keep.tile([P, PAIR_CELLS * PACK], BF16, name="pairs_gpsimd", align_bytes=64),
+        ]
         y = keep.tile([P, U], F32, name="y", align_bytes=64)
         z_bf = [keep.tile([P, width * PACK], BF16, name=f"z_bf{c}", align_bytes=64) for c, width in enumerate(WIDTHS)]
 
-        def add_pair(engine, u, c):
-            span = slice(c * PAIR_WIDTH, (c + 1) * PAIR_WIDTH)
+        def add_pairs(engine, u, first, last):
+            k, at = divmod(first, PAIR_CELLS)
+            start = 2 * (u * PAIR_CELLS + at)
             engine.tensor_tensor(
-                pairs[c][:, u].rearrange("p (g i e) -> p g e i", i=LINE, e=2),
-                up[2 * u][:].rearrange("p (e r) -> p e r", e=2)[:, :, span].rearrange("p e (g i) -> p g e i", i=LINE),
-                up[2 * u + 1][:].rearrange("p (e r) -> p e r", e=2)[:, ::-1, span].rearrange("p e (g i) -> p g e i", i=LINE),
+                pairs[k][:, start : start + 2 * (last - first)].rearrange("p (g i e) -> p g e i", i=LINE, e=2),
+                up[2 * u][:].rearrange("p (e r) -> p e r", e=2)[:, :, first:last].rearrange("p e (g i) -> p g e i", i=LINE),
+                up[2 * u + 1][:].rearrange("p (e r) -> p e r", e=2)[:, ::-1, first:last].rearrange("p e (g i) -> p g e i", i=LINE),
                 ADD,
             )
 
         def weave(c):
-            home, at = divmod(cols[c].start, PAIR_WIDTH)
+            k, at = divmod(chunks[c].start, PAIR_CELLS)
             nc.scalar.copy(
                 z_bf[c][:].bitcast(F32).rearrange("p (r u) -> p r u", u=2),
-                pairs[home][:].rearrange("p u x -> p (u x)").bitcast(F32).rearrange("p (u r) -> p r u", u=2)[:, at : at + WIDTHS[c]],
+                pairs[k][:].bitcast(F32).rearrange("p (u r) -> p r u", u=2)[:, at : at + WIDTHS[c]],
             )
 
         def second_layer(c):
@@ -163,54 +180,53 @@ def tile_picked_devox_relu_p_kernel(tc, x_words, x_scales, w1, w2, gate, emb, of
             )
             return acc
 
-        for c in range(U // PAIR_WIDTH):
-            add_pair(nc.vector if c < 2 else nc.gpsimd, 0, c)
+        add_pairs(nc.vector, 0, 0, PAIR_CELLS)
+        add_pairs(nc.gpsimd, 0, PAIR_CELLS, U)
         nc.vector.quantize_mx(out=w2_code[:].bitcast(FP8X4), scales=w2_scale[:], in_=w2_bf[:].rearrange("p n j -> p (n j)"))
-        for c in range(U // PAIR_WIDTH):
-            add_pair(nc.vector, 1, c)
+        for first in range(0, U, ADD_CELLS):
+            add_pairs(nc.vector, 1, first, first + ADD_CELLS)
         for c in range(len(WIDTHS)):
             weave(c)
-        accs = []
+        accs = [second_layer(c) for c in range(len(WIDTHS))]
         for c in range(len(WIDTHS)):
-            accs.append(second_layer(c))
-        for c in (0, 1, 3, 4):
-            nc.scalar.activation(y[:, cols[c]], accs[c][:], RELU)
-        nc.vector.tensor_scalar_max(y[:, cols[2]], accs[2][:], 0.0)
+            if c != VECTOR_RELU:
+                nc.scalar.activation(y[:, chunks[c]], accs[c][:], RELU)
+        nc.vector.tensor_scalar_max(y[:, chunks[VECTOR_RELU]], accs[VECTOR_RELU][:], 0.0)
 
-        W = V // 2
-        halves = [slice(0, W), slice(W, V)]
-        terms = {d: [keep.tile([P, W], F32, name=f"term{d}{a}", align_bytes=64) for a in range(2)] for d in range(2, D)}
-        turned = [[bank(4 * a + d, [P, 2, P]) for a in range(2)] for d in range(2)]
+        half_v = V // 2
+        halves = [slice(0, half_v), slice(half_v, V)]
+        plain = [[keep.tile([P, half_v], F32, name=f"plain{d}{a}", align_bytes=64) for a in range(2)] for d in range(D - FUSED)]
+        turned = [[bank(4 * a + d, [P, 2, P]) for a in range(2)] for d in range(D - FUSED)]
 
-        def window(d, a):
-            return y[:].indirect(pos_t[d][:, halves[a].start // LIST_ROWS : halves[a].stop // LIST_ROWS])
+        def cells_of(d, first, last):
+            return y[:].indirect(entries(pos_t[d], first, last))
 
-        def turn(d, a):
-            for b in range(2):
-                nc.tensor.transpose(turned[d - 2][a][:, b, :], terms[d][a][:, b * P : (b + 1) * P], ident[:])
-
-        nc.vector.tensor_copy(terms[3][1][:], window(3, 1))
+        nc.vector.tensor_copy(plain[1][1][:], cells_of(3, half_v, V))
         for b in range(2):
-            nc.scalar.activation(terms[2][0][:, b * P : (b + 1) * P], y[:].indirect(pos_t[2][:, b * P // LIST_ROWS : (b + 1) * P // LIST_ROWS]), COPY)
-        for d, a in ((3, 0), (2, 1)):
-            nc.scalar.activation(terms[d][a][:], window(d, a), COPY)
-        for d, a in ((2, 0), (3, 1), (3, 0), (2, 1)):
-            turn(d, a)
-        fused = [keep.tile([P, V], F32, name=f"fused{d}", align_bytes=64) for d in range(2)]
-        nc.vector.tensor_tensor(fused[0][:], y[:].indirect(pos_t[0][:]), gate_t[:, 0, :], MULT)
-        for a, v in enumerate(halves):
-            nc.vector.tensor_tensor(fused[1][:, v], window(1, a), gate_t[:, 1, v], MULT)
+            nc.scalar.activation(plain[0][0][:, b * P : (b + 1) * P], cells_of(2, b * P, (b + 1) * P), COPY)
+        nc.scalar.activation(plain[1][0][:], cells_of(3, 0, half_v), COPY)
+        nc.scalar.activation(plain[0][1][:], cells_of(2, half_v, V), COPY)
+        for d, a in ((0, 0), (1, 1), (1, 0), (0, 1)):
+            for b in range(2):
+                nc.tensor.transpose(turned[d][a][:, b, :], plain[d][a][:, b * P : (b + 1) * P], ident[:])
+
+        fused = [keep.tile([P, V], F32, name=f"fused{d}", align_bytes=64) for d in range(FUSED)]
+        nc.vector.tensor_tensor(fused[0][:], y[:].indirect(pos_t[0][:]), gate_rows[:, 0, :], MULT)
+        for v in halves:
+            nc.vector.tensor_tensor(fused[1][:, v], cells_of(1, v.start, v.stop), gate_rows[:, 1, v], MULT)
         both = keep.tile([P, V], F32, name="both", align_bytes=64)
         for v in halves:
             nc.vector.tensor_tensor(both[:, v], fused[0][:, v], fused[1][:, v], ADD)
+
         res = keep.tile([P, V], F32, name="res", align_bytes=64)
-        scaled = [keep.tile([P, 2, P], F32, name=f"scaled{b}", align_bytes=64) for b in range(V // P)]
-        for index, (first, last) in zip((2, 6, 7), ((0, 2), (2, 3), (3, 4))):
+        scaled = [keep.tile([P, D - FUSED, P], F32, name=f"scaled{b}", align_bytes=64) for b in range(V // P)]
+        free_banks = (2, 6, 7)
+        for index, (first, last) in zip(free_banks, STORES):
             back = bank(index, [P, last - first, P])
             for b in range(first, last):
-                for d in range(2):
+                for d in range(D - FUSED):
                     nc.scalar.activation(scaled[b][:, d, :], turned[d][b // 2][:, b % 2, :], COPY, scale=gate_cols[d][:, b : b + 1])
-                    nc.tensor.matmul(back[:, b - first, :], scaled[b][:, d, :], ident[:], start=d == 0 and b == first, stop=d == 1 and b == last - 1, is_transpose=True)
+                    nc.tensor.matmul(back[:, b - first, :], scaled[b][:, d, :], ident[:], start=d == 0 and b == first, stop=d == D - FUSED - 1 and b == last - 1, is_transpose=True)
             v = slice(first * P, last * P)
             nc.vector.tensor_tensor(res[:, v], both[:, v], back[:].rearrange("p b m -> p (b m)"), ADD)
             nc.sync.dma_start(out[:, v], res[:, v])

@@ -26,7 +26,7 @@ LINE = 4
 HALF = S // 2
 FUSED = 2
 W1_VECTOR = 40
-PAIR_CELLS = U // 2
+PAIR_CELLS = (768, 256)
 ADD_CELLS = 256
 WIDTHS = (256, 256, 256, 128, 128)
 VECTOR_RELU = 2
@@ -110,26 +110,28 @@ def tile_picked_devox_relu_p_kernel(tc, x_words, x_scales, w1, w2, gate, emb, of
             return acc
 
         half_bytes = HALF * 4
-        pair_bytes = PAIR_CELLS * PACK * 2
+        at_h1 = PAIR_CELLS[1] * PACK * 2
+        at_h0 = at_h1 + 3 * half_bytes
         cell_halves = [entries(cell_t, 0, HALF), entries(cell_t, HALF, S)]
-        h0 = [reused.tile([P, HALF], F32, name="h0_first", offset=pair_bytes, align_bytes=64), keep.tile([P, HALF], F32, name="h0_second", align_bytes=64)]
-        h1 = [keep.tile([P, HALF], F32, name="h1_first", align_bytes=64), keep.tile([P, HALF], F32, name="h1_second", align_bytes=64)]
+        h0 = [reused.tile([P, HALF], F32, name="h0_first", offset=at_h0, align_bytes=64), keep.tile([P, HALF], F32, name="h0_second", align_bytes=64)]
+        h1 = [
+            reused.tile([P, HALF], F32, name="h1_first", offset=at_h1, align_bytes=64),
+            reused.tile([P, HALF], F32, name="h1_second", offset=at_h0 - half_bytes // 2, align_bytes=64),
+        ]
+        h2 = reused.tile([P, S], F32, name="h2", offset=at_h0 + half_bytes // 2, align_bytes=64)
+        h3 = [reused.tile([P, HALF], F32, name=f"h3_{a}", offset=at_h1 - half_bytes // 2 + a * half_bytes, align_bytes=64) for a in range(2)]
         nc.scalar.activation(h0[0][:, :P], first_layer(0, 0, P, 0)[:], RELU)
         nc.scalar.activation(h0[0][:, P:], first_layer(0, P, HALF, 1)[:], RELU)
         nc.scalar.activation(h1[0][:], first_layer(1, 0, HALF, 2)[:], RELU)
         nc.scalar.activation(h0[1][:], first_layer(0, HALF, S, 3)[:], RELU)
-        nc.scalar.activation(h1[1][:], first_layer(1, HALF, S, 4)[:], RELU)
-        acc2 = first_layer(2, 0, S, 5)
-        acc3 = [first_layer(3, 0, HALF, 6), first_layer(3, HALF, S, 7)]
         nc.vector.tensor_copy(up[0][:].indirect(cell_halves[0]), h0[0][:])
         nc.scalar.activation(up[1][:].indirect(cell_halves[0]), h1[0][:], COPY)
-        h3 = [reused.tile([P, HALF], F32, name=f"h3_{a}", offset=pair_bytes - half_bytes // 2 + a * half_bytes, align_bytes=64) for a in range(2)]
-        for a in range(2):
-            nc.vector.tensor_scalar_max(h3[a][:], acc3[a][:], 0.0)
-        h2 = keep.tile([P, S], F32, name="h1_first", align_bytes=64)
-        nc.scalar.activation(h2[:], acc2[:], RELU)
+        nc.vector.tensor_scalar_max(h1[1][:], first_layer(1, HALF, S, 4)[:], 0.0)
         nc.vector.tensor_copy(up[0][:].indirect(cell_halves[1]), h0[1][:])
+        nc.vector.tensor_scalar_max(h2[:], first_layer(2, 0, S, 5)[:], 0.0)
+        nc.scalar.activation(h3[0][:], first_layer(3, 0, HALF, 6)[:], RELU)
         nc.scalar.activation(up[1][:].indirect(cell_halves[1]), h1[1][:], COPY)
+        nc.scalar.activation(h3[1][:], first_layer(3, HALF, S, 7)[:], RELU)
         nc.vector.tensor_copy(up[2][:].indirect(cell_t[:]), h2[:])
         for a in range(2):
             nc.scalar.activation(up[3][:].indirect(cell_halves[a]), h3[a][:], COPY)
@@ -141,15 +143,15 @@ def tile_picked_devox_relu_p_kernel(tc, x_words, x_scales, w1, w2, gate, emb, of
 
         chunks = [slice(sum(WIDTHS[:c]), sum(WIDTHS[: c + 1])) for c in range(len(WIDTHS))]
         pairs = [
-            reused.tile([P, PAIR_CELLS * PACK], BF16, name="pairs_vector", offset=0, align_bytes=64),
-            keep.tile([P, PAIR_CELLS * PACK], BF16, name="pairs_gpsimd", align_bytes=64),
+            keep.tile([P, PAIR_CELLS[0] * PACK], BF16, name="pairs_gpsimd", align_bytes=64),
+            reused.tile([P, PAIR_CELLS[1] * PACK], BF16, name="pairs_vector", offset=0, align_bytes=64),
         ]
         y = keep.tile([P, U], F32, name="y", align_bytes=64)
         z_bf = [keep.tile([P, width * PACK], BF16, name=f"z_bf{c}", align_bytes=64) for c, width in enumerate(WIDTHS)]
 
         def add_pairs(engine, u, first, last):
-            k, at = divmod(first, PAIR_CELLS)
-            start = 2 * (u * PAIR_CELLS + at)
+            k, at = divmod(first, PAIR_CELLS[0])
+            start = 2 * (u * PAIR_CELLS[k] + at)
             engine.tensor_tensor(
                 pairs[k][:, start : start + 2 * (last - first)].rearrange("p (g i e) -> p g e i", i=LINE, e=2),
                 up[2 * u][:].rearrange("p (e r) -> p e r", e=2)[:, :, first:last].rearrange("p e (g i) -> p g e i", i=LINE),
@@ -158,7 +160,7 @@ def tile_picked_devox_relu_p_kernel(tc, x_words, x_scales, w1, w2, gate, emb, of
             )
 
         def weave(c):
-            k, at = divmod(chunks[c].start, PAIR_CELLS)
+            k, at = divmod(chunks[c].start, PAIR_CELLS[0])
             nc.scalar.copy(
                 z_bf[c][:].bitcast(F32).rearrange("p (r u) -> p r u", u=2),
                 pairs[k][:].bitcast(F32).rearrange("p (u r) -> p r u", u=2)[:, at : at + WIDTHS[c]],
@@ -180,8 +182,8 @@ def tile_picked_devox_relu_p_kernel(tc, x_words, x_scales, w1, w2, gate, emb, of
             )
             return acc
 
-        add_pairs(nc.vector, 0, 0, PAIR_CELLS)
-        add_pairs(nc.gpsimd, 0, PAIR_CELLS, U)
+        add_pairs(nc.gpsimd, 0, 0, PAIR_CELLS[0])
+        add_pairs(nc.vector, 0, PAIR_CELLS[0], U)
         nc.vector.quantize_mx(out=w2_code[:].bitcast(FP8X4), scales=w2_scale[:], in_=w2_bf[:].rearrange("p n j -> p (n j)"))
         for first in range(0, U, ADD_CELLS):
             add_pairs(nc.vector, 1, first, first + ADD_CELLS)

@@ -24,13 +24,11 @@ LIST_ROWS = 16
 QUADRANT = 32
 LINE = 4
 HALF = S // 2
-FUSED = 2
 W1_VECTOR = 40
 PAIR_CELLS = (768, 256)
 ADD_CELLS = 256
 WIDTHS = (256, 256, 256, 128, 128)
 VECTOR_RELU = 2
-STORES = ((0, 2), (2, 3), (3, 4))
 
 
 def tile_picked_devox_relu_p_kernel(tc, x_words, x_scales, w1, w2, gate, emb, offs, cell, pos1, pos2, pos3, pos4, out):
@@ -53,8 +51,8 @@ def tile_picked_devox_relu_p_kernel(tc, x_words, x_scales, w1, w2, gate, emb, of
         table_scales = keep.tile([P, T], U8, name="table_scales", align_bytes=64)
         w1_raw = keep.tile([P, PACK, H], F32, name="w1_raw", align_bytes=64)
         w2_raw = keep.tile([P, PACK, N], F32, name="w2_raw", align_bytes=64)
-        gate_rows = keep.tile([P, FUSED, V], F32, name="gate_rows", align_bytes=64)
-        gate_cols = [keep.tile([P, V // P], F32, name=f"gate_cols{d}", align_bytes=64) for d in range(D - FUSED)]
+        gate_rows = keep.tile([P, D, V // 2], F32, name="gate_rows", align_bytes=64)
+        gate_cols = [keep.tile([P, D], F32, name=f"gate_cols{b}", align_bytes=64) for b in range(2)]
         up = [keep.tile([P, 2 * U], F32, name=f"up{t}", align_bytes=64) for t in range(PACK)]
         ident = keep.tile([P, P], F32, name="ident", align_bytes=64)
 
@@ -76,10 +74,10 @@ def tile_picked_devox_relu_p_kernel(tc, x_words, x_scales, w1, w2, gate, emb, of
             nc.sync.dma_start(up[2 + t][:, U:], emb_planes[:, 3 - t, :])
         for d, pos in enumerate((pos1, pos2, pos3, pos4)):
             nc.sync.dma_start(pos_t[d][:], pos)
-        nc.sync.dma_start(gate_rows[:], gate[:FUSED].rearrange("d p v -> p d v"))
-        for d in range(FUSED, D):
+        nc.sync.dma_start(gate_rows[:], gate[:, :, V // 2 :].rearrange("d p v -> p d v"))
+        for b in range(2):
             with nc.allow_non_contiguous_dma(reason="one gate value a partition"):
-                nc.sync.dma_start(gate_cols[d - FUSED][:], gate[d, 0].rearrange("(b p) -> p b", p=P))
+                nc.sync.dma_start(gate_cols[b][:], gate[:, 0, b * P : (b + 1) * P].rearrange("d p -> p d"))
         for t in range(PACK):
             nc.vector.tensor_copy(up[t][:, :U].rearrange("p (g i) -> p g i", i=LINE), zero[:].unsqueeze(1).to_broadcast([P, U // LINE, LINE]))
         make_identity(nc, ident[:])
@@ -196,39 +194,41 @@ def tile_picked_devox_relu_p_kernel(tc, x_words, x_scales, w1, w2, gate, emb, of
         nc.vector.tensor_scalar_max(y[:, chunks[VECTOR_RELU]], accs[VECTOR_RELU][:], 0.0)
 
         half_v = V // 2
-        halves = [slice(0, half_v), slice(half_v, V)]
-        plain = [[keep.tile([P, half_v], F32, name=f"plain{d}{a}", align_bytes=64) for a in range(2)] for d in range(D - FUSED)]
-        turned = [[bank(4 * a + d, [P, 2, P]) for a in range(2)] for d in range(D - FUSED)]
+        plain = [keep.tile([P, half_v], F32, name=f"plain{d}", align_bytes=64) for d in range(D)]
+        turned = [bank(index, [P, 2, P]) for index in (0, 1, 5, 6)]
 
         def cells_of(d, first, last):
             return y[:].indirect(entries(pos_t[d], first, last))
 
-        nc.vector.tensor_copy(plain[1][1][:], cells_of(3, half_v, V))
-        for b in range(2):
-            nc.scalar.activation(plain[0][0][:, b * P : (b + 1) * P], cells_of(2, b * P, (b + 1) * P), COPY)
-        nc.scalar.activation(plain[1][0][:], cells_of(3, 0, half_v), COPY)
-        nc.scalar.activation(plain[0][1][:], cells_of(2, half_v, V), COPY)
-        for d, a in ((0, 0), (1, 1), (1, 0), (0, 1)):
+        nc.vector.tensor_copy(plain[3][:], cells_of(3, 0, half_v))
+        for d in range(D - 1):
+            nc.scalar.activation(plain[d][:], cells_of(d, 0, half_v), COPY)
+        order = (3, 0, 1, 2)
+        for d in order:
             for b in range(2):
-                nc.tensor.transpose(turned[d][a][:, b, :], plain[d][a][:, b * P : (b + 1) * P], ident[:])
+                nc.tensor.transpose(turned[d][:, b, :], plain[d][:, b * P : (b + 1) * P], ident[:])
 
-        fused = [keep.tile([P, V], F32, name=f"fused{d}", align_bytes=64) for d in range(FUSED)]
-        nc.vector.tensor_tensor(fused[0][:], y[:].indirect(pos_t[0][:]), gate_rows[:, 0, :], MULT)
-        for v in halves:
-            nc.vector.tensor_tensor(fused[1][:, v], cells_of(1, v.start, v.stop), gate_rows[:, 1, v], MULT)
-        both = keep.tile([P, V], F32, name="both", align_bytes=64)
-        for v in halves:
-            nc.vector.tensor_tensor(both[:, v], fused[0][:, v], fused[1][:, v], ADD)
-
+        fused = [keep.tile([P, half_v], F32, name=f"fused{d}", align_bytes=64) for d in range(D)]
+        sums = [keep.tile([P, half_v], F32, name=f"sums{d}", align_bytes=64) for d in range(2)]
         res = keep.tile([P, V], F32, name="res", align_bytes=64)
-        scaled = [keep.tile([P, D - FUSED, P], F32, name=f"scaled{b}", align_bytes=64) for b in range(V // P)]
-        free_banks = (2, 6, 7)
-        for index, (first, last) in zip(free_banks, STORES):
-            back = bank(index, [P, last - first, P])
-            for b in range(first, last):
-                for d in range(D - FUSED):
-                    nc.scalar.activation(scaled[b][:, d, :], turned[d][b // 2][:, b % 2, :], COPY, scale=gate_cols[d][:, b : b + 1])
-                    nc.tensor.matmul(back[:, b - first, :], scaled[b][:, d, :], ident[:], start=d == 0 and b == first, stop=d == D - FUSED - 1 and b == last - 1, is_transpose=True)
-            v = slice(first * P, last * P)
-            nc.vector.tensor_tensor(res[:, v], both[:, v], back[:].rearrange("p b m -> p (b m)"), ADD)
+        for d in range(D):
+            nc.vector.tensor_tensor(fused[d][:], cells_of(d, half_v, V), gate_rows[:, d, :], MULT)
+            if d == 2:
+                nc.vector.tensor_tensor(sums[0][:], fused[0][:], fused[1][:], ADD)
+        blocks = [slice(b * P, (b + 1) * P) for b in range(2)]
+        for v in blocks:
+            nc.vector.tensor_tensor(sums[1][:, v], sums[0][:, v], fused[2][:, v], ADD)
+        for b, v in enumerate(blocks):
+            at = slice(half_v + b * P, half_v + (b + 1) * P)
+            nc.vector.tensor_tensor(res[:, at], sums[1][:, v], fused[3][:, v], ADD)
+            nc.sync.dma_start(out[:, at], res[:, at])
+
+        scaled = [keep.tile([P, D, P], F32, name=f"scaled{b}", align_bytes=64) for b in range(2)]
+        backs = [bank(index, [P, P]) for index in (2, 7)]
+        for d in order:
+            for b in range(2):
+                nc.scalar.activation(scaled[b][:, d, :], turned[d][:, b, :], COPY, scale=gate_cols[b][:, d : d + 1])
+                nc.tensor.matmul(backs[b][:], scaled[b][:, d, :], ident[:], start=d == order[0], stop=d == order[-1], is_transpose=True)
+        for b, v in enumerate(blocks):
+            nc.scalar.copy(res[:, v], backs[b][:])
             nc.sync.dma_start(out[:, v], res[:, v])

@@ -231,4 +231,4 @@ def tile_picked_devox_relu_p_kernel(tc, x_words, x_scales, w1, w2, gate, emb, of
                 nc.tensor.matmul(backs[b][:], scaled[b][:, d, :], ident[:], start=d == order[0], stop=d == order[-1], is_transpose=True)
         for b, v in enumerate(blocks):
             nc.scalar.copy(res[:, v], backs[b][:])
-            nc.sync.dma_start(out[:, v], res[:, v])
+        nc.sync.dma_start(out[:, :half_v], res[:, :half_v])

@@ -24,7 +24,7 @@ LIST_ROWS = 16
 QUADRANT = 32
 LINE = 4
 HALF = S // 2
-W1_VECTOR = 40
+W1_VECTOR = 64
 PAIR_CELLS = (768, 256)
 ADD_CELLS = 256
 WIDTHS = (256, 256, 256, 128, 128)
@@ -49,8 +49,9 @@ def tile_picked_devox_relu_p_kernel(tc, x_words, x_scales, w1, w2, gate, emb, of
         pos_t = [keep.tile([P, V // LIST_ROWS], U16, name=f"pos_t{d}") for d in range(D)]
         table_words = keep.tile([P, T], U32, name="table_words", align_bytes=64)
         table_scales = keep.tile([P, T], U8, name="table_scales", align_bytes=64)
-        w1_raw = keep.tile([P, PACK, H], F32, name="w1_raw", align_bytes=64)
-        w2_raw = keep.tile([P, PACK, N], F32, name="w2_raw", align_bytes=64)
+        w1_raw = [keep.tile([P, 2, H], F32, name=f"w1_raw{u}", align_bytes=64) for u in range(2)]
+        at_w2 = (PAIR_CELLS[1] + PAIR_CELLS[0]) * PACK * 2 - HALF * 2
+        w2_raw = reused.tile([P, PACK, N], F32, name="w2_raw", offset=at_w2, align_bytes=64)
         gate_rows = keep.tile([P, D, V // 2], F32, name="gate_rows", align_bytes=64)
         gate_cols = [keep.tile([P, D], F32, name=f"gate_cols{b}", align_bytes=64) for b in range(2)]
         up = [keep.tile([P, 2 * U], F32, name=f"up{t}", align_bytes=64) for t in range(PACK)]
@@ -60,14 +61,16 @@ def tile_picked_devox_relu_p_kernel(tc, x_words, x_scales, w1, w2, gate, emb, of
         zero = keep.tile([P, LINE], F32, name="zero", align_bytes=64)
         nc.gpsimd.memset(zero[:], 0.0)
 
-        nc.sync.dma_start(w1_raw[:], w1.rearrange("(p j) c -> p j c", j=PACK))
+        w1_rows = w1.rearrange("(p j) c -> p j c", j=PACK)
+        nc.sync.dma_start(w1_raw[0][:], w1_rows[:, :2, :])
         nc.sync.dma_start(offs_t[:], offs)
         for q in range(P // QUADRANT):
             nc.sync.dma_start(table_scales[QUADRANT * q : QUADRANT * q + 4, :].bitcast(I32), x_scales[0, 4 * q : 4 * q + 4, :].bitcast(I32))
         nc.sync.dma_start(table_words[:].bitcast(I32), x_words[0].rearrange("p n r -> p (n r)").bitcast(I32))
+        nc.sync.dma_start(w1_raw[1][:], w1_rows[:, 2:, :])
         nc.sync.dma_start(cell_t[:], cell)
         emb_planes = emb.rearrange("(p t) r -> p t r", t=PACK)
-        for t in range(2):
+        for t in (1, 0):
             nc.sync.dma_start(up[t][:, U:], emb_planes[:, 1 - t, :])
         nc.sync.dma_start(w2_raw[:], w2.rearrange("(p j) c -> p j c", j=PACK))
         for t in range(2):
@@ -82,17 +85,37 @@ def tile_picked_devox_relu_p_kernel(tc, x_words, x_scales, w1, w2, gate, emb, of
             nc.vector.tensor_copy(up[t][:, :U].rearrange("p (g i) -> p g i", i=LINE), zero[:].unsqueeze(1).to_broadcast([P, U // LINE, LINE]))
         make_identity(nc, ident[:])
 
-        w1_bf = keep.tile([P, PACK, P, PACK], BF16, name="w1_bf", align_bytes=64)
+        w1_bf = [keep.tile([P, 2, P, PACK], BF16, name=f"w1_bf{u}", align_bytes=64) for u in range(2)]
         w1_code = keep.tile([P, H], U32, name="w1_code", align_bytes=64)
         w1_scale = keep.tile([P, H], U8, name="w1_scale", align_bytes=64)
-        for copy, share in ((nc.vector.tensor_copy, slice(0, W1_VECTOR)), (nc.scalar.copy, slice(W1_VECTOR, P))):
-            copy(w1_bf[:, :, share, :].rearrange("p t m j -> p m t j"), w1_raw[:].rearrange("p j (m t) -> p m t j", t=PACK)[:, share])
+
+        def round_w1(copy, rows, u, share):
+            copy(
+                w1_bf[u][:, :, share, 2 * rows : 2 * rows + 2].rearrange("p e m j -> p m e j"),
+                w1_raw[rows][:].rearrange("p j (m t) -> p m t j", t=PACK)[:, share, 2 * u : 2 * u + 2],
+            )
+
+        def quantize_w1(first, last):
+            u, e = divmod(first, 2)
+            columns = slice(first * P, last * P)
+            nc.vector.quantize_mx(
+                out=w1_code[:, columns].bitcast(FP8X4),
+                scales=w1_scale[:, columns],
+                in_=w1_bf[u][:, e : e + last - first].rearrange("p e m j -> p (e m j)"),
+            )
+
+        for u in range(2):
+            round_w1(nc.scalar.copy, 0, u, slice(0, P))
         x_scale = keep.tile([P, S], U8, name="x_scale", align_bytes=64)
         nc.vector.tensor_copy(x_scale[:], table_scales[:].indirect(offs_t[:]))
-        nc.vector.quantize_mx(out=w1_code[:].bitcast(FP8X4), scales=w1_scale[:], in_=w1_bf[:].rearrange("p t m j -> p (t m j)"))
         x_code = keep.tile([P, S], U32, name="x_code", align_bytes=64)
-        for first, last in ((0, P), (P, HALF), (HALF, S)):
-            nc.vector.tensor_copy(x_code[:, first:last], table_words[:].indirect(entries(offs_t, first, last)))
+        nc.vector.tensor_copy(x_code[:], table_words[:].indirect(offs_t[:]))
+        round_w1(nc.vector.tensor_copy, 1, 0, slice(0, W1_VECTOR))
+        round_w1(nc.scalar.copy, 1, 0, slice(W1_VECTOR, P))
+        round_w1(nc.scalar.copy, 1, 1, slice(0, P))
+        quantize_w1(1, 2)
+        quantize_w1(0, 1)
+        quantize_w1(2, 4)
 
         def first_layer(t, first, last, index):
             acc = bank(index, [P, last - first])
@@ -107,41 +130,35 @@ def tile_picked_devox_relu_p_kernel(tc, x_words, x_scales, w1, w2, gate, emb, of
             )
             return acc
 
-        half_bytes = HALF * 4
-        at_h1 = PAIR_CELLS[1] * PACK * 2
-        at_h0 = at_h1 + 3 * half_bytes
         cell_halves = [entries(cell_t, 0, HALF), entries(cell_t, HALF, S)]
-        h0 = [reused.tile([P, HALF], F32, name="h0_first", offset=at_h0, align_bytes=64), keep.tile([P, HALF], F32, name="h0_second", align_bytes=64)]
-        h1 = [
-            reused.tile([P, HALF], F32, name="h1_first", offset=at_h1, align_bytes=64),
-            reused.tile([P, HALF], F32, name="h1_second", offset=at_h0 - half_bytes // 2, align_bytes=64),
-        ]
-        h2 = reused.tile([P, S], F32, name="h2", offset=at_h0 + half_bytes // 2, align_bytes=64)
-        h3 = [reused.tile([P, HALF], F32, name=f"h3_{a}", offset=at_h1 - half_bytes // 2 + a * half_bytes, align_bytes=64) for a in range(2)]
-        nc.scalar.activation(h0[0][:, :P], first_layer(0, 0, P, 0)[:], RELU)
-        nc.scalar.activation(h0[0][:, P:], first_layer(0, P, HALF, 1)[:], RELU)
-        nc.scalar.activation(h1[0][:], first_layer(1, 0, HALF, 2)[:], RELU)
-        nc.scalar.activation(h0[1][:], first_layer(0, HALF, S, 3)[:], RELU)
-        nc.vector.tensor_copy(up[0][:].indirect(cell_halves[0]), h0[0][:])
-        nc.scalar.activation(up[1][:].indirect(cell_halves[0]), h1[0][:], COPY)
-        nc.vector.tensor_scalar_max(h1[1][:], first_layer(1, HALF, S, 4)[:], 0.0)
-        nc.vector.tensor_copy(up[0][:].indirect(cell_halves[1]), h0[1][:])
-        nc.vector.tensor_scalar_max(h2[:], first_layer(2, 0, S, 5)[:], 0.0)
-        nc.scalar.activation(h3[0][:], first_layer(3, 0, HALF, 6)[:], RELU)
-        nc.scalar.activation(up[1][:].indirect(cell_halves[1]), h1[1][:], COPY)
-        nc.scalar.activation(h3[1][:], first_layer(3, HALF, S, 7)[:], RELU)
-        nc.vector.tensor_copy(up[2][:].indirect(cell_t[:]), h2[:])
-        for a in range(2):
-            nc.scalar.activation(up[3][:].indirect(cell_halves[a]), h3[a][:], COPY)
+        h0 = keep.tile([P, S], F32, name="h0", align_bytes=64)
+        h2 = reused.tile([P, S], F32, name="h2", offset=at_w2 + HALF * 2, align_bytes=64)
+        h1 = [keep.tile([P, HALF], F32, name="h1_0", align_bytes=64), reused.tile([P, HALF], F32, name="h1_1", offset=at_w2 - HALF * 2, align_bytes=64)]
+        h3 = [reused.tile([P, HALF], F32, name="h3_0", offset=0, align_bytes=64), keep.tile([P, HALF], F32, name="h3_1", align_bytes=64)]
 
         w2_scale = keep.tile([P, N], U8, name="w2_scale", align_bytes=64)
         w2_bf = keep.tile([P, N, PACK], BF16, name="w2_bf", align_bytes=64)
-        nc.gpsimd.tensor_copy(w2_bf[:], w2_raw[:].rearrange("p j n -> p n j"))
+        nc.gpsimd.tensor_scalar(w2_bf[:], w2_raw[:].rearrange("p j n -> p n j"), 1.0, 0.0, MULT, ADD)
         w2_code = keep.tile([P, N], U32, name="w2_code", align_bytes=64)
+
+        nc.scalar.activation(h1[0][:], first_layer(1, 0, HALF, 0)[:], RELU)
+        nc.vector.tensor_scalar_max(h0[:, :HALF], first_layer(0, 0, HALF, 1)[:], 0.0)
+        nc.vector.tensor_scalar_max(h0[:, HALF:], first_layer(0, HALF, S, 2)[:], 0.0)
+        nc.vector.tensor_scalar_max(h3[0][:], first_layer(3, 0, HALF, 3)[:], 0.0)
+        nc.scalar.activation(up[1][:].indirect(cell_halves[0]), h1[0][:], COPY)
+        nc.vector.tensor_copy(up[0][:].indirect(cell_t[:]), h0[:])
+        nc.scalar.activation(h1[1][:], first_layer(1, HALF, S, 4)[:], RELU)
+        nc.scalar.activation(h2[:], first_layer(2, 0, S, 5)[:], RELU)
+        nc.scalar.activation(up[1][:].indirect(cell_halves[1]), h1[1][:], COPY)
+        nc.vector.quantize_mx(out=w2_code[:].bitcast(FP8X4), scales=w2_scale[:], in_=w2_bf[:].rearrange("p n j -> p (n j)"))
+        nc.vector.tensor_copy(up[2][:].indirect(cell_t[:]), h2[:])
+        nc.scalar.activation(h3[1][:], first_layer(3, HALF, S, 4)[:], RELU)
+        for a in range(2):
+            nc.scalar.activation(up[3][:].indirect(cell_halves[a]), h3[a][:], COPY)
 
         chunks = [slice(sum(WIDTHS[:c]), sum(WIDTHS[: c + 1])) for c in range(len(WIDTHS))]
         pairs = [
-            keep.tile([P, PAIR_CELLS[0] * PACK], BF16, name="pairs_gpsimd", align_bytes=64),
+            reused.tile([P, PAIR_CELLS[0] * PACK], BF16, name="pairs_gpsimd", offset=PAIR_CELLS[1] * PACK * 2, align_bytes=64),
             reused.tile([P, PAIR_CELLS[1] * PACK], BF16, name="pairs_vector", offset=0, align_bytes=64),
         ]
         y = keep.tile([P, U], F32, name="y", align_bytes=64)
@@ -182,7 +199,6 @@ def tile_picked_devox_relu_p_kernel(tc, x_words, x_scales, w1, w2, gate, emb, of
 
         add_pairs(nc.gpsimd, 0, 0, PAIR_CELLS[0])
         add_pairs(nc.vector, 0, PAIR_CELLS[0], U)
-        nc.vector.quantize_mx(out=w2_code[:].bitcast(FP8X4), scales=w2_scale[:], in_=w2_bf[:].rearrange("p n j -> p (n j)"))
         for first in range(0, U, ADD_CELLS):
             add_pairs(nc.vector, 1, first, first + ADD_CELLS)
         for c in range(len(WIDTHS)):

@@ -50,8 +50,8 @@ def tile_picked_devox_relu_p_kernel(tc, x_words, x_scales, w1, w2, gate, emb, of
         table_words = keep.tile([P, T], U32, name="table_words", align_bytes=64)
         table_scales = keep.tile([P, T], U8, name="table_scales", align_bytes=64)
         w1_raw = [keep.tile([P, 2, H], F32, name=f"w1_raw{u}", align_bytes=64) for u in range(2)]
-        at_w2 = (PAIR_CELLS[1] + PAIR_CELLS[0]) * PACK * 2 - HALF * 2
-        w2_raw = reused.tile([P, PACK, N], F32, name="w2_raw", offset=at_w2, align_bytes=64)
+        at_pairs = PAIR_CELLS[1] * PACK * 2
+        w2_raw = reused.tile([P, PACK, N], F32, name="w2_raw", offset=at_pairs, align_bytes=64)
         gate_rows = keep.tile([P, D, V // 2], F32, name="gate_rows", align_bytes=64)
         gate_cols = [keep.tile([P, D], F32, name=f"gate_cols{b}", align_bytes=64) for b in range(2)]
         up = [keep.tile([P, 2 * U], F32, name=f"up{t}", align_bytes=64) for t in range(PACK)]
@@ -132,8 +132,8 @@ def tile_picked_devox_relu_p_kernel(tc, x_words, x_scales, w1, w2, gate, emb, of
 
         cell_halves = [entries(cell_t, 0, HALF), entries(cell_t, HALF, S)]
         h0 = keep.tile([P, S], F32, name="h0", align_bytes=64)
-        h2 = reused.tile([P, S], F32, name="h2", offset=at_w2 + HALF * 2, align_bytes=64)
-        h1 = [keep.tile([P, HALF], F32, name="h1_0", align_bytes=64), reused.tile([P, HALF], F32, name="h1_1", offset=at_w2 - HALF * 2, align_bytes=64)]
+        h2 = keep.tile([P, S], F32, name="h2", align_bytes=64)
+        h1 = [keep.tile([P, HALF], F32, name=f"h1_{a}", align_bytes=64) for a in range(2)]
         h3 = [reused.tile([P, HALF], F32, name="h3_0", offset=0, align_bytes=64), keep.tile([P, HALF], F32, name="h3_1", align_bytes=64)]
 
         w2_scale = keep.tile([P, N], U8, name="w2_scale", align_bytes=64)
@@ -142,12 +142,12 @@ def tile_picked_devox_relu_p_kernel(tc, x_words, x_scales, w1, w2, gate, emb, of
         w2_code = keep.tile([P, N], U32, name="w2_code", align_bytes=64)
 
         nc.scalar.activation(h1[0][:], first_layer(1, 0, HALF, 0)[:], RELU)
+        nc.scalar.activation(h1[1][:], first_layer(1, HALF, S, 4)[:], RELU)
         nc.vector.tensor_scalar_max(h0[:, :HALF], first_layer(0, 0, HALF, 1)[:], 0.0)
         nc.vector.tensor_scalar_max(h0[:, HALF:], first_layer(0, HALF, S, 2)[:], 0.0)
         nc.vector.tensor_scalar_max(h3[0][:], first_layer(3, 0, HALF, 3)[:], 0.0)
         nc.scalar.activation(up[1][:].indirect(cell_halves[0]), h1[0][:], COPY)
         nc.vector.tensor_copy(up[0][:].indirect(cell_t[:]), h0[:])
-        nc.scalar.activation(h1[1][:], first_layer(1, HALF, S, 4)[:], RELU)
         nc.scalar.activation(h2[:], first_layer(2, 0, S, 5)[:], RELU)
         nc.scalar.activation(up[1][:].indirect(cell_halves[1]), h1[1][:], COPY)
         nc.vector.quantize_mx(out=w2_code[:].bitcast(FP8X4), scales=w2_scale[:], in_=w2_bf[:].rearrange("p n j -> p (n j)"))
@@ -158,7 +158,7 @@ def tile_picked_devox_relu_p_kernel(tc, x_words, x_scales, w1, w2, gate, emb, of
 
         chunks = [slice(sum(WIDTHS[:c]), sum(WIDTHS[: c + 1])) for c in range(len(WIDTHS))]
         pairs = [
-            reused.tile([P, PAIR_CELLS[0] * PACK], BF16, name="pairs_gpsimd", offset=PAIR_CELLS[1] * PACK * 2, align_bytes=64),
+            reused.tile([P, PAIR_CELLS[0] * PACK], BF16, name="pairs_gpsimd", offset=at_pairs, align_bytes=64),
             reused.tile([P, PAIR_CELLS[1] * PACK], BF16, name="pairs_vector", offset=0, align_bytes=64),
         ]
         y = keep.tile([P, U], F32, name="y", align_bytes=64)

from contextlib import ExitStack

import concourse.mybir as mybir
from concourse.masks import make_identity

K, T, S, D, V, H, N, U = 512, 2048, 512, 4, 512, 512, 128, 1024
FLOPS = 2 * K * H * S + 2 * H * N * U

F32 = mybir.dt.float32
BF16 = mybir.dt.bfloat16
I32 = mybir.dt.int32
U32 = mybir.dt.uint32
U16 = mybir.dt.uint16
U8 = mybir.dt.uint8
FP8X4 = mybir.dt.float8_e4m3fn_x4
ADD = mybir.AluOpType.add
MULT = mybir.AluOpType.mult
COPY = mybir.ActivationFunctionType.Copy
RELU = mybir.ActivationFunctionType.Relu

P = 128
PACK = 4
LIST_ROWS = 16
QUADRANT = 32
LINE = 4
HALF = S // 2
W1_VECTOR = 64
PAIR_CELLS = (768, 256)
ADD_CELLS = 256
WIDTHS = (256, 256, 256, 128, 128)
VECTOR_RELU = 2


def tile_picked_devox_relu_p_kernel(tc, x_words, x_scales, w1, w2, gate, emb, offs, cell, pos1, pos2, pos3, pos4, out):
    nc = tc.nc
    with ExitStack() as ctx:
        keep = ctx.enter_context(tc.tile_pool(name="keep", bufs=1))
        reused = ctx.enter_context(tc.tile_pool(name="reused", bufs=1))
        psum = ctx.enter_context(tc.psum_pool(name="psum", bufs=1))

        def bank(index, shape):
            return psum.tile(shape, F32, name=f"bank{index}")

        def entries(list_tile, first, last):
            return list_tile[:, first // LIST_ROWS : last // LIST_ROWS]

        offs_t = keep.tile([P, S // LIST_ROWS], U16, name="offs_t")
        cell_t = keep.tile([P, S // LIST_ROWS], U16, name="cell_t")
        pos_t = [keep.tile([P, V // LIST_ROWS], U16, name=f"pos_t{d}") for d in range(D)]
        table_words = keep.tile([P, T], U32, name="table_words", align_bytes=64)
        table_scales = keep.tile([P, T], U8, name="table_scales", align_bytes=64)
        w1_raw = [keep.tile([P, 2, H], F32, name=f"w1_raw{u}", align_bytes=64) for u in range(2)]
        at_pairs = PAIR_CELLS[1] * PACK * 2
        w2_raw = reused.tile([P, PACK, N], F32, name="w2_raw", offset=at_pairs, align_bytes=64)
        gate_rows = keep.tile([P, D, V // 2], F32, name="gate_rows", align_bytes=64)
        gate_cols = [keep.tile([P, D], F32, name=f"gate_cols{b}", align_bytes=64) for b in range(2)]
        up = [keep.tile([P, 2 * U], F32, name=f"up{t}", align_bytes=64) for t in range(PACK)]
        ident = keep.tile([P, P], F32, name="ident", align_bytes=64)

        nc.gpsimd.memset(table_scales[:].bitcast(I32), 0)
        zero = keep.tile([P, LINE], F32, name="zero", align_bytes=64)
        nc.gpsimd.memset(zero[:], 0.0)

        w1_rows = w1.rearrange("(p j) c -> p j c", j=PACK)
        nc.sync.dma_start(w1_raw[0][:], w1_rows[:, :2, :])
        nc.sync.dma_start(offs_t[:], offs)
        for q in range(P // QUADRANT):
            nc.sync.dma_start(table_scales[QUADRANT * q : QUADRANT * q + 4, :].bitcast(I32), x_scales[0, 4 * q : 4 * q + 4, :].bitcast(I32))
        nc.sync.dma_start(table_words[:].bitcast(I32), x_words[0].rearrange("p n r -> p (n r)").bitcast(I32))
        nc.sync.dma_start(w1_raw[1][:], w1_rows[:, 2:, :])
        nc.sync.dma_start(cell_t[:], cell)
        emb_planes = emb.rearrange("(p t) r -> p t r", t=PACK)
        for t in (1, 0):
            nc.sync.dma_start(up[t][:, U:], emb_planes[:, 1 - t, :])
        nc.sync.dma_start(w2_raw[:], w2.rearrange("(p j) c -> p j c", j=PACK))
        for t in range(2):
            nc.sync.dma_start(up[2 + t][:, U:], emb_planes[:, 3 - t, :])
        for d, pos in enumerate((pos1, pos2, pos3, pos4)):
            nc.sync.dma_start(pos_t[d][:], pos)
        nc.sync.dma_start(gate_rows[:], gate[:, :, V // 2 :].rearrange("d p v -> p d v"))
        for b in range(2):
            with nc.allow_non_contiguous_dma(reason="one gate value a partition"):
                nc.sync.dma_start(gate_cols[b][:], gate[:, 0, b * P : (b + 1) * P].rearrange("d p -> p d"))
        for t in range(PACK):
            nc.vector.tensor_copy(up[t][:, :U].rearrange("p (g i) -> p g i", i=LINE), zero[:].unsqueeze(1).to_broadcast([P, U // LINE, LINE]))
        make_identity(nc, ident[:])

        w1_bf = [keep.tile([P, 2, P, PACK], BF16, name=f"w1_bf{u}", align_bytes=64) for u in range(2)]
        w1_code = keep.tile([P, H], U32, name="w1_code", align_bytes=64)
        w1_scale = keep.tile([P, H], U8, name="w1_scale", align_bytes=64)

        def round_w1(copy, rows, u, share):
            copy(
                w1_bf[u][:, :, share, 2 * rows : 2 * rows + 2].rearrange("p e m j -> p m e j"),
                w1_raw[rows][:].rearrange("p j (m t) -> p m t j", t=PACK)[:, share, 2 * u : 2 * u + 2],
            )

        def quantize_w1(first, last):
            u, e = divmod(first, 2)
            columns = slice(first * P, last * P)
            nc.vector.quantize_mx(
                out=w1_code[:, columns].bitcast(FP8X4),
                scales=w1_scale[:, columns],
                in_=w1_bf[u][:, e : e + last - first].rearrange("p e m j -> p (e m j)"),
            )

        for u in range(2):
            round_w1(nc.scalar.copy, 0, u, slice(0, P))
        x_scale = keep.tile([P, S], U8, name="x_scale", align_bytes=64)
        nc.vector.tensor_copy(x_scale[:], table_scales[:].indirect(offs_t[:]))
        x_code = keep.tile([P, S], U32, name="x_code", align_bytes=64)
        nc.vector.tensor_copy(x_code[:], table_words[:].indirect(offs_t[:]))
        round_w1(nc.vector.tensor_copy, 1, 0, slice(0, W1_VECTOR))
        round_w1(nc.scalar.copy, 1, 0, slice(W1_VECTOR, P))
        round_w1(nc.scalar.copy, 1, 1, slice(0, P))
        quantize_w1(1, 2)
        quantize_w1(0, 1)
        quantize_w1(2, 4)

        def first_layer(t, first, last, index):
            acc = bank(index, [P, last - first])
            nc.tensor.matmul_mx(
                out=acc[:],
                lhsT=w1_code[:, t * P : (t + 1) * P].bitcast(FP8X4),
                lhsT_scale=w1_scale[:, t * P : (t + 1) * P],
                rhs=x_code[:, first:last].bitcast(FP8X4),
                rhs_scale=x_scale[:, first:last],
                start=True,
                stop=True,
            )
            return acc

        cell_halves = [entries(cell_t, 0, HALF), entries(cell_t, HALF, S)]
        h0 = keep.tile([P, S], F32, name="h0", align_bytes=64)
        h2 = keep.tile([P, S], F32, name="h2", align_bytes=64)
        h1 = [keep.tile([P, HALF], F32, name=f"h1_{a}", align_bytes=64) for a in range(2)]
        h3 = [reused.tile([P, HALF], F32, name="h3_0", offset=0, align_bytes=64), keep.tile([P, HALF], F32, name="h3_1", align_bytes=64)]

        w2_scale = keep.tile([P, N], U8, name="w2_scale", align_bytes=64)
        w2_bf = keep.tile([P, N, PACK], BF16, name="w2_bf", align_bytes=64)
        nc.gpsimd.tensor_scalar(w2_bf[:], w2_raw[:].rearrange("p j n -> p n j"), 1.0, 0.0, MULT, ADD)
        w2_code = keep.tile([P, N], U32, name="w2_code", align_bytes=64)

        nc.scalar.activation(h1[0][:], first_layer(1, 0, HALF, 0)[:], RELU)
        nc.scalar.activation(h1[1][:], first_layer(1, HALF, S, 4)[:], RELU)
        nc.vector.tensor_scalar_max(h0[:, :HALF], first_layer(0, 0, HALF, 1)[:], 0.0)
        nc.vector.tensor_scalar_max(h0[:, HALF:], first_layer(0, HALF, S, 2)[:], 0.0)
        nc.vector.tensor_scalar_max(h3[0][:], first_layer(3, 0, HALF, 3)[:], 0.0)
        nc.scalar.activation(up[1][:].indirect(cell_halves[0]), h1[0][:], COPY)
        nc.vector.tensor_copy(up[0][:].indirect(cell_t[:]), h0[:])
        nc.scalar.activation(h2[:], first_layer(2, 0, S, 5)[:], RELU)
        nc.scalar.activation(up[1][:].indirect(cell_halves[1]), h1[1][:], COPY)
        nc.vector.quantize_mx(out=w2_code[:].bitcast(FP8X4), scales=w2_scale[:], in_=w2_bf[:].rearrange("p n j -> p (n j)"))
        nc.vector.tensor_copy(up[2][:].indirect(cell_t[:]), h2[:])
        nc.scalar.activation(h3[1][:], first_layer(3, HALF, S, 4)[:], RELU)
        for a in range(2):
            nc.scalar.activation(up[3][:].indirect(cell_halves[a]), h3[a][:], COPY)

        chunks = [slice(sum(WIDTHS[:c]), sum(WIDTHS[: c + 1])) for c in range(len(WIDTHS))]
        pairs = [
            reused.tile([P, PAIR_CELLS[0] * PACK], BF16, name="pairs_gpsimd", offset=at_pairs, align_bytes=64),
            reused.tile([P, PAIR_CELLS[1] * PACK], BF16, name="pairs_vector", offset=0, align_bytes=64),
        ]
        y = keep.tile([P, U], F32, name="y", align_bytes=64)
        z_bf = [keep.tile([P, width * PACK], BF16, name=f"z_bf{c}", align_bytes=64) for c, width in enumerate(WIDTHS)]

        def add_pairs(engine, u, first, last):
            k, at = divmod(first, PAIR_CELLS[0])
            start = 2 * (u * PAIR_CELLS[k] + at)
            engine.tensor_tensor(
                pairs[k][:, start : start + 2 * (last - first)].rearrange("p (g i e) -> p g e i", i=LINE, e=2),
                up[2 * u][:].rearrange("p (e r) -> p e r", e=2)[:, :, first:last].rearrange("p e (g i) -> p g e i", i=LINE),
                up[2 * u + 1][:].rearrange("p (e r) -> p e r", e=2)[:, ::-1, first:last].rearrange("p e (g i) -> p g e i", i=LINE),
                ADD,
            )

        def weave(c):
            k, at = divmod(chunks[c].start, PAIR_CELLS[0])
            nc.scalar.copy(
                z_bf[c][:].bitcast(F32).rearrange("p (r u) -> p r u", u=2),
                pairs[k][:].bitcast(F32).rearrange("p (u r) -> p r u", u=2)[:, at : at + WIDTHS[c]],
            )

        def second_layer(c):
            z_code = keep.tile([P, WIDTHS[c]], U32, name=f"z_code{c}", align_bytes=64)
            z_scale = keep.tile([P, WIDTHS[c]], U8, name=f"z_scale{c}", align_bytes=64)
            nc.vector.quantize_mx(out=z_code[:].bitcast(FP8X4), scales=z_scale[:], in_=z_bf[c][:])
            acc = bank(c, [P, WIDTHS[c]])
            nc.tensor.matmul_mx(
                out=acc[:],
                lhsT=w2_code[:].bitcast(FP8X4),
                lhsT_scale=w2_scale[:],
                rhs=z_code[:].bitcast(FP8X4),
                rhs_scale=z_scale[:],
                start=True,
                stop=True,
            )
            return acc

        add_pairs(nc.gpsimd, 0, 0, PAIR_CELLS[0])
        add_pairs(nc.vector, 0, PAIR_CELLS[0], U)
        for first in range(0, U, ADD_CELLS):
            add_pairs(nc.vector, 1, first, first + ADD_CELLS)
        for c in range(len(WIDTHS)):
            weave(c)
        accs = [second_layer(c) for c in range(len(WIDTHS))]
        for c in range(len(WIDTHS)):
            if c != VECTOR_RELU:
                nc.scalar.activation(y[:, chunks[c]], accs[c][:], RELU)
        nc.vector.tensor_scalar_max(y[:, chunks[VECTOR_RELU]], accs[VECTOR_RELU][:], 0.0)

        half_v = V // 2
        plain = [keep.tile([P, half_v], F32, name=f"plain{d}", align_bytes=64) for d in range(D)]
        turned = [bank(index, [P, 2, P]) for index in (0, 1, 5, 6)]

        def cells_of(d, first, last):
            return y[:].indirect(entries(pos_t[d], first, last))

        nc.vector.tensor_copy(plain[3][:], cells_of(3, 0, half_v))
        for d in range(D - 1):
            nc.scalar.activation(plain[d][:], cells_of(d, 0, half_v), COPY)
        order = (3, 0, 1, 2)
        for d in order:
            for b in range(2):
                nc.tensor.transpose(turned[d][:, b, :], plain[d][:, b * P : (b + 1) * P], ident[:])

        fused = [keep.tile([P, half_v], F32, name=f"fused{d}", align_bytes=64) for d in range(D)]
        sums = [keep.tile([P, half_v], F32, name=f"sums{d}", align_bytes=64) for d in range(2)]
        res = keep.tile([P, V], F32, name="res", align_bytes=64)
        for d in range(D):
            nc.vector.tensor_tensor(fused[d][:], cells_of(d, half_v, V), gate_rows[:, d, :], MULT)
            if d == 2:
                nc.vector.tensor_tensor(sums[0][:], fused[0][:], fused[1][:], ADD)
        blocks = [slice(b * P, (b + 1) * P) for b in range(2)]
        for v in blocks:
            nc.vector.tensor_tensor(sums[1][:, v], sums[0][:, v], fused[2][:, v], ADD)
        for b, v in enumerate(blocks):
            at = slice(half_v + b * P, half_v + (b + 1) * P)
            nc.vector.tensor_tensor(res[:, at], sums[1][:, v], fused[3][:, v], ADD)
            nc.sync.dma_start(out[:, at], res[:, at])

        scaled = [keep.tile([P, D, P], F32, name=f"scaled{b}", align_bytes=64) for b in range(2)]
        backs = [bank(index, [P, P]) for index in (2, 7)]
        for d in order:
            for b in range(2):
                nc.scalar.activation(scaled[b][:, d, :], turned[d][:, b, :], COPY, scale=gate_cols[b][:, d : d + 1])
                nc.tensor.matmul(backs[b][:], scaled[b][:, d, :], ident[:], start=d == order[0], stop=d == order[-1], is_transpose=True)
        for b, v in enumerate(blocks):
            nc.scalar.copy(res[:, v], backs[b][:])
        nc.sync.dma_start(out[:, :half_v], res[:, :half_v])
